import numpy as np, ml_dtypes
CORES = [66,74,82,90,194,202,210,218]
N = 8
BF = ml_dtypes.bfloat16
W, SV, M, HOPS = 4096, 256, 160, [1, 4, 2]
RO = len(HOPS) + 1
def names(rng, power, *shape):
    return np.minimum((W * rng.random(shape) ** power).astype(np.int64), W - 1)
def pairs(rng, C, power):
    a = names(rng, power, N, 8, 16, C); b = np.take_along_axis(a, np.argsort(rng.random((N, 8, 16, C)), axis=2), 2)
    share = rng.choice(np.array([0.0, 0.15, 0.5, 1.0]), (N, 8, 1, C)); b = np.where(rng.random(b.shape) < share, b, names(rng, power, N, 8, 16, C))
    fa = rng.choice(np.array([0.05, 0.12, 0.3, 0.7, 1.0]), (N, 8, 1, C), p=[0.2, 0.25, 0.2, 0.2, 0.15])
    fb = rng.choice(np.array([0.0, 0.3, 0.7, 1.0]), (N, 8, 1, C), p=[0.05, 0.25, 0.3, 0.4])
    return np.where(rng.random(a.shape) < fa, a, -1), np.where(rng.random(b.shape) < fb, b, -1)
def parts(rng, power):
    clk = rng.integers(0, 256, (N, 8, 16, W)); z = rng.integers(0, 256, (N, 8, 16, M)); th = rng.integers(1200, 1600, (N, 8))
    sc, st = pairs(rng, SV, power); d, t = pairs(rng, M, power)
    return clk, sc, st, d, t, z, th
def pack(clk, sc, st, d, t, z, th):
    return {"clk": clk.reshape(N, 128, W).astype(np.float32).astype(BF), "sc": sc.reshape(N, 128, SV).astype(np.int32), "st": st.reshape(N, 128, SV).astype(np.int32),
            "dl": d.reshape(N, 128, M).astype(np.int32), "tl": t.reshape(N, 128, M).astype(np.int32), "z0": z.reshape(N, 128, M).astype(np.float32).astype(BF),
            "th": np.repeat(th.reshape(N, 8), 16, axis=1).reshape(N, 128, 1).astype(np.int32)}
def setup_inputs(rng):
    return pack(*parts(rng, 1))
def setup_inputs_spread(rng):
    clk, sc, st, d, t, z, th = parts(rng, 4)
    clk = np.floor(np.exp2(8 * rng.random((N, 8, 1, W))) * rng.random((N, 8, 16, W))).astype(np.int64)
    z = np.floor(np.exp2(8 * rng.random((N, 8, 1, M))) * rng.random((N, 8, 16, M))).astype(np.int64)
    th = np.minimum(np.floor(np.exp2(12 * rng.random((N, 8)))).astype(np.int64), 4080)
    return pack(np.minimum(clk, 255), sc, st, d, t, np.minimum(z, 255), th)
def setup_inputs_ends(rng):
    def rec(C):
        p = rng.choice(np.array([0.0, 0.06, 0.5, 1.0]), (N, 8, 1, C)); s = (N, 8, 16, C)
        a = np.where(rng.random(s) < p, W - 1, -1)
        o = np.where(rng.random(s) < 0.3, -1, np.where(rng.random(s) < 0.15, W - 1, rng.integers(0, W, s)))
        return np.where(rng.random((N, 8, 1, C)) < 0.6, a, o)
    def half(C):
        k = rng.integers(0, 3, (N, 8, 1, C))
        return np.where(k == 0, 0, np.where(k == 1, 255, 255 * rng.integers(0, 2, (N, 8, 16, C))))
    clk = half(W); z = half(M); sc = rec(SV); st = rec(SV); d = rec(M); t = rec(M)
    g = np.arange(8)[None, :]; q = np.arange(N)[:, None]
    clk[..., 0] = 255; clk[..., W - 1] = np.where(((g + q + N) & 1) == 0, 255, 0)[:, :, None]
    clk[..., W - 2] = 255; clk[:, :, 15, W - 2] = 254
    z[..., 0] = 255; z[..., M - 1] = 255; z[..., M - 2] = 0
    th = 4080 * ((g // 2 + q + rng.integers(0, 2, (N, 1))) & 1); th[:, 5] = 4080
    for m, lo, hi in ((M - 1, 0, W - 1), (0, W - 1, 0)):
        d[..., m] = -1; d[:, :, 15, m] = W - 1; d[:, :, 4, m] = 5; t[..., m] = -1; t[:, :, 2, m] = lo; t[:, :, 15, m] = hi
    s = slice(M - 6, M - 2); z[..., s] = 255; d[:, :, 15, s] = W - 1; t[..., s] = -1; t[:, :, 2, s] = W - 2; t[:, :, 15, s] = 0
    d[:, 5] = W - 1; t[:, 5] = W - 1; sc[:, 5] = W - 1; st[:, 5] = W - 1; z[:, 5] = z[:, 5, :1]
    return pack(clk, sc, st, d, t, z, th)
def setup_inputs_corners(rng):
    clk, sc, st, d, t, z, th = parts(rng, 1)
    clk[:, 1::2, :, 1::2] = clk[:, 1::2, :, 0::2]
    th = rng.choice(np.array([0, 1, 126, 128, 1000, 1999, 4080]), (N, 8)); th[:, 0] = 1000; th[:, 7] = 1999; th[:, 3] = 0
    th[:, 5] = 2051 + 4 * rng.integers(0, 100, N); th[:, 6] = 2052 + 4 * rng.integers(0, 100, N)
    lanes = np.array([0, 1, SV - 1, SV, W - 2, W - 1])
    for q in range(N):
        for g in range(8):
            kind = rng.permutation(M) % 10; n = np.where(rng.random(M) < 0.5, rng.choice(lanes, M), rng.integers(0, W, M)); full = rng.integers(0, W, (16, M))
            D = d[q, g]; T = t[q, g]; x = clk[q, g][:, n]; room = np.maximum(x, 255 - x)
            gap = np.maximum(int(th[q, g]) + rng.integers(-1, 2, M), 0); step = np.clip(gap[None, :] - (np.add.accumulate(room, axis=0) - room), 0, room)
            near = np.where(x < 128, x + step, x - step)
            s = kind == 0; D[:, s] = -1; T[:, s] = -1; T[15, s] = n[s]
            s = kind == 1; D[:, s] = -1; T[:, s] = -1
            s = kind == 2; D[:, s] = full[:, s]; T[:, s] = -1
            s = kind == 3; D[:, s] = full[:, s]; T[:, s] = full[::-1][:, s]
            s = kind == 4; D[:, s] = n[s]; T[:, s] = -1; T[15, s] = n[s]
            s = kind == 5; D[:, s] = full[:, s] & ~1; T[:, s] = full[::-1][:, s] | 1
            s = kind == 6; D[:, s] = -1; D[15, s] = n[s]; T[:, s] = -1; T[0, s] = n[s]
            s = kind == 7; D[:, s] = -1; D[0, s] = n[s]; T[:, s] = -1; T[15, s] = n[s] ^ 1
            s = kind == 8; D[:, s] = -1; D[7, s] = n[s]; D[8, s] = (n[s] + 5) % W; T[:, s] = -1; T[15, s] = n[s]; T[3, s] = n[s] ^ 1
            s = kind == 9; D[:, s] = n[s]; D[0, s] = n[s] ^ 1; T[:, s] = n[s]
            s = (kind == 4) | (kind == 6) | (kind == 8) | (kind == 9); z[q, g][:, s] = near[:, s]
    k = rng.integers(0, 6, (N, 8, 1, SV)); more = rng.integers(0, W, (2, N, 8, 16, SV))
    st = np.where(k == 4, sc[:, :, ::-1], st)
    sc = np.where((k == 0) | (k == 2), -1, np.where(k == 1, more[0], sc)); st = np.where((k == 0) | (k == 3), -1, np.where(k == 1, more[1], st))
    return pack(clk, sc, st, d, t, z, th)
def setup_inputs_crowd(rng):
    clk, sc, st, d, t, z, th = parts(rng, 1); h = SV >> 1
    def high(*shape):
        return h + rng.integers(0, h - 1, shape) + SV * rng.integers(0, W // SV, shape)
    for q in range(N):
        for g in (0, 1):
            keep = d[q, g, :, M - 1].copy(), z[q, g, :, M - 1].copy()
            z[q, g] = rng.permuted(np.repeat(rng.integers(0, 256, (16, 1)), M, axis=1), axis=0); t[q, g] = -1
            if g == 1: d[q, g, :, M - 1], z[q, g, :, M - 1] = keep; t[q, g, 15, M - 1] = W - 1
        for g in (2, 3):
            v = int(rng.choice(np.array([0, SV - 1, SV >> 1]))); n = v + SV * rng.integers(0, W // SV, (16, M))
            t[q, g] = np.where(rng.random((16, M)) < 0.5, n, -1); t[q, g, 9] = n[9]; d[q, g] = -1
            if g == 3: d[q, g, 15, M - 1] = (v + 1) % W
        for g in (6, 7):
            n = rng.integers(0, W, M); z[q, g] = clk[q, g][:, n]; t[q, g, 5] = n
            d[q, g] = -1; d[q, g, 15] = n
            if g == 7: d[q, g, 15, M - 1] = -1
    for g, c, lim in ((4, 20, 219), (5, 35, 212)):
        clk[:, g] = rng.integers(0, 8, (N, 16, W)); clk[:, g, :, W - 1] = c
        d[:, g] = high(N, 16, M); t[:, g] = rng.permuted(d[:, g], axis=1)
        sc[:, g, :, :h] = high(N, 16, h); st[:, g, :, :h] = rng.permuted(sc[:, g, :, :h], axis=1)
        z[:, g] = rng.integers(0, 7, (N, 16, M))
        for q in range(N):
            z[q, g, :, M - 1] = 6 + (np.arange(16) < 4 + q)
            b = (q + int(np.sum(HOPS[:-1]))) % N; sc[b, g, :, 100 + q] = W - 1; st[b, g, :, 100 + q] = W - 1
            th[(b + HOPS[-1]) % N, g] = lim - q
    d[:, 5, 15, 0] = -1
    return pack(clk, sc, st, d, t, z, th)
def check_inputs(d):
    bad = []
    for k, lo, hi in (("clk", 0, 255), ("z0", 0, 255), ("sc", -1, W - 1), ("st", -1, W - 1), ("dl", -1, W - 1), ("tl", -1, W - 1), ("th", 0, 4080)):
        a = np.asarray(d[k]).astype(np.float64)
        if not (np.min(a) >= lo and np.max(a) <= hi): bad.append("range of " + k)
        elif np.any(a != np.floor(a)): bad.append("whole numbers in " + k)
    h = np.asarray(d["th"]).reshape(-1, 16)
    if np.any(h != h[:, :1]): bad.append("th alike in a group")
    return bad
def reference(clk, sc, st, dl, tl, z0, th):
    X = clk.astype(np.float32).astype(np.int64).reshape(N, 8, 16, W); Z = z0.astype(np.float32).astype(np.int64).reshape(N, 8, 16, M)
    C = sc.astype(np.int64).reshape(N, 8, 16, SV); S = st.astype(np.int64).reshape(N, 8, 16, SV)
    D = dl.astype(np.int64).reshape(N, 8, 16, M); T = tl.astype(np.int64).reshape(N, 8, 16, M)
    base = th.astype(np.int64).reshape(N, 8, 16)[:, :, 0]; A = np.zeros((N, 8), np.int64); row = np.arange(16).reshape(1, 16, 1)
    for visit in range(RO):
        nd, nt, nz = [], [], []
        for a in range(N):
            d, t, z = D[a], T[a], Z[a]
            x = np.take_along_axis(X[a], np.maximum(d, 0).reshape(8, 1, 16 * M), 2).reshape(8, 16, 16, M)
            y = np.take_along_axis(X[a], np.maximum(t, 0).reshape(8, 1, 16 * M), 2).reshape(8, 16, 16, M)
            dist = np.sum(np.abs(x - z[:, :, None, :]), axis=1)
            score = np.where(t >= 0, np.sum(np.minimum(y, z[:, :, None, :]), axis=1), -1)
            ks = np.argmax(score, axis=1)
            has = np.any(t >= 0, axis=1); v = np.take_along_axis(t, ks[:, None, :], 1)[:, 0] & (SV - 1)
            eq = (d[:, :, None, :] == t[:, None, :, :]) & (d >= 0)[:, :, None, :]
            cd = np.any(eq, axis=2); ct = np.any(eq, axis=1)
            lim = base[a] + 8 * (A[a] & 31)
            abort = np.any(cd & (dist > lim[:, None, None]), axis=1)
            d1 = np.where(cd, -1, d); t1 = np.where(ct | (row == ks[:, None, :]), -1, t)
            left = np.any(d1 >= 0, axis=1); proof = has & ~abort & ~left; go = has & ~abort & left
            yk = np.take_along_axis(y, ks[:, None, None, :], 2)[:, :, 0]
            top = np.max(np.where((d1 >= 0)[:, None, :, :], x, 0), axis=2)
            cv = np.take_along_axis(C[a], v[:, None, :], 2); sv = np.take_along_axis(S[a], v[:, None, :], 2)
            u = np.sum(z, axis=1) & (SV - 1)
            cu = np.take_along_axis(C[a], u[:, None, :], 2); su = np.take_along_axis(S[a], u[:, None, :], 2)
            hd = np.any(cv[:, :, None, :] == d[:, None, :, :], axis=2); ht = np.any(sv[:, :, None, :] == t[:, None, :, :], axis=2)
            d2 = np.where((d1 < 0) & ~hd, cv, d1); t2 = np.where((t1 < 0) & ~ht, sv, t1)
            ab = abort[:, None, :]; on = go[:, None, :]
            nd.append(np.where(ab, cv, np.where(on, d2, cu))); nt.append(np.where(ab, sv, np.where(on, t2, su)))
            nz.append(np.where(ab, np.abs(z - yk), np.where(on, (yk + top) >> 1, z)))
            A[a] += np.sum(cd & ~ab, axis=(1, 2))
            for g in range(8):
                for m in np.nonzero(proof[g])[0]: C[a, g, :, v[g, m]] = t1[g, :, m]
        D, T, Z = np.stack(nd), np.stack(nt), np.stack(nz)
        if visit < RO - 1: D, T, Z = [np.roll(b, HOPS[visit], axis=0) for b in (D, T, Z)]
    return {"yd": D.reshape(N, 128, M).astype(np.float32), "yt": T.reshape(N, 128, M).astype(np.float32), "yz": Z.reshape(N, 128, M).astype(np.float32), "ys": C.reshape(N, 128, SV).astype(np.float32)}

@@ -1,0 +1,648 @@
+from concourse.mybir import AluOpType, ActivationFunctionType
+
+OP = AluOpType
+AF = ActivationFunctionType
+NH = 2
+n = 80
+NM = 160
+G16 = 16 * n
+VIS = 4
+CW = 4112
+EQ = "vvs"
+PH = ["S", 0, 0]
+BIAS = {('y', 1): -6593, ('P', 0): -437, ('m', 0): -1080, ('l', 1): 1848, (3, 1): -469, ('l', 0): -1593, ('A', 0): -7776, ('m', 1): -1226, (0, 0): -1353,
+        ('c', 0): 1837, ('k', 1): 116, ('z', 0): 2276, (2, 1): 1600, (2, 0): -144, ('h', 1): 702, ('d', 1): 926, ('q', 1): -665, ('z', 1): -13,
+        ('r', 0): 25389, (1, 1): -21, ('d', 0): 380, ('h', 0): -302, ('r', 1): -434, ('c', 1): -2889, (3, 0): -495, (1, 0): -675, ('y', 0): -6007,
+        ('S', 0): -356, ('q', 0): -98, ('k', 0): 13095, (0, 1): -341, ('x', 0): -1682, ('x', 1): 84}
+
+SCRATCH = {}
+_W = {}
+
+
+def _buf(name, cols, dtype, where="sbuf"):
+    SCRATCH[name] = (where, [128, cols], dtype)
+    _W[name] = where
+
+
+for _i in range(8):
+    _buf("p%d" % _i, 512, "float32", "psum")
+_buf("clkw", CW, "bfloat16")
+for _nm, _c in (("dli", NM), ("tli", NM), ("sci", 256), ("sti", 256), ("thi", 1)):
+    _buf(_nm, _c, "int32")
+_buf("zin", NM, "bfloat16")
+_buf("tf", 256, "float32"); _buf("tf2", 256, "float32")
+_buf("sct", 256 + NM, "float32")
+_buf("stt", 256, "float32")
+_buf("ic", NM, "int32"); _buf("ik", 1, "int32"); _buf("id4", NM, "int32"); _buf("im", NM, "int32")
+_buf("kf", 4, "float32"); _buf("kdi", 1, "int32"); _buf("kmi", 1, "int32"); _buf("K16", 16, "float32")
+for _nm in ("BD", "ID", "I4096", "N25", "NI", "HI", "N512", "N8192", "BDa", "BDr"):
+    _buf(_nm, 128, "bfloat16")
+_buf("BDf", 128, "float32"); _buf("R15f", 128, "float32")
+_buf("RR", 2048, "float16"); _buf("SS", 2048, "bfloat16"); _buf("bia", 10, "bfloat16")
+_buf("seg0", G16, "bfloat16"); _buf("segM", G16, "bfloat16"); _buf("segV", 96, "float32")
+_buf("LOW", NM, "bfloat16"); _buf("co", 10, "uint16"); _buf("DUM", 10, "float32"); _buf("dmi", 10, "int32")
+_buf("thc", 1, "float32"); _buf("lim", 1, "float32"); _buf("As", 1, "int32"); _buf("Am", 1, "int32"); _buf("ac", 2, "float32")
+_buf("t1s", NM, "float32"); _buf("pv", 10, "float32"); _buf("pvb", 10, "bfloat16")
+_buf("VBs", NM, "bfloat16"); _buf("VL", NM, "bfloat16"); _buf("eb", NM, "bfloat16"); _buf("el", 16 * 45, "bfloat16")
+_buf("lo", NM, "bfloat16"); _buf("l0", 10, "float32"); _buf("xa", 10, "float32"); _buf("sou", 10, "uint16")
+_buf("yso", 256, "float32"); _buf("fin", 480, "float32")
+for _h in range(NH):
+    for _t in range(VIS):
+        _buf("msg%d%d" % (_t, _h), 320, "float16")
+        if _t < VIS - 1:
+            _buf("out%d%d" % (_t, _h), 240, "float16")
+    for _nm, _c, _d in (("offT", n, "uint16"), ("off1", n, "uint16"), ("Y", G16, "bfloat16"), ("X", G16, "bfloat16"), ("mn", G16, "bfloat16"),
+                        ("eq", G16, "bfloat16"), ("ea", 480, "bfloat16"), ("ab", 2 * G16, "bfloat16"), ("sm", 2 * G16, "bfloat16"),
+                        ("tp", G16, "bfloat16"), ("bf", 1840, "bfloat16"), ("f3", 1104, "float32"), ("hf", 160, "float16"),
+                        ("li", 16, "int32"), ("uv", 10, "int32"), ("lu", 16, "uint16"), ("lf", 40, "float32")):
+        _buf(_nm + str(_h), _c, _d)
+
+SEMAPHORES = ["sv", "ss", "st_", "sg", "snd"] + ["ld%d" % i for i in range(7)] + ["arr%d%d" % (t, h) for t in range(1, VIS) for h in range(NH)] + ["wr0", "wr1"]
+
+
+def F(name, a=0, b=None, s=1):
+    if b is None:
+        b = SCRATCH[name][1][1]
+    return (name, a, b, s)
+
+
+def IND(win, off):
+    return ("IND", win, off)
+
+
+def _build():
+    ops = []
+
+    def add(q, call, args, reads, writes, cost, **kw):
+        d = {"ph": tuple(PH), "q": q, "call": call, "args": args, "r": reads, "w": writes, "cost": cost, "id": len(ops)}
+        d.update(kw)
+        ops.append(d)
+
+    def rd(*refs):
+        res = []
+        for x in refs:
+            res += [x[1], x[2]] if x[0] == "IND" else [x]
+        return res
+
+    def wid(x):
+        return 16 * (x[2][2] - x[2][1]) if x[0] == "IND" else -(-(x[2] - x[1]) // x[3])
+
+    def two(x):
+        return SCRATCH[x[0]][2] in ("bfloat16", "float16", "uint16")
+
+    def ps(x):
+        return _W[x[0]] == "psum"
+
+    CY = 0.83
+
+    def vcost(out, ins, tt):
+        k = wid(out)
+        if any(x[0] == "IND" for x in ins):
+            return 50 + 1.56 * CY * k
+        if out[0] == "IND":
+            return 50 + 3.8 * CY * k
+        if tt:
+            k = k if any(ps(x) for x in ins) else 2 * k
+        elif all(two(x) for x in ins + [out]):
+            k = k / 2
+        return max(64, k) * CY
+
+    def TT(out, a, b, op):
+        add("v", "tt", (out, a, b, op), rd(a, b), [out], vcost(out, [a, b], True))
+
+    def TS(out, a, s1, op0, s2=None, op1=None):
+        sr = [x for x in (s1, s2) if isinstance(x, tuple)]
+        add("v", "ts", (out, a, s1, s2, op0, op1), rd(a) + sr, [out], vcost(out, [a], False))
+
+    def CP(out, a):
+        w = [out[1]] if out[0] == "IND" else [out]
+        add("v", "cp", (out, a), rd(a) + ([out[2]] if out[0] == "IND" else []), w, vcost(out, [a], False))
+
+    def MS(out, c):
+        add("v", "ms", (out, c), [], [out], max(64, wid(out) * (0.5 if two(out) else 1)) * CY)
+
+    def SC(out, d0, d1, init, op0, op1):
+        add("v", "sc", (out, d0, d1, init, op0, op1), [d0, d1], [out], vcost(out, [d0, d1], False))
+
+    def VT(out, a):
+        add("v", "vt", (out, a), [a], [out], vcost(out, [a], False))
+
+    def ACT(out, a, f, bias=0.0, scale=1.0, acc=None):
+        k = wid(out)
+        c = 65 + 1.56 * CY * k if a[0] == "IND" else max(64, k) * CY
+        add("s", "act", (out, a, f, bias, scale, acc), rd(a) + [x for x in (bias, scale) if isinstance(x, tuple)], [out] + ([acc] if acc else []), c)
+
+    def MM(lst, more=False, cont=False):
+        c = 0
+        for (o, l, r) in lst:
+            c += max(64, wid(r)) * 0.42 * (4 if SCRATCH[r[0]][2] == "float32" else 1)
+        reads = [x[1] for x in lst] + [x[2] for x in lst]
+        add("t", "mm", (lst, not cont, not more), reads, [x[0] for x in lst], c)
+
+    def LD(q, out, name, sem):
+        add(q, "ld", (out, name), [], [out], 50, dma=sem, lat=6000 if name == "clk" else 2500)
+
+    def IO(x, c):
+        add("g", "iota", (x, [[0, wid(x)]], c, 0), [], [x], 130 + 1.7 * wid(x))
+
+    def AS(x, c):
+        add("g", "asel", (x, [[0, wid(x) // 16], [1, 16]], c), [x], [x], 170 + 1.7 * wid(x))
+
+    LD("y", F("tli"), "tl", "ld0")
+    LD("y", F("dli"), "dl", "ld1")
+    LD("y", F("zin"), "z0", "ld2")
+    LD("y", F("thi"), "th", "ld3")
+    LD("y", F("sci"), "sc", "ld4")
+    LD("y", F("sti"), "st", "ld5")
+    LD("s", F("clkw", 16, CW), "clk", "ld6")
+    add("g", "iota", (F("ik"), [[0, 1]], 0, 1), [], [F("ik")], 135)
+    add("g", "iota", (F("ic"), [[1, NM]], 0, 0), [], [F("ic")], 400)
+    add("g", "iota", (F("dmi"), [[16, 10]], 256, 0), [], [F("dmi")], 150)
+    MS(F("clkw", 0, 16), -1.0)
+    TS(F("kdi"), F("ik"), 4, OP.arith_shift_right)
+    TS(F("kmi"), F("ik"), 15, OP.bitwise_and)
+    CP(F("kf", 0, 1), F("ik"))
+    CP(F("kf", 1, 2), F("kdi"))
+    CP(F("kf", 2, 3), F("kmi"))
+    TS(F("id4"), F("ic"), 4, OP.arith_shift_right)
+    TS(F("BD"), F("id4", 0, 128), F("kf", 1, 2), OP.is_equal)
+    TS(F("K16"), F("ic", 0, 16), F("kf", 2, 3), OP.is_equal)
+    TS(F("ID"), F("ic", 0, 128), F("kf", 0, 1), OP.is_equal)
+    for q in range(16):
+        TS(F("RR", 128 * q, 128 * q + 128), F("BD"), F("K16", q, q + 1), OP.mult)
+    IO(F("SS"), 0)
+    IO(F("segM"), 0)
+    AS(F("segM"), 8192.0)
+    IO(F("seg0"), 1)
+    AS(F("seg0"), 0.0)
+    for q in range(16):
+        ACT(F("SS", 129 * q, 128 * q + 128, 16), F("BD", q, 128, 16), AF.Copy)
+    for nm, src, c in (("I4096", "ID", 4096.0), ("NI", "ID", -1.0), ("HI", "ID", 0.5), ("N512", "ID", -512.0), ("N8192", "ID", -8192.0),
+                       ("N25", "ID", -33554432.0), ("BDa", "BD", -128.0), ("BDr", "BD", -2.125), ("BDf", "BD", 1.0)):
+        ACT(F(nm), F(src), AF.Copy, 0.0, c)
+    ACT(F("R15f"), F("BD"), AF.Copy, 0.0, F("K16", 15, 16))
+    MS(F("segV"), 1000000.0)
+    MS(F("segV", 0, 96, 16), -1000000.0)
+    MS(F("bia"), 0.0)
+    MS(F("bia", 5, 10), -1.0 / 16)
+    for h in range(NH):
+        MS(F("f3%d" % h, 0, 96), 0.0)
+    CP(F("tf", 0, NM), F("tli"))
+    ACT(F("t1s"), F("tf", 0, NM), AF.Copy, 0.0, 3.0)
+    TT(F("t1s"), F("t1s"), F("tf", 0, NM), OP.min)
+    for h in range(NH):
+        m = "msg0%d" % h
+        TS(F(m, n, 2 * n), F("t1s", h * n, h * n + n), -2047.0, OP.add)
+        TS(F(m, 0, n), F("dli", h * n, h * n + n), -2047.0, OP.add)
+        CP(F(m, 2 * n, 3 * n), F("zin", h * n, h * n + n))
+    CP(F("thc"), F("thi"))
+    TS(F("kf", 3, 4), F("kf", 2, 3), -1.0 / 16, OP.mult, 31.0 / 32, OP.add)
+    TT(F("thc"), F("thc"), F("kf", 3, 4), OP.add)
+    CP(F("lim"), F("thc"))
+    MS(F("As"), 0)
+    TS(F("sct", 0, 256), F("sci"), 1.0, OP.add)
+    MS(F("sct", 256, 256 + NM), 0.0)
+    CP(F("tf2"), F("sti"))
+    ACT(F("stt"), F("tf2"), AF.Copy, 0.0, 3.0)
+    TT(F("stt"), F("stt"), F("tf2"), OP.min)
+    ACT(F("stt"), F("stt"), AF.Copy, -2047.0)
+    TS(F("im"), F("ic"), 15, OP.bitwise_and)
+    TS(F("LOW"), F("im"), F("kf", 2, 3), OP.is_ge, 1024.0, OP.mult)
+    CP(F("co"), F("ic", 0, 10))
+    TS(F("DUM"), F("dmi"), F("kf", 2, 3), OP.add)
+
+    def Rq(q):
+        return F("RR", 128 * q, 128 * q + 128)
+
+    def Sq(q):
+        return F("SS", 128 * q, 128 * q + 128)
+
+    CH = [list(range(0, 6)), list(range(6, 12)), list(range(12, 16))]
+
+    def visit(t, h):
+        last = t == VIS - 1
+        H = str(h)
+        m = "msg%d%d" % (t, h)
+        D, TL, Z, ts = F(m, 0, n), F(m, n, 2 * n), F(m, 2 * n, 3 * n), F(m, 3 * n, 4 * n)
+        B = ["p%d" % (4 * h + i) for i in range(4)]
+        ID, N8, BD = F("ID"), F("N8192"), F("BD")
+
+        def bf(i, k=1):
+            return F("bf" + H, i * n, (i + k) * n)
+
+        def f3(a, b):
+            return F("f3" + H, a, b)
+
+        def lf(i):
+            return F("lf" + H, 8 * i, 8 * i + 5)
+
+        def lu(i):
+            return F("lu" + H, 8 * i, 8 * i + 5)
+
+        def eqs(q, k=1):
+            return F("eq" + H, q * n, (q + k) * n)
+        offT, off1, clk = F("offT" + H), F("off1" + H), F("clkw")
+        PH[0] = "y"
+        TS(offT, TL, 2063.0, OP.add)
+        ACT(F("Y" + H), IND(clk, offT), AF.Copy)
+        PH[0] = "q"
+        for j, qs in enumerate(CH):
+            bk = B[j % 2]
+            for i, q in enumerate(qs):
+                o = F(bk, i * n, i * n + n)
+                MM([(o, Rq(q), TL)] + ([(o, F("NI"), D)] if EQ[j] == "s" else []))
+            if EQ[j] == "s":
+                k = len(qs)
+                ACT(F("ea" + H, 0, k * n), F(bk, 0, k * n), AF.Abs)
+                ACT(eqs(qs[0], k), F("ea" + H, 0, k * n), AF.Relu, 1.0, -1.0)
+            else:
+                for i, q in enumerate(qs):
+                    TT(eqs(q), D, F(bk, i * n, i * n + n), OP.is_equal)
+        cdp, ctp = F(B[2], 0, n), F(B[2], n, 2 * n)
+        ACT(bf(21), TL, AF.Sign, 2048.5)
+        MM([(F(B[3], 240, 320), BD, bf(21))])
+        rs = bf(6)
+        ACT(rs, F(B[3], 240, 320), AF.Relu, -15.0, -1.0)
+        for j, qs in enumerate(CH):
+            MM([(cdp, F("I4096"), eqs(q)) for q in qs], j < 2, j > 0)
+        for j, qs in enumerate(CH):
+            MM([(ctp, Sq(q), eqs(q)) for q in qs], j < 2, j > 0)
+        PH[0] = "x"
+        d1 = f3(96, 176)
+        TT(d1, D, cdp, OP.subtract)
+        TS(off1, d1, -2048.0, OP.max, 2063.0, OP.add)
+        ACT(F("X" + H), IND(clk, off1), AF.Copy)
+        fl = bf(0)
+        ACT(fl, d1, AF.Sign, 2047.5)
+        cdb, ctb = bf(1), bf(2)
+        ACT(bf(1, 2), F(B[2], 0, 2 * n), AF.Copy, 0.0, 1.0 / 4096)
+        PH[0] = "m"
+        zps, tlp = F(B[3], 400, 480), F(B[3], 320, 400)
+        MM([(zps, ID, Z)])
+        MM([(tlp, ID, TL)])
+        for q in range(16):
+            TT(F("mn" + H, q * n, q * n + n), F("Y" + H, q, G16, 16), zps, OP.min)
+        Gp, scp, kbp = F(B[1], 0, n), F(B[0], 0, n), F(B[0], n, 2 * n)
+        MM([(Gp, BD, Z)] + [(Gp, Sq(q), F("Y" + H, q, G16, 16)) for q in range(16)])
+        for j, qs in enumerate(CH):
+            MM([(scp, Sq(q), F("mn" + H, q * n, q * n + n)) for q in qs], j < 2, j > 0)
+        PH[0] = "k"
+        nk = f3(0, n)
+        ACT(nk, scp, AF.Identity, F("lim"), 2.0)
+        vt, vs, vb = f3(176, 272), f3(272, 368), f3(368, 464)
+        VT(vt, f3(0, 96))
+        SC(vs, F("segV"), vt, -1000000.0, OP.min, OP.max)
+        VT(vb, vs)
+        MM([(kbp, F("R15f"), f3(368, 448))])
+        oh, far, fc = bf(3), bf(4), bf(5)
+        TT(far, nk, Gp, OP.is_lt)
+        TT(fc, far, ctp, OP.mult)
+        TT(oh, nk, kbp, OP.is_equal)
+        TT(ts, oh, tlp, OP.mult)
+        lst = F(B[0], 160, 170)
+        MM([(lst, Sq(r), F(m, 2 * n + r, 4 * n, 16)) for r in range(16)] + [(lst, BD, F("bia"))])
+        PH[0] = "c"
+        cp = F(B[1], n, 2 * n)
+        MM([(cp, BD, fl), (cp, F("BDa"), fc), (cp, F("BDr"), rs)])
+        nm1, sq, q0, nm2, nm3, abm = bf(7), bf(9), bf(10), bf(11), bf(12), bf(18)
+        ACT(sq, cp, AF.Square, 32.5)
+        ACT(q0, cp, AF.Abs, 2048.0, 128.0)
+        ACT(nm1, cp, AF.Relu, -15.0, -1.0)
+        ACT(nm2, cp, AF.Relu, 80.0)
+        if not last:
+            ACT(abm, cp, AF.Relu, -65536.0 * 80, -65536.0)
+            TT(bf(8), cdp, abm, OP.is_gt)
+            ACT(bf(22), bf(8), AF.Copy, 0.0, 1.0, F("ac", h, h + 1))
+        ACT(nm3, sq, AF.Relu, -324.0)
+        PH[0] = "l"
+        sql = F(B[0], 170, 180)
+        MM([(sql, Sq(r), F("bf" + H, 9 * n + r, 11 * n, 16)) for r in range(16)])
+        TS(lu(0), F(B[0], 165, 170), 2064.0, OP.add)
+        yk = bf(13)
+        ACT(yk, IND(clk, lu(0)), AF.Copy)
+        CP(F("li" + H, 0, 10), lst)
+        TS(F("uv" + H), F("li" + H, 0, 10), 255, OP.bitwise_and)
+        uu, v32 = F("uv" + H, 0, 5), F("uv" + H, 5, 10)
+        TT(lf(0), v32, uu, OP.subtract)
+        nu = lf(1)
+        TS(nu, F(B[0], 170, 175), 5184.0, OP.is_gt)
+        TT(F("pv", 5 * h, 5 * h + 5), v32, F(B[0], 175, 180), OP.max)
+        TT(lf(2), lf(0), nu, OP.mult)
+        TT(lf(3), lf(2), uu, OP.add)
+        CP(lu(1), lf(3))
+        cs, csD, csT = F("hf" + H), F("hf" + H, 0, n), F("hf" + H, n, 2 * n)
+        TS(csD, IND(F("sct", 0, 256), lu(1)), -2048.0, OP.add)
+        CP(csT, IND(F("stt"), lu(1)))
+        PH[0] = "h"
+        for e in range(2):
+            for j, qs in enumerate(CH):
+                bk = B[(j + e) % 2]
+                for i, q in enumerate(qs):
+                    o = F(bk, i * n, i * n + n)
+                    MM([(o, Rq(q), F(m, e * n, e * n + n)), (o, F("NI"), F("hf" + H, e * n, e * n + n))])
+                for i, q in enumerate(qs):
+                    ACT(F("ab" + H, e * G16 + q, (e + 1) * G16, 16), F(bk, i * n, i * n + n), AF.Abs)
+            SC(F("sm" + H, e * G16, (e + 1) * G16), F("segM", 0, G16), F("ab" + H, e * G16, (e + 1) * G16), 0.0, OP.max, OP.min)
+        PH[0] = "d"
+        dg, tg, t1p = F(B[2], 160, 240), F(B[2], 240, 320), F(B[3], 320, 400)
+        MM([(dg, ID, D), (dg, N8, cdb), (dg, N8, nm1)])
+        MM([(tg, ID, TL), (tg, F("N25"), ctb), (tg, N8, oh), (tg, N8, nm1)])
+        MM([(t1p, ID, TL), (t1p, F("N25"), ctb), (t1p, N8, oh)])
+        ACT(F("t1s", h * n, h * n + n), t1p, AF.Relu, 2048.0)
+        km, kx = bf(14, 2), f3(464, 624)
+        ACT(km, F(B[2], 160, 320), AF.Relu, 2048.0)
+        TS(f3(464, 544), dg, -2048.0, OP.max)
+        TS(f3(544, 624), tg, -2050.0, OP.max)
+        PH[0] = "z"
+        SC(F("tp" + H), F("seg0"), F("X" + H), 0.0, OP.mult, OP.max)
+        zd, z1, z2, z4 = [F(B[3], i * n, i * n + n) for i in range(4)]
+        MM([(zd, ID, Z), (zd, F("NI"), yk)])
+        A2 = bf(19)
+        ACT(A2, zd, AF.Abs)
+        MM([(z1, F("HI"), yk), (z1, F("HI"), F("tp" + H, 15, G16, 16)), (z1, F("N512"), nm1)])
+        MM([(z2, ID, A2), (z2, F("N512"), nm2)])
+        MM([(z4, ID, Z), (z4, F("N512"), nm3)])
+        ACT(f3(624, 704), z1, AF.Identity, -0.25)
+        TT(f3(704, 784), f3(624, 704), z2, OP.max)
+        TT(f3(784, 864), f3(704, 784), z4, OP.max)
+        o = "out%d%d" % (t, h)
+        zo = F("fin", 320 + h * n, 320 + h * n + n) if last else F(o, 160, 240)
+        TS(zo, f3(784, 864), 8388608.0, OP.add, 8388608.0, OP.subtract)
+        PH[0] = "r"
+        hp, hd = F(B[0], 0, 2 * n), bf(16, 2)
+        for e in range(2):
+            x = F(B[0], e * n, e * n + n)
+            MM([(x, ID, F("sm" + H, e * G16 + 15, (e + 1) * G16, 16)), (x, ID, nm1)])
+        ACT(hd, hp, AF.Relu, 1.0, -1.0)
+        rp = F(B[2], 320, 480)
+        MM([(rp, ID, cs), (rp, N8, km), (rp, N8, hd)])
+        if last:
+            TT(f3(944, 1104), kx, rp, OP.max)
+            TS(F("fin", h * n, h * n + n), f3(944, 1024), 2047.0, OP.add, -1.0, OP.max)
+            TS(F("fin", 160 + h * n, 160 + h * n + n), f3(1024, 1104), 2047.0, OP.add, -1.0, OP.max)
+        else:
+            TT(F(o, 0, 160), kx, rp, OP.max)
+            add("g", "send", (t, h), [F(o)], [], 200)
+            add("n", "arrive", (t, h), [], [F("msg%d%d" % (t + 1, h), 0, 240)], 0, arr=(t + 1, h))
+
+    def proofs(t):
+        pb = "p7"
+        TS(F("pvb"), F("pv"), 4096.0, OP.min)
+        VB, lp, ll = F(pb, 0, NM), F(pb, NM, 2 * NM), F(pb, 488, 498)
+        for r in range(16):
+            MM([(F(pb, r, NM, 16), Rq(r), F("pvb"))])
+        ACT(F("VBs"), VB, AF.Copy)
+        TT(F("VL"), F("VBs"), F("LOW"), OP.max)
+        TT(F("eb"), IND(F("pv"), F("co")), F("VL"), OP.is_equal)
+        lst = [(lp, F("BD"), F("eb"))]
+        a = 0
+        for c in range(1, 10):
+            TS(F("el", a, a + 16 * c), F("VBs", 0, 16 * c), F("pv", c, c + 1), OP.is_equal)
+            lst.append((F(pb, NM, NM + 16 * c), F("BD"), F("el", a, a + 16 * c)))
+            a += 16 * c
+        MM(lst)
+        ACT(F("lo"), lp, AF.Copy)
+        MM([(ll, Sq(r), F("lo", r, NM, 16)) for r in range(16)])
+        TS(F("l0"), ll, 0.5, OP.is_gt, 4096.0, OP.mult)
+        TT(F("xa"), F("l0"), F("pv"), OP.add)
+        TT(F("xa"), F("xa"), F("DUM"), OP.min)
+        CP(F("sou"), F("xa"))
+        CP(IND(F("sct"), F("sou")), F("t1s"))
+
+    def count():
+        pa = F("p7", 504, 505)
+        MM([(pa, F("BDf"), F("ac", 0, 1)), (pa, F("BDf"), F("ac", 1, 2))])
+        TT(F("As"), F("As"), pa, OP.add)
+        TS(F("Am"), F("As"), 31, OP.bitwise_and)
+        TS(F("lim"), F("Am"), 8.0, OP.mult, F("thc"), OP.add)
+
+    for t in range(VIS):
+        for h in range(NH):
+            PH[1:] = [t, h]
+            visit(t, h)
+        PH[:] = ["A", t, 0]
+        if t < VIS - 1:
+            count()
+        PH[:] = ["P", t, 0]
+        proofs(t)
+    PH[:] = ["E", 0, 0]
+    TS(F("yso"), F("sct", 0, 256), -1.0, OP.add)
+    add("y", "sto", [("yd", 0), ("yt", 160), ("yz", 320)], [F("fin")], [], 100, dma="wr0", lat=2500)
+    add("y", "stys", None, [F("yso")], [], 50, dma="wr1", lat=2500)
+    return ops
+
+
+def _overlap(a, b):
+    if a[0] != b[0] or a[1] >= b[2] or b[1] >= a[2]:
+        return False
+    return not (a[3] == b[3] and a[3] > 1 and (a[1] - b[1]) % a[3])
+
+
+def _covers(a, b):
+    return a[3] == 1 and a[1] <= b[1] and a[2] >= b[2] or a == b
+
+
+def _deps(ops):
+    hist = {}
+    sends = {}
+    for o in ops:
+        dep = {}
+        acc = [(x, False) for x in o["r"]] + [(x, True) for x in o["w"]]
+        for (x, wr) in acc:
+            psum = _W[x[0]] == "psum"
+            for (y, ywr, yo) in hist.get(x[0], []):
+                if yo is o:
+                    continue
+                same = yo["q"] == o["q"]
+                if psum and not same:
+                    dep[yo["id"]] = True
+                elif psum and o["q"] == "t":
+                    dep.setdefault(yo["id"], False)
+                elif (wr or ywr) and _overlap(x, y):
+                    need = (not same) or (ywr and o["q"] != "t")
+                    dep[yo["id"]] = dep.get(yo["id"], False) or need
+        for (x, wr) in acc:
+            L = hist.setdefault(x[0], [])
+            if wr:
+                ps = _W[x[0]] == "psum"
+                L[:] = [e for e in L if e[2] is o or not (_covers(x, e[0]) and (not ps or e[2]["q"] == o["q"]))]
+            L.append((x, wr, o))
+        if o["call"] == "send":
+            sends[o["args"]] = o["id"]
+        if o["call"] == "arrive":
+            dep[sends[o["args"]]] = False
+        o["dep"] = dep
+
+
+LAT = {"x": 130.0, "own": 80.0, "arr": 3800.0, "fix": 20.0}
+SCALE = 1.1
+
+
+def _schedule(ops, seed=0):
+    succ = [[] for _ in ops]
+    for o in ops:
+        for d in o["dep"]:
+            succ[d].append(o["id"])
+
+    def dly(a, b):
+        if a["call"] == "send":
+            return LAT["arr"] if b["call"] == "arrive" else 0.0
+        if "dma" in a:
+            return a["lat"]
+        if not b["dep"][a["id"]]:
+            return 0.0
+        return LAT["own"] if a["q"] == b["q"] else LAT["x"]
+    pri = [0.0] * len(ops)
+    for o in reversed(ops):
+        pri[o["id"]] = o["cost"] + max([pri[s] + dly(o, ops[s]) for s in succ[o["id"]]] + [0.0])
+    pri = [p + BIAS.get((o["ph"][0], o["ph"][2]), 0.0) + BIAS.get(o["ph"][1:], 0.0) for p, o in zip(pri, ops)]
+    left = [len(o["dep"]) for o in ops]
+    rt = [0.0] * len(ops)
+    ready, free, order, start, end = {}, {}, {}, [0.0] * len(ops), 0.0
+    for o in ops:
+        if not left[o["id"]]:
+            ready.setdefault(o["q"], []).append(o["id"])
+    for _ in range(len(ops)):
+        best = None
+        for q, L in ready.items():
+            f = free.get(q, 0.0)
+            for i in L:
+                k = (rt[i] if q == "n" else max(f, rt[i]), -pri[i])
+                if best is None or k < best[0]:
+                    best = (k, q, i)
+        (s, _p), q, i = best
+        ready[q].remove(i)
+        o = ops[i]
+        e = s + o["cost"] + (0.0 if q == "n" else LAT["fix"])
+        start[i] = s
+        free[q] = e
+        end = max(end, e)
+        order.setdefault(q, []).append(i)
+        for x in succ[i]:
+            rt[x] = max(rt[x], e + dly(o, ops[x]))
+            left[x] -= 1
+            if not left[x]:
+                ready.setdefault(ops[x]["q"], []).append(x)
+    return end, seed, order, start
+
+
+_CACHE = {}
+SEMQ = {"v": "sv", "s": "ss", "t": "st_", "g": "sg"}
+
+
+def _plan():
+    if "p" in _CACHE:
+        return _CACHE["p"]
+    ops = _build()
+    _deps(ops)
+    for o in ops:
+        o["cost"] *= SCALE
+    end, _s, order, start = _schedule(ops)
+    cnt = {}
+    for q, L in order.items():
+        for i in L:
+            o = ops[i]
+            o["start"] = start[i]
+            if "dma" in o:
+                o["tok"] = (o["dma"], 48 if o["call"] == "sto" else 16)
+            elif o["call"] == "arrive":
+                o["tok"] = ("arr%d%d" % o["arr"], None)
+            elif o["call"] != "send":
+                cnt[SEMQ[q]] = cnt.get(SEMQ[q], 0) + 1
+                o["tok"] = (SEMQ[q], cnt[SEMQ[q]])
+    known = {}
+    for i in sorted((i for L in order.values() for i in L), key=lambda i: (ops[i]["start"], i)):
+        o = ops[i]
+        kn = known.setdefault(o["q"], {})
+        w = {}
+        for d in sorted((d for d, nd in o["dep"].items() if nd), key=lambda d: -ops[d]["start"]):
+            s, v = ops[d]["tok"]
+            if v is None:
+                v = 1
+            if kn.get(s, 0) >= v:
+                continue
+            w[s] = max(w.get(s, 0), v)
+            for s2, v2 in list(ops[d]["kn"].items()) + [(s, v)]:
+                kn[s2] = max(kn.get(s2, 0), v2)
+        o["wait"] = sorted(w.items())
+        o["kn"] = dict(kn)
+    _CACHE["p"] = (ops, order, cnt, end)
+    return _CACHE["p"]
+
+
+def rank_program(g, core, T, topo):
+    rank = T.rank_of(core)
+    if rank is None:
+        return
+    ops, order, cnt, _end = _plan()
+    hops = [1, 4, 2]
+    eng = {"v": g.vector, "s": g.scalar, "t": g.tensor, "g": g, "y": g.sync}
+    N = len(T.cores)
+    arrn = [0] + [len(topo.engines(T.cores[(rank - hops[t]) % N], core)) for t in range(VIS - 1)]
+
+    def ap(x):
+        if not isinstance(x, tuple):
+            return x
+        if x[0] == "IND":
+            return ap(x[1]).indirect(ap(x[2]))
+        if x[3] == 1:
+            return T[x[0]][:, x[1]:x[2]]
+        return T[x[0]][:, x[1]:x[2]:x[3]]
+
+    nsend = 0
+    for q in ("y", "s", "v", "t", "g"):
+        e = eng[q]
+        for i in order[q]:
+            o = ops[i]
+            for s, v in o["wait"]:
+                e.wait_ge(T.sem[s], arrn[int(s[3])] if s[:3] == "arr" else v)
+            a, call = o["args"], o["call"]
+            if call == "send":
+                t, h = a
+                dst = T.cores[(rank + hops[t]) % N]
+                rid, pid = topo.addr(dst, core)
+                g.remote_dma(T["msg%d%d" % (t + 1, h)][:, 0:240], T["out%d%d" % (t, h)][:], T.sem["arr%d%d" % (t + 1, h)], T.sem.snd, pid, rid, topo.mask(core, dst))
+                nsend += len(topo.engines(core, dst))
+                continue
+            if call == "ld":
+                e.dma_start(ap(a[0]), T[a[1]][:, :]).then_inc(T.sem[o["dma"]], 16)
+                continue
+            if call == "sto":
+                for nm, c in a:
+                    e.dma_start(T[nm][:, :], T.fin[:, c:c + NM]).then_inc(T.sem[o["dma"]], 16)
+                continue
+            if call == "stys":
+                e.dma_start(T.ys[:, :], T.yso[:, :]).then_inc(T.sem[o["dma"]], 16)
+                continue
+            if call == "mm":
+                lst, st, sp = a
+                for k, (oo, l, r) in enumerate(lst):
+                    ins = e.matmul(ap(oo), ap(l), ap(r), st and k == 0, sp and k == len(lst) - 1)
+            elif call == "tt":
+                ins = e.tensor_tensor(ap(a[0]), ap(a[1]), ap(a[2]), a[3])
+            elif call == "ts":
+                if a[5] is None:
+                    ins = e.tensor_scalar(ap(a[0]), ap(a[1]), ap(a[2]), None, a[4])
+                else:
+                    ins = e.tensor_scalar(ap(a[0]), ap(a[1]), ap(a[2]), ap(a[3]), a[4], a[5])
+            elif call == "cp":
+                ins = e.tensor_copy(ap(a[0]), ap(a[1]))
+            elif call == "ms":
+                ins = e.memset(ap(a[0]), a[1])
+            elif call == "sc":
+                ins = e.tensor_tensor_scan(ap(a[0]), ap(a[1]), ap(a[2]), a[3], a[4], a[5])
+            elif call == "vt":
+                ins = e.transpose(ap(a[0]), ap(a[1]))
+            elif call == "act":
+                kw = {} if a[5] is None else {"accum_out": ap(a[5])}
+                ins = e.activation(ap(a[0]), ap(a[1]), a[2], ap(a[3]), ap(a[4]), **kw)
+            elif call == "iota":
+                ins = e.iota(ap(a[0]), a[1], a[2], a[3], allow_small_or_imprecise_dtypes=True)
+            elif call == "asel":
+                ins = e.affine_select(ap(a[0]), ap(a[0]), a[1], OP.not_equal, a[2], 0, 0)
+            ins.then_inc(T.sem[o["tok"][0]], 1)
+    g.wait_ge(T.sem.snd, nsend)
+    for s, v in sorted(cnt.items()):
+        g.wait_ge(T.sem[s], v)
+    g.wait_ge(T.sem.wr0, 48)
+    g.wait_ge(T.sem.wr1, 16)

@@ -8,19 +8,16 @@ NM = 160
 G16 = 16 * n
 VIS = 4
 CW = 4112
-EQ = "vvs"
+SENDS = [(0, 80), (80, 240)]
 PH = ["S", 0, 0]
-BIAS = {('y', 1): -6593, ('P', 0): -437, ('m', 0): -1080, ('l', 1): 1848, (3, 1): -469, ('l', 0): -1593, ('A', 0): -7776, ('m', 1): -1226, (0, 0): -1353,
-        ('c', 0): 1837, ('k', 1): 116, ('z', 0): 2276, (2, 1): 1600, (2, 0): -144, ('h', 1): 702, ('d', 1): 926, ('q', 1): -665, ('z', 1): -13,
-        ('r', 0): 25389, (1, 1): -21, ('d', 0): 380, ('h', 0): -302, ('r', 1): -434, ('c', 1): -2889, (3, 0): -495, (1, 0): -675, ('y', 0): -6007,
-        ('S', 0): -356, ('q', 0): -98, ('k', 0): 13095, (0, 1): -341, ('x', 0): -1682, ('x', 1): 84}
+BIAS = {(0, 0): 4360, (1, 0): 5000, (2, 0): 3610, (3, 0): 6440, ('y', 1): -37030, ('P', 0): -4710, ('l', 1): -2010, (1, 1): 470, (0, 1): -860, ('l', 0): -60, ('E', 0): 4060, ('g', 1): 10, ('y', 0): -4660, ('r', 0): 4940, ('r', 1): -1280, ('e', 1): 14430, ('x', 1): -10870, (3, 1): 3360, ('q', 0): -1940, ('d', 0): 15140, ('c', 0): 130, ('e', 0): -5260, ('c', 1): 50, ('k', 1): 1300, ('z', 0): -1340, ('f', 0): -640, ('m', 1): -7610, ('A', 0): 4760, ('q', 1): 3420, ('z', 1): 210, ('f', 1): -390, ('k', 0): -1840, (2, 1): 12020, ('d', 1): -190, ('m', 0): -13880, ('x', 0): 15080, ('g', 0): 5650, ('S', 0): 2260}
 
 SCRATCH = {}
 _W = {}
 
 
 def _buf(name, cols, dtype, where="sbuf"):
-    SCRATCH[name] = (where, [128, cols], dtype)
+    SCRATCH[name] = (where, [128] + (cols if isinstance(cols, list) else [cols]), dtype)
     _W[name] = where
 
 
@@ -31,47 +28,61 @@ for _nm, _c in (("dli", NM), ("tli", NM), ("sci", 256), ("sti", 256), ("thi", 1)
     _buf(_nm, _c, "int32")
 _buf("zin", NM, "bfloat16")
 _buf("tf", 256, "float32"); _buf("tf2", 256, "float32")
-_buf("sct", 256 + NM, "float32")
-_buf("stt", 256, "float32")
-_buf("ic", NM, "int32"); _buf("ik", 1, "int32"); _buf("id4", NM, "int32"); _buf("im", NM, "int32")
-_buf("kf", 4, "float32"); _buf("kdi", 1, "int32"); _buf("kmi", 1, "int32"); _buf("K16", 16, "float32")
-for _nm in ("BD", "ID", "I4096", "N25", "NI", "HI", "N512", "N8192", "BDa", "BDr"):
+_buf("sct", 257 + NM, "float32")
+_buf("stt", 257, "float32")
+_buf("ic", 128, "int32"); _buf("ik", 1, "int32"); _buf("i1", 128, "int32"); _buf("i2", 128, "int32"); _buf("i3", 128, "int32")
+_buf("ki", 3, "int32"); _buf("kf", 8, "float32"); _buf("JF", 128, "bfloat16")
+for _nm in ("J1", "J2", "J3", "BD", "ID", "NI", "Ik", "Nh", "Ic", "N8", "P8", "N256", "NU", "P512", "N1024", "PBD8", "NBD8"):
     _buf(_nm, 128, "bfloat16")
-_buf("BDf", 128, "float32"); _buf("R15f", 128, "float32")
-_buf("RR", 2048, "float16"); _buf("SS", 2048, "bfloat16"); _buf("bia", 10, "bfloat16")
-_buf("seg0", G16, "bfloat16"); _buf("segM", G16, "bfloat16"); _buf("segV", 96, "float32")
-_buf("LOW", NM, "bfloat16"); _buf("co", 10, "uint16"); _buf("DUM", 10, "float32"); _buf("dmi", 10, "int32")
+_buf("BDf", 128, "float32")
+_buf("ROT", 2048, "float16"); _buf("AS", 2048, "bfloat16"); _buf("SS", 2048, "bfloat16"); _buf("TRI", 2048, "bfloat16")
+_buf("seg0", G16, "bfloat16"); _buf("EQ", G16, "bfloat16"); _buf("seg32", NM, "float32"); _buf("seg16", NM, "float32")
+_buf("pen", NM, "float16"); _buf("NE", NM, "bfloat16"); _buf("CN", 240, "bfloat16"); _buf("IT", 272, "bfloat16")
+_buf("DUM", 10, "float32"); _buf("CK", 5, "float32"); _buf("dmi", 10, "int32"); _buf("cki", 5, "int32")
 _buf("thc", 1, "float32"); _buf("lim", 1, "float32"); _buf("As", 1, "int32"); _buf("Am", 1, "int32"); _buf("ac", 2, "float32")
-_buf("t1s", NM, "float32"); _buf("pv", 10, "float32"); _buf("pvb", 10, "bfloat16")
-_buf("VBs", NM, "bfloat16"); _buf("VL", NM, "bfloat16"); _buf("eb", NM, "bfloat16"); _buf("el", 16 * 45, "bfloat16")
-_buf("lo", NM, "bfloat16"); _buf("l0", 10, "float32"); _buf("xa", 10, "float32"); _buf("sou", 10, "uint16")
+_buf("t1s", NM, "float32"); _buf("pv", 10, "bfloat16"); _buf("VB", NM, "bfloat16"); _buf("el", 1600, "bfloat16")
+_buf("ls", NM, "float32"); _buf("xa", 10, "float32"); _buf("sou", 10, "uint16")
 _buf("yso", 256, "float32"); _buf("fin", 480, "float32")
+_buf("msg", 240 * NH * VIS, "float16"); _buf("out", 240 * NH * (VIS - 1), "float16")
 for _h in range(NH):
-    for _t in range(VIS):
-        _buf("msg%d%d" % (_t, _h), 320, "float16")
-        if _t < VIS - 1:
-            _buf("out%d%d" % (_t, _h), 240, "float16")
     for _nm, _c, _d in (("offT", n, "uint16"), ("off1", n, "uint16"), ("Y", G16, "bfloat16"), ("X", G16, "bfloat16"), ("mn", G16, "bfloat16"),
-                        ("eq", G16, "bfloat16"), ("ea", 480, "bfloat16"), ("ab", 2 * G16, "bfloat16"), ("sm", 2 * G16, "bfloat16"),
-                        ("tp", G16, "bfloat16"), ("bf", 1840, "bfloat16"), ("f3", 1104, "float32"), ("hf", 160, "float16"),
-                        ("li", 16, "int32"), ("uv", 10, "int32"), ("lu", 16, "uint16"), ("lf", 40, "float32")):
+                        ("eq", G16, "bfloat16"), ("eg", G16, "bfloat16"), ("tp", G16, "bfloat16"), ("bf", 16 * n, "bfloat16"), ("hf", 8 * n, "float16"),
+                        ("f3", 8 * n, "float32"), ("nk", [5, 32], "float32"), ("vs", NM, "int32"), ("ri", n, "int32"),
+                        ("li", 16, "int32"), ("lu", 24, "uint16"), ("lf", 8, "float32")):
         _buf(_nm + str(_h), _c, _d)
 
-SEMAPHORES = ["sv", "ss", "st_", "sg", "snd"] + ["ld%d" % i for i in range(7)] + ["arr%d%d" % (t, h) for t in range(1, VIS) for h in range(NH)] + ["wr0", "wr1"]
+SEMAPHORES = (["sv", "ss", "st_", "sg", "snd"] + ["ld%d" % i for i in range(7)]
+              + ["arr%d%d%d" % (t, h, k) for t in range(1, VIS) for h in range(NH) for k in range(len(SENDS))] + ["wr0", "wr1"])
+
+
+def _cols(name):
+    c = 1
+    for x in SCRATCH[name][1][1:]:
+        c *= x
+    return c
 
 
 def F(name, a=0, b=None, s=1):
-    if b is None:
-        b = SCRATCH[name][1][1]
-    return (name, a, b, s)
+    return (name, a, _cols(name) if b is None else b, s)
+
+
+def BLK(name, j):
+    return (name, 0, _cols(name), 1, j)
 
 
 def IND(win, off):
     return ("IND", win, off)
 
 
+def wid(x):
+    if x[0] == "IND":
+        return 16 * (x[2][2] - x[2][1])
+    return x[2] // 2 if len(x) == 5 else -(-(x[2] - x[1]) // x[3])
+
+
 def _build():
     ops = []
+    PH[:] = ["S", 0, 0]
 
     def add(q, call, args, reads, writes, cost, **kw):
         d = {"ph": tuple(PH), "q": q, "call": call, "args": args, "r": reads, "w": writes, "cost": cost, "id": len(ops)}
@@ -83,9 +94,6 @@ def _build():
         for x in refs:
             res += [x[1], x[2]] if x[0] == "IND" else [x]
         return res
-
-    def wid(x):
-        return 16 * (x[2][2] - x[2][1]) if x[0] == "IND" else -(-(x[2] - x[1]) // x[3])
 
     def two(x):
         return SCRATCH[x[0]][2] in ("bfloat16", "float16", "uint16")
@@ -112,11 +120,11 @@ def _build():
 
     def TS(out, a, s1, op0, s2=None, op1=None):
         sr = [x for x in (s1, s2) if isinstance(x, tuple)]
-        add("v", "ts", (out, a, s1, s2, op0, op1), rd(a) + sr, [out], vcost(out, [a], False))
+        ind = out[0] == "IND"
+        add("v", "ts", (out, a, s1, s2, op0, op1), rd(a) + sr + ([out[2]] if ind else []), [out[1] if ind else out], vcost(out, [a], False))
 
     def CP(out, a):
-        w = [out[1]] if out[0] == "IND" else [out]
-        add("v", "cp", (out, a), rd(a) + ([out[2]] if out[0] == "IND" else []), w, vcost(out, [a], False))
+        add("v", "cp", (out, a), rd(a), [out], vcost(out, [a], False))
 
     def MS(out, c):
         add("v", "ms", (out, c), [], [out], max(64, wid(out) * (0.5 if two(out) else 1)) * CY)
@@ -129,7 +137,7 @@ def _build():
 
     def ACT(out, a, f, bias=0.0, scale=1.0, acc=None):
         k = wid(out)
-        c = 65 + 1.56 * CY * k if a[0] == "IND" else max(64, k) * CY
+        c = 65 + 1.56 * CY * k if a[0] == "IND" else max(64, k) * CY + (20 if acc else 0)
         add("s", "act", (out, a, f, bias, scale, acc), rd(a) + [x for x in (bias, scale) if isinstance(x, tuple)], [out] + ([acc] if acc else []), c)
 
     def MM(lst, more=False, cont=False):
@@ -142,279 +150,251 @@ def _build():
     def LD(q, out, name, sem):
         add(q, "ld", (out, name), [], [out], 50, dma=sem, lat=6000 if name == "clk" else 2500)
 
-    def IO(x, c):
-        add("g", "iota", (x, [[0, wid(x)]], c, 0), [], [x], 130 + 1.7 * wid(x))
+    def IO(x, pat, base, mul):
+        add("g", "iota", (x, pat, base, mul), [], [x], 130 + 1.7 * wid(x))
 
-    def AS(x, c):
-        add("g", "asel", (x, [[0, wid(x) // 16], [1, 16]], c), [x], [x], 170 + 1.7 * wid(x))
+    def blk(name, q):
+        return F(name, 128 * q, 128 * q + 128)
 
+    ID, BD, N8, P8 = F("ID"), F("BD"), F("N8"), F("P8")
+    LD("s", F("clkw", 16, CW), "clk", "ld6")
     LD("y", F("tli"), "tl", "ld0")
     LD("y", F("dli"), "dl", "ld1")
     LD("y", F("zin"), "z0", "ld2")
     LD("y", F("thi"), "th", "ld3")
-    LD("y", F("sci"), "sc", "ld4")
     LD("y", F("sti"), "st", "ld5")
-    LD("s", F("clkw", 16, CW), "clk", "ld6")
-    add("g", "iota", (F("ik"), [[0, 1]], 0, 1), [], [F("ik")], 135)
-    add("g", "iota", (F("ic"), [[1, NM]], 0, 0), [], [F("ic")], 400)
-    add("g", "iota", (F("dmi"), [[16, 10]], 256, 0), [], [F("dmi")], 150)
+    LD("y", F("sci"), "sc", "ld4")
+    IO(F("ik"), [[0, 1]], 0, 1)
+    IO(F("ic"), [[1, 128]], 0, 0)
+    IO(F("i1"), [[-1, 128]], 128, 1)
+    IO(F("dmi"), [[16, 10]], 257, 0)
+    IO(F("cki"), [[256, 5]], 15, 0)
+    IO(F("IT"), [[1, 272]], 0, 0)
     MS(F("clkw", 0, 16), -1.0)
-    TS(F("kdi"), F("ik"), 4, OP.arith_shift_right)
-    TS(F("kmi"), F("ik"), 15, OP.bitwise_and)
-    CP(F("kf", 0, 1), F("ik"))
-    CP(F("kf", 1, 2), F("kdi"))
-    CP(F("kf", 2, 3), F("kmi"))
-    TS(F("id4"), F("ic"), 4, OP.arith_shift_right)
-    TS(F("BD"), F("id4", 0, 128), F("kf", 1, 2), OP.is_equal)
-    TS(F("K16"), F("ic", 0, 16), F("kf", 2, 3), OP.is_equal)
-    TS(F("ID"), F("ic", 0, 128), F("kf", 0, 1), OP.is_equal)
+    TS(F("ki", 0, 1), F("ik"), 4, OP.arith_shift_right)
+    TS(F("ki", 1, 2), F("ik"), 15, OP.bitwise_and)
+    TS(F("ki", 2, 3), F("ik"), 4, OP.arith_shift_right, 1, OP.bitwise_and)
+    CP(F("kf", 0, 3), F("ki"))
+    kg, kp, ko = F("kf", 0, 1), F("kf", 1, 2), F("kf", 2, 3)
+    TS(F("i2"), F("ic"), 4, OP.arith_shift_right)
+    TS(BD, F("i2"), kg, OP.is_equal)
+    TS(F("JF"), F("i2"), kg, OP.not_equal, 99.0, OP.mult)
+    TS(F("i1"), F("i1"), 15, OP.bitwise_and)
+    TS(F("i3"), F("ic"), 15, OP.bitwise_and)
+    TT(F("J1"), F("i1"), F("JF"), OP.max)
+    TT(F("J2"), F("i3"), F("JF"), OP.max)
+    TS(F("J3"), BD, kp, OP.mult)
+    TS(ID, F("J1"), 0.0, OP.is_equal)
     for q in range(16):
-        TS(F("RR", 128 * q, 128 * q + 128), F("BD"), F("K16", q, q + 1), OP.mult)
-    IO(F("SS"), 0)
-    IO(F("segM"), 0)
-    AS(F("segM"), 8192.0)
-    IO(F("seg0"), 1)
-    AS(F("seg0"), 0.0)
+        TS(blk("ROT", q), F("J1"), float(q), OP.is_equal)
     for q in range(16):
-        ACT(F("SS", 129 * q, 128 * q + 128, 16), F("BD", q, 128, 16), AF.Copy)
-    for nm, src, c in (("I4096", "ID", 4096.0), ("NI", "ID", -1.0), ("HI", "ID", 0.5), ("N512", "ID", -512.0), ("N8192", "ID", -8192.0),
-                       ("N25", "ID", -33554432.0), ("BDa", "BD", -128.0), ("BDr", "BD", -2.125), ("BDf", "BD", 1.0)):
-        ACT(F(nm), F(src), AF.Copy, 0.0, c)
-    ACT(F("R15f"), F("BD"), AF.Copy, 0.0, F("K16", 15, 16))
-    MS(F("segV"), 1000000.0)
-    MS(F("segV", 0, 96, 16), -1000000.0)
-    MS(F("bia"), 0.0)
-    MS(F("bia", 5, 10), -1.0 / 16)
+        TS(blk("SS", q), F("J2"), float(q), OP.is_equal)
+    for q in range(15):
+        TS(blk("TRI", q), F("J3"), float(q), OP.is_gt, 8192.0, OP.mult)
+    for nm, src, c in (("Ic", ID, 1.0 / 64), ("N8", ID, -8192.0), ("Ik", ID, 1.0 / 4096), ("Nh", ID, -1.0 / 16), ("P8", ID, 8192.0),
+                       ("PBD8", BD, 8192.0), ("NBD8", BD, -8192.0), ("N256", ID, -256.0), ("NU", ID, -16640.0), ("P512", ID, 512.0),
+                       ("N1024", ID, -1024.0), ("NI", ID, -1.0), ("BDf", BD, 0.5)):
+        ACT(F(nm), src, AF.Copy, 0.0, c)
+    for j in range(4):
+        for i in range(4):
+            o = F("p%d" % (4 + j), 128 * i, 128 * i + 128)
+            MM([(o, F("Ic"), blk("ROT", (16 - 4 * j - i) % 16)), (o, N8, ID)])
+        ACT(F("AS", 512 * j, 512 * j + 512), F("p%d" % (4 + j)), AF.Copy)
+    TS(F("EQ", 0, 128), F("i3"), kp, OP.is_equal)
+    for a, b in ((128, 256), (256, 512), (512, 1024), (1024, 1280)):
+        ACT(F("EQ", a, b), F("EQ", 0, b - a), AF.Copy)
+    TS(F("pen", 0, n), F("EQ", 0, n), 60000.0, OP.mult, 1.0 - 60000.0, OP.add)
+    TS(F("pen", n, NM), F("EQ", 0, n), 60000.0, OP.mult, -1535.0 - 60000.0, OP.add)
+    TS(F("NE"), F("EQ", 0, NM), -256.0, OP.mult, 256.0, OP.add)
+    MS(F("seg0"), 1.0)
+    MS(F("seg0", 0, G16, 16), 0.0)
+    for nm, k in (("seg32", 32), ("seg16", 16)):
+        MS(F(nm), 1e9)
+        MS(F(nm, 0, NM, k), -1e9)
+    MS(F("CN", 0, NM), -2.0)
+    MS(F("CN", NM, 240), -1.0)
+    TS(F("DUM"), F("dmi"), kp, OP.add)
+    TS(F("kf", 3, 4), kp, 16.0, OP.mult)
+    TS(F("CK"), F("cki"), F("kf", 3, 4), OP.add)
+    TS(F("kf", 4, 5), kp, -256.0, OP.mult, 35071.0 + 3840.0, OP.add)
+    TS(F("kf", 5, 6), ko, -33554432.0, OP.mult, F("kf", 4, 5), OP.add)
+    TS(F("kf", 7, 8), ko, 33554432.0, OP.mult, -33554432.0, OP.add)
+    TS(F("kf", 6, 7), F("kf", 7, 8), F("kf", 4, 5), OP.add)
+    ACT(F("t1s"), F("tli"), AF.Copy, 0.0, 3.0)
+    TT(F("t1s"), F("t1s"), F("tli"), OP.min)
     for h in range(NH):
-        MS(F("f3%d" % h, 0, 96), 0.0)
-    CP(F("tf", 0, NM), F("tli"))
-    ACT(F("t1s"), F("tf", 0, NM), AF.Copy, 0.0, 3.0)
-    TT(F("t1s"), F("t1s"), F("tf", 0, NM), OP.min)
-    for h in range(NH):
-        m = "msg0%d" % h
-        TS(F(m, n, 2 * n), F("t1s", h * n, h * n + n), -2047.0, OP.add)
-        TS(F(m, 0, n), F("dli", h * n, h * n + n), -2047.0, OP.add)
-        CP(F(m, 2 * n, 3 * n), F("zin", h * n, h * n + n))
-    CP(F("thc"), F("thi"))
-    TS(F("kf", 3, 4), F("kf", 2, 3), -1.0 / 16, OP.mult, 31.0 / 32, OP.add)
-    TT(F("thc"), F("thc"), F("kf", 3, 4), OP.add)
+        m = 240 * h
+        TS(F("msg", m, m + n), F("t1s", h * n, h * n + n), -2047.0, OP.add)
+        ACT(F("msg", m + n, m + 2 * n), F("dli", h * n, h * n + n), AF.Copy, -2047.0)
+        ACT(F("msg", m + 2 * n, m + 3 * n), F("zin", h * n, h * n + n), AF.Copy, 1024.0)
+    TS(F("thc"), F("thi"), -0.5, OP.mult, -8200.8125, OP.add)
     CP(F("lim"), F("thc"))
     MS(F("As"), 0)
-    TS(F("sct", 0, 256), F("sci"), 1.0, OP.add)
-    MS(F("sct", 256, 256 + NM), 0.0)
-    CP(F("tf2"), F("sti"))
-    ACT(F("stt"), F("tf2"), AF.Copy, 0.0, 3.0)
-    TT(F("stt"), F("stt"), F("tf2"), OP.min)
-    ACT(F("stt"), F("stt"), AF.Copy, -2047.0)
-    TS(F("im"), F("ic"), 15, OP.bitwise_and)
-    TS(F("LOW"), F("im"), F("kf", 2, 3), OP.is_ge, 1024.0, OP.mult)
-    CP(F("co"), F("ic", 0, 10))
-    TS(F("DUM"), F("dmi"), F("kf", 2, 3), OP.add)
-
-    def Rq(q):
-        return F("RR", 128 * q, 128 * q + 128)
-
-    def Sq(q):
-        return F("SS", 128 * q, 128 * q + 128)
+    MS(F("sct"), -2048.0)
+    ACT(F("sct", 1, 257), F("sci"), AF.Copy, -2047.0)
+    MS(F("stt", 0, 1), -2050.0)
+    ACT(F("tf"), F("sti"), AF.Copy, 0.0, 3.0)
+    TT(F("tf2"), F("tf"), F("sti"), OP.min)
+    ACT(F("stt", 1, 257), F("tf2"), AF.Copy, -2047.0)
 
     CH = [list(range(0, 6)), list(range(6, 12)), list(range(12, 16))]
 
     def visit(t, h):
         last = t == VIS - 1
         H = str(h)
-        m = "msg%d%d" % (t, h)
-        D, TL, Z, ts = F(m, 0, n), F(m, n, 2 * n), F(m, 2 * n, 3 * n), F(m, 3 * n, 4 * n)
+        m = 240 * (NH * t + h)
+        TL, D, Z = F("msg", m, m + n), F("msg", m + n, m + 2 * n), F("msg", m + 2 * n, m + 3 * n)
         B = ["p%d" % (4 * h + i) for i in range(4)]
-        ID, N8, BD = F("ID"), F("N8192"), F("BD")
+
+        def P(b, i, k=1):
+            return F(B[b], i * n, (i + k) * n)
 
         def bf(i, k=1):
             return F("bf" + H, i * n, (i + k) * n)
 
-        def f3(a, b):
-            return F("f3" + H, a, b)
+        def hf(i, k=1):
+            return F("hf" + H, i * n, (i + k) * n)
 
-        def lf(i):
-            return F("lf" + H, 8 * i, 8 * i + 5)
+        def f3(i, k=1):
+            return F("f3" + H, i * n, (i + k) * n)
 
-        def lu(i):
-            return F("lu" + H, 8 * i, 8 * i + 5)
-
-        def eqs(q, k=1):
-            return F("eq" + H, q * n, (q + k) * n)
-        offT, off1, clk = F("offT" + H), F("off1" + H), F("clkw")
-        PH[0] = "y"
-        TS(offT, TL, 2063.0, OP.add)
-        ACT(F("Y" + H), IND(clk, offT), AF.Copy)
-        PH[0] = "q"
-        for j, qs in enumerate(CH):
-            bk = B[j % 2]
-            for i, q in enumerate(qs):
-                o = F(bk, i * n, i * n + n)
-                MM([(o, Rq(q), TL)] + ([(o, F("NI"), D)] if EQ[j] == "s" else []))
-            if EQ[j] == "s":
-                k = len(qs)
-                ACT(F("ea" + H, 0, k * n), F(bk, 0, k * n), AF.Abs)
-                ACT(eqs(qs[0], k), F("ea" + H, 0, k * n), AF.Relu, 1.0, -1.0)
-            else:
+        def compare(src, own, e, acc, w, first, rest):
+            for j, qs in enumerate(CH):
+                MM([(P(j % 2, i), blk("ROT", q), src) for i, q in enumerate(qs)])
                 for i, q in enumerate(qs):
-                    TT(eqs(q), D, F(bk, i * n, i * n + n), OP.is_equal)
-        cdp, ctp = F(B[2], 0, n), F(B[2], n, 2 * n)
-        ACT(bf(21), TL, AF.Sign, 2048.5)
-        MM([(F(B[3], 240, 320), BD, bf(21))])
-        rs = bf(6)
-        ACT(rs, F(B[3], 240, 320), AF.Relu, -15.0, -1.0)
-        for j, qs in enumerate(CH):
-            MM([(cdp, F("I4096"), eqs(q)) for q in qs], j < 2, j > 0)
-        for j, qs in enumerate(CH):
-            MM([(ctp, Sq(q), eqs(q)) for q in qs], j < 2, j > 0)
+                    TT(F(e, q * n, q * n + n), own, P(j % 2, i), OP.is_equal)
+                MM((first if j == 0 else []) + [(acc, w(q), F(e, q * n, q * n + n)) for q in qs], True, j > 0)
+            MM(rest, False, True)
+
+        offT, off1, clk, Y = F("offT" + H), F("off1" + H), F("clkw"), F("Y" + H)
+        hi, E, hiU, fl, nct, fc, NG, oh, kmT, ykm, A2 = bf(0), bf(1), bf(2), bf(3), bf(4), bf(5), bf(6, 2), bf(8), bf(9), bf(10), bf(11)
+        N, G = bf(6), bf(7)
+        cv, sv, wD, wT, yk, r1, tD, tT = [hf(i) for i in range(8)]
+        luv, luk, luw = [F("lu" + H, 8 * i, 8 * i + 5) for i in range(3)]
+        PH[0] = "y"
+        ACT(offT, TL, AF.Identity, 2063.0)
+        ACT(Y, IND(clk, offT), AF.Copy)
+        PH[0] = "e"
+        ACT(hi, TL, AF.Identity, 136.498046875, 1.0 / 256)
+        MM([(P(2, 1), BD, hi)])
+        ACT(E, P(2, 1), AF.Relu, 2049.0, -1.0)
+        MM([(P(2, 2), BD, Z)])
+        ACT(hiU, P(2, 2), AF.Identity, 64.501953125, 1.0 / 256)
+        PH[0] = "q"
+        acc = P(2, 0)
+        compare(TL, D, "eq" + H, acc, lambda q: blk("AS", q), [(acc, ID, D)], [(acc, F("Ic"), F("eq" + H, 0, n)), (acc, N8, E)])
         PH[0] = "x"
-        d1 = f3(96, 176)
-        TT(d1, D, cdp, OP.subtract)
-        TS(off1, d1, -2048.0, OP.max, 2063.0, OP.add)
+        ACT(off1, acc, AF.Relu, 2063.0)
+        ACT(F("ri" + H), acc, AF.Identity)
+        ACT(fl, acc, AF.Sign, 2047.5)
+        TT(nct, F("ri" + H), acc, OP.is_equal)
         ACT(F("X" + H), IND(clk, off1), AF.Copy)
-        fl = bf(0)
-        ACT(fl, d1, AF.Sign, 2047.5)
-        cdb, ctb = bf(1), bf(2)
-        ACT(bf(1, 2), F(B[2], 0, 2 * n), AF.Copy, 0.0, 1.0 / 4096)
+        SC(F("tp" + H), F("seg0"), F("X" + H), 0.0, OP.mult, OP.max)
         PH[0] = "m"
-        zps, tlp = F(B[3], 400, 480), F(B[3], 320, 400)
-        MM([(zps, ID, Z)])
-        MM([(tlp, ID, TL)])
+        zps, Gp, key = P(3, 0), P(0, 0), P(1, 0)
+        MM([(zps, F("P512"), F("CN", 0, n)), (zps, ID, Z)])
         for q in range(16):
             TT(F("mn" + H, q * n, q * n + n), F("Y" + H, q, G16, 16), zps, OP.min)
-        Gp, scp, kbp = F(B[1], 0, n), F(B[0], 0, n), F(B[0], n, 2 * n)
-        MM([(Gp, BD, Z)] + [(Gp, Sq(q), F("Y" + H, q, G16, 16)) for q in range(16)])
+        MM([(Gp, blk("SS", q), F("Y" + H, q, G16, 16)) for q in range(16)], True)
+        MM([(Gp, BD, Z), (Gp, N8, nct)], False, True)
+        MM([(key, F("Ik"), TL), (key, F("Nh"), hi)], True)
         for j, qs in enumerate(CH):
-            MM([(scp, Sq(q), F("mn" + H, q * n, q * n + n)) for q in qs], j < 2, j > 0)
+            MM([(key, blk("SS", q), F("mn" + H, q * n, q * n + n)) for q in qs], j < 2, True)
         PH[0] = "k"
-        nk = f3(0, n)
-        ACT(nk, scp, AF.Identity, F("lim"), 2.0)
-        vt, vs, vb = f3(176, 272), f3(272, 368), f3(368, 464)
-        VT(vt, f3(0, 96))
-        SC(vs, F("segV"), vt, -1000000.0, OP.min, OP.max)
-        VT(vb, vs)
-        MM([(kbp, F("R15f"), f3(368, 448))])
-        oh, far, fc = bf(3), bf(4), bf(5)
-        TT(far, nk, Gp, OP.is_lt)
-        TT(fc, far, ctp, OP.mult)
-        TT(oh, nk, kbp, OP.is_equal)
-        TT(ts, oh, tlp, OP.mult)
-        lst = F(B[0], 160, 170)
-        MM([(lst, Sq(r), F(m, 2 * n + r, 4 * n, 16)) for r in range(16)] + [(lst, BD, F("bia"))])
+        ACT(BLK("nk" + H, 0), key, AF.Identity, F("kf", 5, 6), 4096.0)
+        ACT(BLK("nk" + H, 1), key, AF.Identity, F("kf", 6, 7), 4096.0)
+        vt, vs = f3(0, 2), F("vs" + H)
+        VT(vt, F("nk" + H))
+        SC(vs, F("seg32"), vt, -1e9, OP.min, OP.max)
+        kb, va, kk = F("vs" + H, 31, NM, 32), F("li" + H, 0, 5), F("li" + H, 8, 13)
+        TS(va, kb, 255, OP.bitwise_and)
+        TS(luv, va, 1.0, OP.add)
+        ACT(sv, IND(F("stt"), luv), AF.Copy)
+        TS(kk, kb, 8, OP.arith_shift_right, 15, OP.bitwise_and)
+        TT(luk, F("CK"), kk, OP.subtract)
+        ACT(oh, IND(F("EQ"), luk), AF.Copy)
+        ACT(yk, IND(Y, luk), AF.Copy)
         PH[0] = "c"
-        cp = F(B[1], n, 2 * n)
-        MM([(cp, BD, fl), (cp, F("BDa"), fc), (cp, F("BDr"), rs)])
-        nm1, sq, q0, nm2, nm3, abm = bf(7), bf(9), bf(10), bf(11), bf(12), bf(18)
-        ACT(sq, cp, AF.Square, 32.5)
-        ACT(q0, cp, AF.Abs, 2048.0, 128.0)
-        ACT(nm1, cp, AF.Relu, -15.0, -1.0)
-        ACT(nm2, cp, AF.Relu, 80.0)
+        G2 = f3(2)
+        ACT(G2, Gp, AF.Identity, F("lim"), 0.5)
+        TT(fc, G2, key, OP.is_gt)
+        MM([(P(2, 3), BD, fl), (P(2, 3), F("PBD8"), fc)])
+        MM([(P(2, 4), BD, fl), (P(2, 4), F("NBD8"), fc)])
+        ACT(NG, P(2, 3, 2), AF.Sign, 15.0)
         if not last:
-            ACT(abm, cp, AF.Relu, -65536.0 * 80, -65536.0)
-            TT(bf(8), cdp, abm, OP.is_gt)
-            ACT(bf(22), bf(8), AF.Copy, 0.0, 1.0, F("ac", h, h + 1))
-        ACT(nm3, sq, AF.Relu, -324.0)
+            cx = P(3, 5)
+            MM([(cx, ID, D), (cx, N8, fl), (cx, N8, E), (cx, F("NBD8"), fc)])
+            ACT(bf(12), cx, AF.Sign, -6144.5, 1.0, F("ac", h, h + 1))
         PH[0] = "l"
-        sql = F(B[0], 170, 180)
-        MM([(sql, Sq(r), F("bf" + H, 9 * n + r, 11 * n, 16)) for r in range(16)])
-        TS(lu(0), F(B[0], 165, 170), 2064.0, OP.add)
-        yk = bf(13)
-        ACT(yk, IND(clk, lu(0)), AF.Copy)
-        CP(F("li" + H, 0, 10), lst)
-        TS(F("uv" + H), F("li" + H, 0, 10), 255, OP.bitwise_and)
-        uu, v32 = F("uv" + H, 0, 5), F("uv" + H, 5, 10)
-        TT(lf(0), v32, uu, OP.subtract)
-        nu = lf(1)
-        TS(nu, F(B[0], 170, 175), 5184.0, OP.is_gt)
-        TT(F("pv", 5 * h, 5 * h + 5), v32, F(B[0], 175, 180), OP.max)
-        TT(lf(2), lf(0), nu, OP.mult)
-        TT(lf(3), lf(2), uu, OP.add)
-        CP(lu(1), lf(3))
-        cs, csD, csT = F("hf" + H), F("hf" + H, 0, n), F("hf" + H, n, 2 * n)
-        TS(csD, IND(F("sct", 0, 256), lu(1)), -2048.0, OP.add)
-        CP(csT, IND(F("stt"), lu(1)))
-        PH[0] = "h"
-        for e in range(2):
-            for j, qs in enumerate(CH):
-                bk = B[(j + e) % 2]
-                for i, q in enumerate(qs):
-                    o = F(bk, i * n, i * n + n)
-                    MM([(o, Rq(q), F(m, e * n, e * n + n)), (o, F("NI"), F("hf" + H, e * n, e * n + n))])
-                for i, q in enumerate(qs):
-                    ACT(F("ab" + H, e * G16 + q, (e + 1) * G16, 16), F(bk, i * n, i * n + n), AF.Abs)
-            SC(F("sm" + H, e * G16, (e + 1) * G16), F("segM", 0, G16), F("ab" + H, e * G16, (e + 1) * G16), 0.0, OP.max, OP.min)
+        X1, X2 = P(3, 1), P(3, 2)
+        MM([(P(3, 1, 2), ID, F("pen")), (X1, BD, Z), (X1, F("N256"), hiU), (X2, F("N1024"), E), (X1, F("NU"), N), (X2, F("P512"), N), (X2, F("N1024"), G)])
+        SC(f3(3, 2), F("seg16"), P(3, 1, 2), -1e9, OP.min, OP.max)
+        a1 = F("lf" + H, 0, 5)
+        TT(a1, va, F("f3" + H, 4 * n + 15, 5 * n, 16), OP.add)
+        TT(luw, a1, F("f3" + H, 3 * n + 15, 4 * n, 16), OP.max)
+        ACT(wT, IND(F("stt"), luw), AF.Copy)
+        ACT(F("pv", 5 * h, 5 * h + 5), a1, AF.Abs, 1024.0)
         PH[0] = "d"
-        dg, tg, t1p = F(B[2], 160, 240), F(B[2], 240, 320), F(B[3], 320, 400)
-        MM([(dg, ID, D), (dg, N8, cdb), (dg, N8, nm1)])
-        MM([(tg, ID, TL), (tg, F("N25"), ctb), (tg, N8, oh), (tg, N8, nm1)])
-        MM([(t1p, ID, TL), (t1p, F("N25"), ctb), (t1p, N8, oh)])
-        ACT(F("t1s", h * n, h * n + n), t1p, AF.Relu, 2048.0)
-        km, kx = bf(14, 2), f3(464, 624)
-        ACT(km, F(B[2], 160, 320), AF.Relu, 2048.0)
-        TS(f3(464, 544), dg, -2048.0, OP.max)
-        TS(f3(544, 624), tg, -2050.0, OP.max)
+        t1p, dg, tg = P(3, 0), P(3, 3), P(3, 4)
+        MM([(t1p, ID, TL), (t1p, P8, nct), (t1p, N8, oh)])
+        ACT(kmT, t1p, AF.Relu, -6144.0)
+        MM([(P(3, 3, 2), P8, F("CN", 0, NM)), (dg, ID, D), (dg, P8, fl), (tg, ID, TL), (tg, P8, nct), (tg, N8, oh), (dg, P8, G), (tg, P8, G)])
+        TT(tT, wT, tg, OP.max)
+        o = 240 * (NH * t + h)
+        oT, oD, oZ = (f3(5), f3(6), f3(7)) if last else [F("out", o + i * n, o + i * n + n) for i in range(3)]
+        PH[0] = "g"
+        rT = P(2, 5)
+        compare(TL, sv, "eg" + H, rT, lambda q: N8, [(rT, ID, sv), (rT, P8, F("CN", NM, 240))], [(rT, N8, kmT), (rT, P8, G)])
+        TT(oT, tT, rT, OP.max)
+        PH[0] = "f"
+        ACT(F("t1s", h * n, h * n + n), t1p, AF.Relu, -6144.0)
+        ACT(F("VB", h * n, h * n + n), IND(F("IT"), luv), AF.Copy)
+        ACT(cv, IND(F("sct", 0, 257), luv), AF.Copy)
+        ACT(wD, IND(F("sct", 0, 257), luw), AF.Copy)
+        TT(tD, wD, dg, OP.max)
+        rD = P(3, 1)
+        compare(D, cv, "eq" + H, rD, lambda q: N8, [(rD, ID, cv), (rD, P8, F("CN", 0, n))], [(rD, N8, fl), (rD, P8, G)])
+        TT(oD, tD, rD, OP.max)
         PH[0] = "z"
-        SC(F("tp" + H), F("seg0"), F("X" + H), 0.0, OP.mult, OP.max)
-        zd, z1, z2, z4 = [F(B[3], i * n, i * n + n) for i in range(4)]
-        MM([(zd, ID, Z), (zd, F("NI"), yk)])
-        A2 = bf(19)
-        ACT(A2, zd, AF.Abs)
-        MM([(z1, F("HI"), yk), (z1, F("HI"), F("tp" + H, 15, G16, 16)), (z1, F("N512"), nm1)])
-        MM([(z2, ID, A2), (z2, F("N512"), nm2)])
-        MM([(z4, ID, Z), (z4, F("N512"), nm3)])
-        ACT(f3(624, 704), z1, AF.Identity, -0.25)
-        TT(f3(704, 784), f3(624, 704), z2, OP.max)
-        TT(f3(784, 864), f3(704, 784), z4, OP.max)
-        o = "out%d%d" % (t, h)
-        zo = F("fin", 320 + h * n, 320 + h * n + n) if last else F(o, 160, 240)
-        TS(zo, f3(784, 864), 8388608.0, OP.add, 8388608.0, OP.subtract)
+        yp, zd, z1, zp = P(2, 1), P(2, 2), P(2, 3), P(2, 4)
+        MM([(yp, ID, yk), (yp, F("P512"), N)])
+        ACT(ykm, yp, AF.Relu, -512.0)
+        MM([(zd, ID, Z), (zd, F("P512"), G), (zd, F("NI"), ykm)])
+        ACT(A2, zd, AF.Abs, -512.0)
+        MM([(z1, F("N1024"), G), (z1, ID, ykm), (z1, ID, F("tp" + H, 15, G16, 16))])
+        ACT(r1, z1, AF.Identity, 1535.8, 0.5)
+        MM([(zp, F("N1024"), F("CN", NM, 240)), (zp, ID, A2)])
+        TT(oZ, r1, zp, OP.min)
         PH[0] = "r"
-        hp, hd = F(B[0], 0, 2 * n), bf(16, 2)
-        for e in range(2):
-            x = F(B[0], e * n, e * n + n)
-            MM([(x, ID, F("sm" + H, e * G16 + 15, (e + 1) * G16, 16)), (x, ID, nm1)])
-        ACT(hd, hp, AF.Relu, 1.0, -1.0)
-        rp = F(B[2], 320, 480)
-        MM([(rp, ID, cs), (rp, N8, km), (rp, N8, hd)])
         if last:
-            TT(f3(944, 1104), kx, rp, OP.max)
-            TS(F("fin", h * n, h * n + n), f3(944, 1024), 2047.0, OP.add, -1.0, OP.max)
-            TS(F("fin", 160 + h * n, 160 + h * n + n), f3(1024, 1104), 2047.0, OP.add, -1.0, OP.max)
+            TS(F("fin", h * n, h * n + n), oD, 2047.0, OP.add, -1.0, OP.max)
+            TS(F("fin", 160 + h * n, 160 + h * n + n), oT, 2047.0, OP.add, -1.0, OP.max)
+            ACT(F("fin", 320 + h * n, 320 + h * n + n), oZ, AF.Copy, -1024.0)
         else:
-            TT(F(o, 0, 160), kx, rp, OP.max)
-            add("g", "send", (t, h), [F(o)], [], 200)
-            add("n", "arrive", (t, h), [], [F("msg%d%d" % (t + 1, h), 0, 240)], 0, arr=(t + 1, h))
+            for k, (a, b) in enumerate(SENDS):
+                add("g", "send", (t, h, k), [F("out", o + a, o + b)], [], 200)
+                add("n", "arrive", (t, h, k), [], [F("msg", o + 240 * NH + a, o + 240 * NH + b)], 0)
 
     def proofs(t):
-        pb = "p7"
-        TS(F("pvb"), F("pv"), 4096.0, OP.min)
-        VB, lp, ll = F(pb, 0, NM), F(pb, NM, 2 * NM), F(pb, 488, 498)
-        for r in range(16):
-            MM([(F(pb, r, NM, 16), Rq(r), F("pvb"))])
-        ACT(F("VBs"), VB, AF.Copy)
-        TT(F("VL"), F("VBs"), F("LOW"), OP.max)
-        TT(F("eb"), IND(F("pv"), F("co")), F("VL"), OP.is_equal)
-        lst = [(lp, F("BD"), F("eb"))]
-        a = 0
-        for c in range(1, 10):
-            TS(F("el", a, a + 16 * c), F("VBs", 0, 16 * c), F("pv", c, c + 1), OP.is_equal)
-            lst.append((F(pb, NM, NM + 16 * c), F("BD"), F("el", a, a + 16 * c)))
-            a += 16 * c
+        lp = F("p7", 320, 480) if t == VIS - 1 else F("p3", 320, 480)
+        lst = [(lp, N8, F("NE"))]
+        for c in range(10):
+            TS(F("el", 160 * c, 176 * c + 16), F("VB", 0, 16 * c + 16), F("pv", c, c + 1), OP.is_equal)
+            if c:
+                lst.append((F(lp[0], 320, 320 + 16 * c), F("PBD8"), F("el", 160 * c, 176 * c)))
+        lst += [(F(lp[0], 320 + r, 480, 16), blk("TRI", r), F("el", r, 1600, 176)) for r in range(15)]
         MM(lst)
-        ACT(F("lo"), lp, AF.Copy)
-        MM([(ll, Sq(r), F("lo", r, NM, 16)) for r in range(16)])
-        TS(F("l0"), ll, 0.5, OP.is_gt, 4096.0, OP.mult)
-        TT(F("xa"), F("l0"), F("pv"), OP.add)
-        TT(F("xa"), F("xa"), F("DUM"), OP.min)
-        CP(F("sou"), F("xa"))
-        CP(IND(F("sct"), F("sou")), F("t1s"))
+        SC(F("ls"), F("seg16"), lp, -1e9, OP.min, OP.max)
+        TT(F("xa"), F("ls", 15, NM, 16), F("pv"), OP.max)
+        TT(F("sou"), F("xa"), F("DUM"), OP.min)
+        TS(IND(F("sct"), F("sou")), F("t1s"), 1.0, OP.mult, -2048.0, OP.add)
 
     def count():
         pa = F("p7", 504, 505)
         MM([(pa, F("BDf"), F("ac", 0, 1)), (pa, F("BDf"), F("ac", 1, 2))])
         TT(F("As"), F("As"), pa, OP.add)
         TS(F("Am"), F("As"), 31, OP.bitwise_and)
-        TS(F("lim"), F("Am"), 8.0, OP.mult, F("thc"), OP.add)
+        TS(F("lim"), F("Am"), -4.0, OP.mult, F("thc"), OP.add)
 
     for t in range(VIS):
         for h in range(NH):
@@ -426,7 +406,7 @@ def _build():
         PH[:] = ["P", t, 0]
         proofs(t)
     PH[:] = ["E", 0, 0]
-    TS(F("yso"), F("sct", 0, 256), -1.0, OP.add)
+    ACT(F("yso"), F("sct", 1, 257), AF.Copy, 2047.0)
     add("y", "sto", [("yd", 0), ("yt", 160), ("yz", 320)], [F("fin")], [], 100, dma="wr0", lat=2500)
     add("y", "stys", None, [F("yso")], [], 50, dma="wr1", lat=2500)
     return ops
@@ -435,11 +415,13 @@ def _build():
 def _overlap(a, b):
     if a[0] != b[0] or a[1] >= b[2] or b[1] >= a[2]:
         return False
+    if len(a) == 5 and len(b) == 5:
+        return a[4] == b[4]
     return not (a[3] == b[3] and a[3] > 1 and (a[1] - b[1]) % a[3])
 
 
 def _covers(a, b):
-    return a[3] == 1 and a[1] <= b[1] and a[2] >= b[2] or a == b
+    return len(a) == 4 and a[3] == 1 and a[1] <= b[1] and a[2] >= b[2] or a == b
 
 
 def _deps(ops):
@@ -449,36 +431,44 @@ def _deps(ops):
         dep = {}
         acc = [(x, False) for x in o["r"]] + [(x, True) for x in o["w"]]
         for (x, wr) in acc:
-            psum = _W[x[0]] == "psum"
             for (y, ywr, yo) in hist.get(x[0], []):
-                if yo is o:
-                    continue
-                same = yo["q"] == o["q"]
-                if psum and not same:
-                    dep[yo["id"]] = True
-                elif psum and o["q"] == "t":
-                    dep.setdefault(yo["id"], False)
-                elif (wr or ywr) and _overlap(x, y):
-                    need = (not same) or (ywr and o["q"] != "t")
+                if yo is not o and (wr or ywr) and _overlap(x, y):
+                    need = yo["q"] != o["q"] or (ywr and o["q"] != "t")
                     dep[yo["id"]] = dep.get(yo["id"], False) or need
         for (x, wr) in acc:
             L = hist.setdefault(x[0], [])
             if wr:
-                ps = _W[x[0]] == "psum"
-                L[:] = [e for e in L if e[2] is o or not (_covers(x, e[0]) and (not ps or e[2]["q"] == o["q"]))]
+                L[:] = [e for e in L if e[2] is o or not _covers(x, e[0])]
             L.append((x, wr, o))
         if o["call"] == "send":
             sends[o["args"]] = o["id"]
         if o["call"] == "arrive":
             dep[sends[o["args"]]] = False
         o["dep"] = dep
+        o["banks"] = sorted(set(x[0] for (x, wr) in acc if _W[x[0]] == "psum"))
+    anc, starts, opener = [], {}, {}
+    for o in ops:
+        a = 0
+        for d in o["dep"]:
+            a |= anc[d] | (1 << d)
+        anc.append(a)
+        if o["call"] == "mm":
+            key = (o["banks"][0], o["w"][-1][1])
+            if o["args"][1]:
+                starts.setdefault(key[0], []).append(o["id"])
+                opener[key] = o
+            elif o["args"][2]:
+                f = opener[key]
+                for s in starts[key[0]]:
+                    if s != f["id"] and a >> s & 1 and not anc[s] >> f["id"] & 1:
+                        f["dep"].setdefault(s, False)
 
 
 LAT = {"x": 130.0, "own": 80.0, "arr": 3800.0, "fix": 20.0}
 SCALE = 1.1
 
 
-def _schedule(ops, seed=0):
+def _schedule(ops, bias):
     succ = [[] for _ in ops]
     for o in ops:
         for d in o["dep"]:
@@ -493,12 +483,13 @@ def _schedule(ops, seed=0):
             return 0.0
         return LAT["own"] if a["q"] == b["q"] else LAT["x"]
     pri = [0.0] * len(ops)
-    for o in reversed(ops):
+    for o in list(reversed(ops)) * 2:
         pri[o["id"]] = o["cost"] + max([pri[s] + dly(o, ops[s]) for s in succ[o["id"]]] + [0.0])
-    pri = [p + BIAS.get((o["ph"][0], o["ph"][2]), 0.0) + BIAS.get(o["ph"][1:], 0.0) for p, o in zip(pri, ops)]
+    pri = [p + bias.get((o["ph"][0], o["ph"][2]), 0.0) + bias.get(o["ph"][1:], 0.0) for p, o in zip(pri, ops)]
     left = [len(o["dep"]) for o in ops]
     rt = [0.0] * len(ops)
     ready, free, order, start, end = {}, {}, {}, [0.0] * len(ops), 0.0
+    users, opened, extra = {}, set(), {}
     for o in ops:
         if not left[o["id"]]:
             ready.setdefault(o["q"], []).append(o["id"])
@@ -507,13 +498,32 @@ def _schedule(ops, seed=0):
         for q, L in ready.items():
             f = free.get(q, 0.0)
             for i in L:
-                k = (rt[i] if q == "n" else max(f, rt[i]), -pri[i])
+                s = rt[i] if q == "n" else max(f, rt[i])
+                if best is not None and s > best[0][0]:
+                    continue
+                o = ops[i]
+                if o["banks"]:
+                    if q == "t" and o["args"][1] and o["banks"][0] in opened:
+                        continue
+                    for b in o["banks"]:
+                        for q2, (e2, _j) in users.get(b, {}).items():
+                            if q2 != q:
+                                s = max(s, e2 + LAT["x"])
+                k = (s, -pri[i])
                 if best is None or k < best[0]:
                     best = (k, q, i)
         (s, _p), q, i = best
         ready[q].remove(i)
         o = ops[i]
         e = s + o["cost"] + (0.0 if q == "n" else LAT["fix"])
+        extra[i] = [j for b in o["banks"] for q2, (e2, j) in users.get(b, {}).items() if q2 != q]
+        for b in o["banks"]:
+            users.setdefault(b, {})[q] = (e, i)
+        if q == "t":
+            if o["args"][2]:
+                opened.discard(o["banks"][0])
+            else:
+                opened.add(o["banks"][0])
         start[i] = s
         free[q] = e
         end = max(end, e)
@@ -523,7 +533,7 @@ def _schedule(ops, seed=0):
             left[x] -= 1
             if not left[x]:
                 ready.setdefault(ops[x]["q"], []).append(x)
-    return end, seed, order, start
+    return end, order, start, extra
 
 
 _CACHE = {}
@@ -537,16 +547,18 @@ def _plan():
     _deps(ops)
     for o in ops:
         o["cost"] *= SCALE
-    end, _s, order, start = _schedule(ops)
+    end, order, start, extra = _schedule(ops, BIAS)
     cnt = {}
     for q, L in order.items():
         for i in L:
             o = ops[i]
             o["start"] = start[i]
+            for j in extra[i]:
+                o["dep"][j] = True
             if "dma" in o:
                 o["tok"] = (o["dma"], 48 if o["call"] == "sto" else 16)
             elif o["call"] == "arrive":
-                o["tok"] = ("arr%d%d" % o["arr"], None)
+                o["tok"] = ("arr%d%d%d" % (o["args"][0] + 1, o["args"][1], o["args"][2]), None)
             elif o["call"] != "send":
                 cnt[SEMQ[q]] = cnt.get(SEMQ[q], 0) + 1
                 o["tok"] = (SEMQ[q], cnt[SEMQ[q]])
@@ -565,7 +577,7 @@ def _plan():
             for s2, v2 in list(ops[d]["kn"].items()) + [(s, v)]:
                 kn[s2] = max(kn.get(s2, 0), v2)
         o["wait"] = sorted(w.items())
-        o["kn"] = dict(kn)
+        o["kn"] = {} if o["call"] == "arrive" else dict(kn)
     _CACHE["p"] = (ops, order, cnt, end)
     return _CACHE["p"]
 
@@ -585,6 +597,10 @@ def rank_program(g, core, T, topo):
             return x
         if x[0] == "IND":
             return ap(x[1]).indirect(ap(x[2]))
+        if len(x) == 5:
+            return T[x[0]][:, :, 16 * x[4]:16 * x[4] + 16]
+        if len(SCRATCH[x[0]][1]) == 3:
+            return T[x[0]][:]
         if x[3] == 1:
             return T[x[0]][:, x[1]:x[2]]
         return T[x[0]][:, x[1]:x[2]:x[3]]
@@ -598,10 +614,12 @@ def rank_program(g, core, T, topo):
                 e.wait_ge(T.sem[s], arrn[int(s[3])] if s[:3] == "arr" else v)
             a, call = o["args"], o["call"]
             if call == "send":
-                t, h = a
+                t, h, k = a
                 dst = T.cores[(rank + hops[t]) % N]
                 rid, pid = topo.addr(dst, core)
-                g.remote_dma(T["msg%d%d" % (t + 1, h)][:, 0:240], T["out%d%d" % (t, h)][:], T.sem["arr%d%d" % (t + 1, h)], T.sem.snd, pid, rid, topo.mask(core, dst))
+                c0, c1 = o["r"][0][1:3]
+                g.remote_dma(T.msg[:, c0 + 240 * NH:c1 + 240 * NH], T.out[:, c0:c1], T.sem["arr%d%d%d" % (t + 1, h, k)], T.sem.snd, pid, rid,
+                             topo.mask(core, dst))
                 nsend += len(topo.engines(core, dst))
                 continue
             if call == "ld":
@@ -638,8 +656,6 @@ def rank_program(g, core, T, topo):
                 ins = e.activation(ap(a[0]), ap(a[1]), a[2], ap(a[3]), ap(a[4]), **kw)
             elif call == "iota":
                 ins = e.iota(ap(a[0]), a[1], a[2], a[3], allow_small_or_imprecise_dtypes=True)
-            elif call == "asel":
-                ins = e.affine_select(ap(a[0]), ap(a[0]), a[1], OP.not_equal, a[2], 0, 0)
             ins.then_inc(T.sem[o["tok"][0]], 1)
     g.wait_ge(T.sem.snd, nsend)
     for s, v in sorted(cnt.items()):

@@ -8,9 +8,10 @@ NM = 160
 G16 = 16 * n
 VIS = 4
 CW = 4112
-SENDS = [(0, 80), (80, 240)]
+SENDS = [("T", 0, 80), ("D", 0, 160)]
+KY, KX = [(0, 80, "s")], [(0, 40, "s"), (40, 80, "s")]
+ONV = ["TL", "hi"]
 PH = ["S", 0, 0]
-BIAS = {(0, 0): 4360, (1, 0): 5000, (2, 0): 3610, (3, 0): 6440, ('y', 1): -37030, ('P', 0): -4710, ('l', 1): -2010, (1, 1): 470, (0, 1): -860, ('l', 0): -60, ('E', 0): 4060, ('g', 1): 10, ('y', 0): -4660, ('r', 0): 4940, ('r', 1): -1280, ('e', 1): 14430, ('x', 1): -10870, (3, 1): 3360, ('q', 0): -1940, ('d', 0): 15140, ('c', 0): 130, ('e', 0): -5260, ('c', 1): 50, ('k', 1): 1300, ('z', 0): -1340, ('f', 0): -640, ('m', 1): -7610, ('A', 0): 4760, ('q', 1): 3420, ('z', 1): 210, ('f', 1): -390, ('k', 0): -1840, (2, 1): 12020, ('d', 1): -190, ('m', 0): -13880, ('x', 0): 15080, ('g', 0): 5650, ('S', 0): 2260}
 
 SCRATCH = {}
 _W = {}
@@ -27,32 +28,34 @@ _buf("clkw", CW, "bfloat16")
 for _nm, _c in (("dli", NM), ("tli", NM), ("sci", 256), ("sti", 256), ("thi", 1)):
     _buf(_nm, _c, "int32")
 _buf("zin", NM, "bfloat16")
-_buf("tf", 256, "float32"); _buf("tf2", 256, "float32")
+for _nm in ("tf", "tf2", "tf3", "tf4"):
+    _buf(_nm, 256, "float32")
 _buf("sct", 257 + NM, "float32")
 _buf("stt", 257, "float32")
 _buf("ic", 128, "int32"); _buf("ik", 1, "int32"); _buf("i1", 128, "int32"); _buf("i2", 128, "int32"); _buf("i3", 128, "int32")
 _buf("ki", 3, "int32"); _buf("kf", 8, "float32"); _buf("JF", 128, "bfloat16")
-for _nm in ("J1", "J2", "J3", "BD", "ID", "NI", "Ik", "Nh", "Ic", "N8", "P8", "N256", "NU", "P512", "N1024", "PBD8", "NBD8"):
+for _nm in ("J1", "J2", "ZE", "BD", "ID", "NI", "Ik", "Nh", "Ic", "N8", "P8", "N256", "NU", "P512", "N1024", "PBD8", "NBD8"):
     _buf(_nm, 128, "bfloat16")
 _buf("BDf", 128, "float32")
 _buf("ROT", 2048, "float16"); _buf("AS", 2048, "bfloat16"); _buf("SS", 2048, "bfloat16"); _buf("TRI", 2048, "bfloat16")
 _buf("seg0", G16, "bfloat16"); _buf("EQ", G16, "bfloat16"); _buf("seg32", NM, "float32"); _buf("seg16", NM, "float32")
-_buf("pen", NM, "float16"); _buf("NE", NM, "bfloat16"); _buf("CN", 240, "bfloat16"); _buf("IT", 272, "bfloat16")
+_buf("pen", NM, "float16"); _buf("NE", NM, "bfloat16"); _buf("CN", 5 * n, "float16"); _buf("IT", 272, "bfloat16")
 _buf("DUM", 10, "float32"); _buf("CK", 5, "float32"); _buf("dmi", 10, "int32"); _buf("cki", 5, "int32")
 _buf("thc", 1, "float32"); _buf("lim", 1, "float32"); _buf("As", 1, "int32"); _buf("Am", 1, "int32"); _buf("ac", 2, "float32")
 _buf("t1s", NM, "float32"); _buf("pv", 10, "bfloat16"); _buf("VB", NM, "bfloat16"); _buf("el", 1600, "bfloat16")
 _buf("ls", NM, "float32"); _buf("xa", 10, "float32"); _buf("sou", 10, "uint16")
 _buf("yso", 256, "float32"); _buf("fin", 480, "float32")
-_buf("msg", 240 * NH * VIS, "float16"); _buf("out", 240 * NH * (VIS - 1), "float16")
+_buf("inT", n * NH * VIS, "uint16"); _buf("outT", n * NH * (VIS - 1), "uint16")
+_buf("inD", NM * NH * VIS, "float16"); _buf("outD", NM * NH * (VIS - 1), "float16")
 for _h in range(NH):
-    for _nm, _c, _d in (("offT", n, "uint16"), ("off1", n, "uint16"), ("Y", G16, "bfloat16"), ("X", G16, "bfloat16"), ("mn", G16, "bfloat16"),
-                        ("eq", G16, "bfloat16"), ("eg", G16, "bfloat16"), ("tp", G16, "bfloat16"), ("bf", 16 * n, "bfloat16"), ("hf", 8 * n, "float16"),
-                        ("f3", 8 * n, "float32"), ("nk", [5, 32], "float32"), ("vs", NM, "int32"), ("ri", n, "int32"),
+    for _nm, _c, _d in (("off1", n, "uint16"), ("Y", G16, "bfloat16"), ("X", G16, "bfloat16"), ("mn", G16, "bfloat16"),
+                        ("eq", G16, "bfloat16"), ("eg", G16, "bfloat16"), ("tp", G16, "bfloat16"), ("bf", 13 * n, "bfloat16"), ("hf", 7 * n, "float16"),
+                        ("f3", 10 * n, "float32"), ("nk", [5, 32], "float32"), ("vs", NM, "int32"), ("ri", n, "int32"),
                         ("li", 16, "int32"), ("lu", 24, "uint16"), ("lf", 8, "float32")):
         _buf(_nm + str(_h), _c, _d)
 
 SEMAPHORES = (["sv", "ss", "st_", "sg", "snd"] + ["ld%d" % i for i in range(7)]
-              + ["arr%d%d%d" % (t, h, k) for t in range(1, VIS) for h in range(NH) for k in range(len(SENDS))] + ["wr0", "wr1"])
+              + ["arr%d%d%d" % (t, h, k) for t in range(1, VIS) for h in range(NH) for k in range(len(SENDS))] + ["wr0", "wr1", "wr2", "wr3"])
 
 
 def _cols(name):
@@ -83,6 +86,7 @@ def wid(x):
 def _build():
     ops = []
     PH[:] = ["S", 0, 0]
+    ring = [0]
 
     def add(q, call, args, reads, writes, cost, **kw):
         d = {"ph": tuple(PH), "q": q, "call": call, "args": args, "r": reads, "w": writes, "cost": cost, "id": len(ops)}
@@ -135,9 +139,15 @@ def _build():
     def VT(out, a):
         add("v", "vt", (out, a), [a], [out], vcost(out, [a], False))
 
-    def ACT(out, a, f, bias=0.0, scale=1.0, acc=None):
+    def ACT(out, a, f, bias=0.0, scale=1.0, acc=None, nm=None):
         k = wid(out)
-        c = 65 + 1.56 * CY * k if a[0] == "IND" else max(64, k) * CY + (20 if acc else 0)
+        if nm == "v" or nm in ONV:
+            if f == AF.Relu:
+                return TS(out, a, bias, OP.add, 0.0, OP.max) if scale == 1.0 else TS(out, a, bias - 0.5, OP.is_lt)
+            if scale == 1.0:
+                return CP(out, a) if bias == 0.0 else TS(out, a, bias, OP.add)
+            return TS(out, a, scale, OP.mult, bias, OP.add)
+        c = 65 + 1.56 * CY * k if a[0] == "IND" else 10 + max(64, k) * CY + (20 if acc else 0)
         add("s", "act", (out, a, f, bias, scale, acc), rd(a) + [x for x in (bias, scale) if isinstance(x, tuple)], [out] + ([acc] if acc else []), c)
 
     def MM(lst, more=False, cont=False):
@@ -153,8 +163,14 @@ def _build():
     def IO(x, pat, base, mul):
         add("g", "iota", (x, pat, base, mul), [], [x], 130 + 1.7 * wid(x))
 
+    def SEL(out, a, pat, op, fill, base):
+        add("g", "asel", (out, a, pat, op, fill, base), [a], [out], 170 + 1.7 * wid(out))
+
     def blk(name, q):
         return F(name, 128 * q, 128 * q + 128)
+
+    def CN(i, k=1):
+        return F("CN", i * n, (i + k) * n)
 
     ID, BD, N8, P8 = F("ID"), F("BD"), F("N8"), F("P8")
     LD("s", F("clkw", 16, CW), "clk", "ld6")
@@ -171,6 +187,7 @@ def _build():
     IO(F("cki"), [[256, 5]], 15, 0)
     IO(F("IT"), [[1, 272]], 0, 0)
     MS(F("clkw", 0, 16), -1.0)
+    MS(F("ZE"), 0.0)
     TS(F("ki", 0, 1), F("ik"), 4, OP.arith_shift_right)
     TS(F("ki", 1, 2), F("ik"), 15, OP.bitwise_and)
     TS(F("ki", 2, 3), F("ik"), 4, OP.arith_shift_right, 1, OP.bitwise_and)
@@ -183,18 +200,17 @@ def _build():
     TS(F("i3"), F("ic"), 15, OP.bitwise_and)
     TT(F("J1"), F("i1"), F("JF"), OP.max)
     TT(F("J2"), F("i3"), F("JF"), OP.max)
-    TS(F("J3"), BD, kp, OP.mult)
-    TS(ID, F("J1"), 0.0, OP.is_equal)
     for q in range(16):
         TS(blk("ROT", q), F("J1"), float(q), OP.is_equal)
     for q in range(16):
         TS(blk("SS", q), F("J2"), float(q), OP.is_equal)
+    for nm, c in (("ID", 1.0), ("Ic", 1.0 / 64), ("N8", -8192.0), ("Ik", 1.0 / 4096), ("Nh", -1.0 / 16), ("P8", 8192.0), ("N256", -256.0),
+                  ("NU", -16640.0), ("P512", 512.0), ("N1024", -1024.0), ("NI", -1.0)):
+        SEL(F(nm), F("ZE"), [[-1, 128]], OP.not_equal, c, 0)
+    for nm, c in (("PBD8", 8192.0), ("NBD8", -8192.0), ("BDf", 0.5)):
+        ACT(F(nm), BD, AF.Copy, 0.0, c)
     for q in range(15):
-        TS(blk("TRI", q), F("J3"), float(q), OP.is_gt, 8192.0, OP.mult)
-    for nm, src, c in (("Ic", ID, 1.0 / 64), ("N8", ID, -8192.0), ("Ik", ID, 1.0 / 4096), ("Nh", ID, -1.0 / 16), ("P8", ID, 8192.0),
-                       ("PBD8", BD, 8192.0), ("NBD8", BD, -8192.0), ("N256", ID, -256.0), ("NU", ID, -16640.0), ("P512", ID, 512.0),
-                       ("N1024", ID, -1024.0), ("NI", ID, -1.0), ("BDf", BD, 0.5)):
-        ACT(F(nm), src, AF.Copy, 0.0, c)
+        SEL(blk("TRI", q), F("PBD8"), [[-16, 8], [0, 16]], OP.is_gt, 0.0, -q)
     for j in range(4):
         for i in range(4):
             o = F("p%d" % (4 + j), 128 * i, 128 * i + 128)
@@ -211,190 +227,197 @@ def _build():
     for nm, k in (("seg32", 32), ("seg16", 16)):
         MS(F(nm), 1e9)
         MS(F(nm, 0, NM, k), -1e9)
-    MS(F("CN", 0, NM), -2.0)
-    MS(F("CN", NM, 240), -1.0)
+    for i, c in enumerate((-16384.0, 2064.0 - 16384.0, 2064.0 - 8192.0, -1024.0, 1024.0)):
+        MS(CN(i), c)
     TS(F("DUM"), F("dmi"), kp, OP.add)
     TS(F("kf", 3, 4), kp, 16.0, OP.mult)
     TS(F("CK"), F("cki"), F("kf", 3, 4), OP.add)
-    TS(F("kf", 4, 5), kp, -256.0, OP.mult, 35071.0 + 3840.0, OP.add)
+    TS(F("kf", 4, 5), kp, -256.0, OP.mult, 35072.0 + 3840.0, OP.add)
     TS(F("kf", 5, 6), ko, -33554432.0, OP.mult, F("kf", 4, 5), OP.add)
     TS(F("kf", 7, 8), ko, 33554432.0, OP.mult, -33554432.0, OP.add)
     TS(F("kf", 6, 7), F("kf", 7, 8), F("kf", 4, 5), OP.add)
-    ACT(F("t1s"), F("tli"), AF.Copy, 0.0, 3.0)
-    TT(F("t1s"), F("t1s"), F("tli"), OP.min)
+    for src, tmp, k, c, out in (("tli", "tf", NM, 4.0, None), ("dli", "tf2", NM, 2.0, None), ("sti", "tf3", 256, 4.0, "stt"), ("sci", "tf4", 256, 2.0, "sct")):
+        ACT(F(tmp, 0, k), F(src), AF.Copy, 0.0, c)
+        TT(F(tmp, 0, k), F(tmp, 0, k), F(src), OP.min)
+        if out:
+            MS(F(out), -2048.0 - c)
+            ACT(F(out, 1, 257), F(tmp), AF.Copy, -2048.0)
+    TS(F("inT", 0, NM), F("tf", 0, NM), 16.0, OP.add)
     for h in range(NH):
-        m = 240 * h
-        TS(F("msg", m, m + n), F("t1s", h * n, h * n + n), -2047.0, OP.add)
-        ACT(F("msg", m + n, m + 2 * n), F("dli", h * n, h * n + n), AF.Copy, -2047.0)
-        ACT(F("msg", m + 2 * n, m + 3 * n), F("zin", h * n, h * n + n), AF.Copy, 1024.0)
-    TS(F("thc"), F("thi"), -0.5, OP.mult, -8200.8125, OP.add)
+        ACT(F("inD", NM * h, NM * h + n), F("tf2", h * n, h * n + n), AF.Copy, -2048.0)
+        ACT(F("inD", NM * h + n, NM * h + NM), F("zin", h * n, h * n + n), AF.Copy, 1024.0)
+    TS(F("thc"), F("thi"), 16401.525, OP.add)
     CP(F("lim"), F("thc"))
     MS(F("As"), 0)
-    MS(F("sct"), -2048.0)
-    ACT(F("sct", 1, 257), F("sci"), AF.Copy, -2047.0)
-    MS(F("stt", 0, 1), -2050.0)
-    ACT(F("tf"), F("sti"), AF.Copy, 0.0, 3.0)
-    TT(F("tf2"), F("tf"), F("sti"), OP.min)
-    ACT(F("stt", 1, 257), F("tf2"), AF.Copy, -2047.0)
 
-    CH = [list(range(0, 6)), list(range(6, 12)), list(range(12, 16))]
+    CH = [range(0, 7), range(7, 14), range(14, 16)]
+    CQ = [range(0, 4), range(4, 10), range(10, 16)]
+    CS = [range(0, 7), range(7, 14)]
 
     def visit(t, h):
         last = t == VIS - 1
         H = str(h)
-        m = 240 * (NH * t + h)
-        TL, D, Z = F("msg", m, m + n), F("msg", m + n, m + 2 * n), F("msg", m + 2 * n, m + 3 * n)
-        B = ["p%d" % (4 * h + i) for i in range(4)]
+        k0 = NH * t + h
+        offT, D, Z = F("inT", n * k0, n * k0 + n), F("inD", NM * k0, NM * k0 + n), F("inD", NM * k0 + n, NM * k0 + NM)
 
         def P(b, i, k=1):
-            return F(B[b], i * n, (i + k) * n)
+            return F("p%d" % (4 + 2 * h + b), i * n, (i + k) * n)
+
+        def R(j, i):
+            return F("p%d" % (j + 1 if j else ring[0] % 2), i * n, i * n + n)
 
         def bf(i, k=1):
             return F("bf" + H, i * n, (i + k) * n)
 
-        def hf(i, k=1):
-            return F("hf" + H, i * n, (i + k) * n)
-
         def f3(i, k=1):
             return F("f3" + H, i * n, (i + k) * n)
 
-        def compare(src, own, e, acc, w, first, rest):
-            for j, qs in enumerate(CH):
-                MM([(P(j % 2, i), blk("ROT", q), src) for i, q in enumerate(qs)])
+        def compare(src, own, e, w, first, rest):
+            for j, qs in enumerate(CQ):
+                MM([(R(j, i), blk("ROT", q), src) for i, q in enumerate(qs)])
+            for j, qs in enumerate(CQ):
                 for i, q in enumerate(qs):
-                    TT(F(e, q * n, q * n + n), own, P(j % 2, i), OP.is_equal)
-                MM((first if j == 0 else []) + [(acc, w(q), F(e, q * n, q * n + n)) for q in qs], True, j > 0)
-            MM(rest, False, True)
+                    TT(F(e, q * n, q * n + n), own, R(j, i), OP.is_equal)
+            for j, qs in enumerate(CS):
+                MM((first if j == 0 else []) + [(R(0, 4), w(q), F(e, q * n, q * n + n)) for q in qs], True, j > 0)
+            MM(rest[0], True, True)
+            MM([(R(0, 4), w(q), F(e, q * n, q * n + n)) for q in (14, 15)] + rest[1], False, True)
+            ring[0] += 1
 
-        offT, off1, clk, Y = F("offT" + H), F("off1" + H), F("clkw"), F("Y" + H)
+        def gather(out, off, parts):
+            for a, b, q in parts:
+                ACT(F(out, 16 * a, 16 * b), IND(F("clkw"), F(off[0], off[1] + a, off[1] + b)), AF.Copy, nm=q)
+
+        off1, Y = F("off1" + H), F("Y" + H)
         hi, E, hiU, fl, nct, fc, NG, oh, kmT, ykm, A2 = bf(0), bf(1), bf(2), bf(3), bf(4), bf(5), bf(6, 2), bf(8), bf(9), bf(10), bf(11)
         N, G = bf(6), bf(7)
-        cv, sv, wD, wT, yk, r1, tD, tT = [hf(i) for i in range(8)]
+        TL, cv, sv, wD, yk, r1, tD = [F("hf" + H, i * n, i * n + n) for i in range(7)]
         luv, luk, luw = [F("lu" + H, 8 * i, 8 * i + 5) for i in range(3)]
         PH[0] = "y"
-        ACT(offT, TL, AF.Identity, 2063.0)
-        ACT(Y, IND(clk, offT), AF.Copy)
+        gather("Y" + H, offT, KY)
         PH[0] = "e"
-        ACT(hi, TL, AF.Identity, 136.498046875, 1.0 / 256)
-        MM([(P(2, 1), BD, hi)])
-        ACT(E, P(2, 1), AF.Relu, 2049.0, -1.0)
-        MM([(P(2, 2), BD, Z)])
-        ACT(hiU, P(2, 2), AF.Identity, 64.501953125, 1.0 / 256)
+        ACT(TL, offT, AF.Identity, -2064.0, nm="TL")
+        ACT(hi, offT, AF.Identity, 129 - 143.5 / 256, 1.0 / 256, nm="hi")
+        MM([(P(0, 3), BD, hi)])
+        ACT(E, P(0, 3), AF.Relu, 2049.0, -1.0, nm="E")
+        MM([(P(0, 4), BD, Z)])
+        ACT(hiU, P(0, 4), AF.Identity, 64.501953125, 1.0 / 256, nm="hiU")
         PH[0] = "q"
-        acc = P(2, 0)
-        compare(TL, D, "eq" + H, acc, lambda q: blk("AS", q), [(acc, ID, D)], [(acc, F("Ic"), F("eq" + H, 0, n)), (acc, N8, E)])
+        acc = R(0, 4)
+        compare(TL, D, "eq" + H, lambda q: blk("AS", q), [], [[(acc, ID, D), (acc, F("Ic"), F("eq" + H, 0, n)), (acc, N8, E)], []])
         PH[0] = "x"
-        ACT(off1, acc, AF.Relu, 2063.0)
-        ACT(F("ri" + H), acc, AF.Identity)
-        ACT(fl, acc, AF.Sign, 2047.5)
+        ACT(F("ri" + H), acc, AF.Identity, nm="ri")
         TT(nct, F("ri" + H), acc, OP.is_equal)
-        ACT(F("X" + H), IND(clk, off1), AF.Copy)
+        ACT(off1, acc, AF.Relu, 2064.0, nm="off1")
+        ACT(fl, acc, AF.Sign, 2049.0)
+        gather("X" + H, off1, KX)
         SC(F("tp" + H), F("seg0"), F("X" + H), 0.0, OP.mult, OP.max)
         PH[0] = "m"
-        zps, Gp, key = P(3, 0), P(0, 0), P(1, 0)
-        MM([(zps, F("P512"), F("CN", 0, n)), (zps, ID, Z)])
+        zps, Gp, key = P(1, 0), R(0, 5), P(0, 0)
+        MM([(zps, ID, CN(3)), (zps, ID, Z)])
         for q in range(16):
             TT(F("mn" + H, q * n, q * n + n), F("Y" + H, q, G16, 16), zps, OP.min)
-        MM([(Gp, blk("SS", q), F("Y" + H, q, G16, 16)) for q in range(16)], True)
-        MM([(Gp, BD, Z), (Gp, N8, nct)], False, True)
+        MM([(Gp, blk("SS", q), F("Y" + H, q, G16, 16)) for q in range(16)] + [(Gp, BD, Z)], True)
+        MM([(Gp, N8, nct)], False, True)
         MM([(key, F("Ik"), TL), (key, F("Nh"), hi)], True)
         for j, qs in enumerate(CH):
             MM([(key, blk("SS", q), F("mn" + H, q * n, q * n + n)) for q in qs], j < 2, True)
         PH[0] = "k"
-        ACT(BLK("nk" + H, 0), key, AF.Identity, F("kf", 5, 6), 4096.0)
-        ACT(BLK("nk" + H, 1), key, AF.Identity, F("kf", 6, 7), 4096.0)
+        ACT(BLK("nk" + H, 0), key, AF.Identity, F("kf", 5, 6), 4096.0, nm="nk0")
+        ACT(BLK("nk" + H, 1), key, AF.Identity, F("kf", 6, 7), 4096.0, nm="nk1")
         vt, vs = f3(0, 2), F("vs" + H)
         VT(vt, F("nk" + H))
         SC(vs, F("seg32"), vt, -1e9, OP.min, OP.max)
         kb, va, kk = F("vs" + H, 31, NM, 32), F("li" + H, 0, 5), F("li" + H, 8, 13)
         TS(va, kb, 255, OP.bitwise_and)
         TS(luv, va, 1.0, OP.add)
-        ACT(sv, IND(F("stt"), luv), AF.Copy)
+        ACT(sv, IND(F("stt"), luv), AF.Copy, nm="sv")
         TS(kk, kb, 8, OP.arith_shift_right, 15, OP.bitwise_and)
         TT(luk, F("CK"), kk, OP.subtract)
-        ACT(oh, IND(F("EQ"), luk), AF.Copy)
-        ACT(yk, IND(Y, luk), AF.Copy)
+        ACT(oh, IND(F("EQ"), luk), AF.Copy, nm="oh")
+        ACT(yk, IND(Y, luk), AF.Copy, nm="yk")
         PH[0] = "c"
-        G2 = f3(2)
-        ACT(G2, Gp, AF.Identity, F("lim"), 0.5)
-        TT(fc, G2, key, OP.is_gt)
-        MM([(P(2, 3), BD, fl), (P(2, 3), F("PBD8"), fc)])
-        MM([(P(2, 4), BD, fl), (P(2, 4), F("NBD8"), fc)])
-        ACT(NG, P(2, 3, 2), AF.Sign, 15.0)
+        K2 = f3(2)
+        ACT(K2, key, AF.Identity, F("lim"), 2.0, nm="K2")
+        TT(fc, K2, Gp, OP.is_lt)
+        MM([(P(0, 1), BD, fl), (P(0, 2), BD, fl), (P(0, 1), F("PBD8"), fc), (P(0, 2), F("NBD8"), fc)])
+        ACT(NG, P(0, 1, 2), AF.Sign, 15.0)
         if not last:
-            cx = P(3, 5)
+            cx = P(1, 5)
             MM([(cx, ID, D), (cx, N8, fl), (cx, N8, E), (cx, F("NBD8"), fc)])
-            ACT(bf(12), cx, AF.Sign, -6144.5, 1.0, F("ac", h, h + 1))
+            ACT(bf(12), cx, AF.Sign, -6143.0, 1.0, F("ac", h, h + 1))
         PH[0] = "l"
-        X1, X2 = P(3, 1), P(3, 2)
-        MM([(P(3, 1, 2), ID, F("pen")), (X1, BD, Z), (X1, F("N256"), hiU), (X2, F("N1024"), E), (X1, F("NU"), N), (X2, F("P512"), N), (X2, F("N1024"), G)])
-        SC(f3(3, 2), F("seg16"), P(3, 1, 2), -1e9, OP.min, OP.max)
+        X1, X2 = P(1, 1), P(1, 2)
+        MM([(P(1, 1, 2), ID, F("pen")), (X1, BD, Z), (X1, F("N256"), hiU), (X2, F("N1024"), E), (X1, F("NU"), N), (X2, F("P512"), N), (X2, F("N1024"), G)])
+        SC(f3(3, 2), F("seg16"), P(1, 1, 2), -1e9, OP.min, OP.max)
         a1 = F("lf" + H, 0, 5)
         TT(a1, va, F("f3" + H, 4 * n + 15, 5 * n, 16), OP.add)
         TT(luw, a1, F("f3" + H, 3 * n + 15, 4 * n, 16), OP.max)
-        ACT(wT, IND(F("stt"), luw), AF.Copy)
+        wT, tT = f3(8), f3(9)
+        ACT(wT, IND(F("stt"), luw), AF.Identity, 2064.0, nm="wT")
         ACT(F("pv", 5 * h, 5 * h + 5), a1, AF.Abs, 1024.0)
         PH[0] = "d"
-        t1p, dg, tg = P(3, 0), P(3, 3), P(3, 4)
+        t1p, dg, tg = P(1, 0), P(1, 3), P(1, 4)
         MM([(t1p, ID, TL), (t1p, P8, nct), (t1p, N8, oh)])
-        ACT(kmT, t1p, AF.Relu, -6144.0)
-        MM([(P(3, 3, 2), P8, F("CN", 0, NM)), (dg, ID, D), (dg, P8, fl), (tg, ID, TL), (tg, P8, nct), (tg, N8, oh), (dg, P8, G), (tg, P8, G)])
+        ACT(kmT, t1p, AF.Relu, -6142.0, nm="kmT")
+        MM([(P(1, 3, 2), ID, CN(0, 2)), (dg, ID, D), (dg, P8, fl), (tg, ID, TL), (tg, P8, nct), (tg, N8, oh), (dg, P8, G), (tg, P8, G)])
         TT(tT, wT, tg, OP.max)
-        o = 240 * (NH * t + h)
-        oT, oD, oZ = (f3(5), f3(6), f3(7)) if last else [F("out", o + i * n, o + i * n + n) for i in range(3)]
+        oT, oD, oZ = (f3(5), f3(6), f3(7)) if last else (F("outT", n * k0, n * k0 + n), F("outD", NM * k0, NM * k0 + n), F("outD", NM * k0 + n, NM * k0 + NM))
         PH[0] = "g"
-        rT = P(2, 5)
-        compare(TL, sv, "eg" + H, rT, lambda q: N8, [(rT, ID, sv), (rT, P8, F("CN", NM, 240))], [(rT, N8, kmT), (rT, P8, G)])
+        rT = R(0, 4)
+        compare(TL, sv, "eg" + H, lambda q: N8, [(rT, ID, CN(2))], [[(rT, ID, sv), (rT, P8, G)], [(rT, N8, kmT)]])
         TT(oT, tT, rT, OP.max)
         PH[0] = "f"
-        ACT(F("t1s", h * n, h * n + n), t1p, AF.Relu, -6144.0)
-        ACT(F("VB", h * n, h * n + n), IND(F("IT"), luv), AF.Copy)
-        ACT(cv, IND(F("sct", 0, 257), luv), AF.Copy)
-        ACT(wD, IND(F("sct", 0, 257), luw), AF.Copy)
+        ACT(F("t1s", h * n, h * n + n), t1p, AF.Relu, -6142.0, nm="t1s")
+        ACT(F("VB", h * n, h * n + n), IND(F("IT"), luv), AF.Copy, nm="VB")
+        ACT(cv, IND(F("sct", 0, 257), luv), AF.Copy, nm="cv")
+        ACT(wD, IND(F("sct", 0, 257), luw), AF.Copy, nm="wD")
         TT(tD, wD, dg, OP.max)
-        rD = P(3, 1)
-        compare(D, cv, "eq" + H, rD, lambda q: N8, [(rD, ID, cv), (rD, P8, F("CN", 0, n))], [(rD, N8, fl), (rD, P8, G)])
+        rD = R(0, 4)
+        compare(D, cv, "eq" + H, lambda q: N8, [(rD, ID, CN(0)), (rD, N8, fl)], [[(rD, ID, cv), (rD, P8, G)], []])
         TT(oD, tD, rD, OP.max)
         PH[0] = "z"
-        yp, zd, z1, zp = P(2, 1), P(2, 2), P(2, 3), P(2, 4)
+        yp, zd, z1, zp = P(0, 3), P(0, 4), P(0, 1), P(0, 2)
         MM([(yp, ID, yk), (yp, F("P512"), N)])
-        ACT(ykm, yp, AF.Relu, -512.0)
+        ACT(ykm, yp, AF.Relu, -512.0, nm="ykm")
         MM([(zd, ID, Z), (zd, F("P512"), G), (zd, F("NI"), ykm)])
         ACT(A2, zd, AF.Abs, -512.0)
-        MM([(z1, F("N1024"), G), (z1, ID, ykm), (z1, ID, F("tp" + H, 15, G16, 16))])
-        ACT(r1, z1, AF.Identity, 1535.8, 0.5)
-        MM([(zp, F("N1024"), F("CN", NM, 240)), (zp, ID, A2)])
+        MM([(z1, F("N1024"), G), (z1, ID, yk), (z1, ID, F("tp" + H, 15, G16, 16))])
+        ACT(r1, z1, AF.Identity, 1535.8, 0.5, nm="r1")
+        MM([(zp, ID, CN(4)), (zp, ID, A2)])
         TT(oZ, r1, zp, OP.min)
         PH[0] = "r"
         if last:
-            TS(F("fin", h * n, h * n + n), oD, 2047.0, OP.add, -1.0, OP.max)
-            TS(F("fin", 160 + h * n, 160 + h * n + n), oT, 2047.0, OP.add, -1.0, OP.max)
+            TS(F("fin", h * n, h * n + n), oD, 2048.0, OP.add, -1.0, OP.max)
+            TS(F("fin", 160 + h * n, 160 + h * n + n), oT, -16.0, OP.add, -1.0, OP.max)
             ACT(F("fin", 320 + h * n, 320 + h * n + n), oZ, AF.Copy, -1024.0)
         else:
-            for k, (a, b) in enumerate(SENDS):
-                add("g", "send", (t, h, k), [F("out", o + a, o + b)], [], 200)
-                add("n", "arrive", (t, h, k), [], [F("msg", o + 240 * NH + a, o + 240 * NH + b)], 0)
+            for k, (x, a, b) in enumerate(SENDS):
+                w = n if x == "T" else NM
+                add("g", "send", (t, h, k), [F("out" + x, w * k0 + a, w * k0 + b)], [], 200, to=F("in" + x, w * (k0 + NH) + a, w * (k0 + NH) + b))
+                add("n", "arrive", (t, h, k), [], [ops[-1]["to"]], 0)
 
     def proofs(t):
-        lp = F("p7", 320, 480) if t == VIS - 1 else F("p3", 320, 480)
+        a = 3 * n
+        lp = F("p6", a, a + NM)
         lst = [(lp, N8, F("NE"))]
         for c in range(10):
             TS(F("el", 160 * c, 176 * c + 16), F("VB", 0, 16 * c + 16), F("pv", c, c + 1), OP.is_equal)
             if c:
-                lst.append((F(lp[0], 320, 320 + 16 * c), F("PBD8"), F("el", 160 * c, 176 * c)))
-        lst += [(F(lp[0], 320 + r, 480, 16), blk("TRI", r), F("el", r, 1600, 176)) for r in range(15)]
+                lst.append((F("p6", a, a + 16 * c), F("PBD8"), F("el", 160 * c, 176 * c)))
+        lst += [(F("p6", a + r, a + NM, 16), blk("TRI", r), F("el", r, 1600, 176)) for r in range(15)]
         MM(lst)
         SC(F("ls"), F("seg16"), lp, -1e9, OP.min, OP.max)
         TT(F("xa"), F("ls", 15, NM, 16), F("pv"), OP.max)
         TT(F("sou"), F("xa"), F("DUM"), OP.min)
-        TS(IND(F("sct"), F("sou")), F("t1s"), 1.0, OP.mult, -2048.0, OP.add)
+        TS(IND(F("sct"), F("sou")), F("t1s"), 1.0, OP.mult, -2050.0, OP.add)
 
     def count():
         pa = F("p7", 504, 505)
         MM([(pa, F("BDf"), F("ac", 0, 1)), (pa, F("BDf"), F("ac", 1, 2))])
         TT(F("As"), F("As"), pa, OP.add)
         TS(F("Am"), F("As"), 31, OP.bitwise_and)
-        TS(F("lim"), F("Am"), -4.0, OP.mult, F("thc"), OP.add)
+        TS(F("lim"), F("Am"), 8.0, OP.mult, F("thc"), OP.add)
 
     for t in range(VIS):
         for h in range(NH):
@@ -406,9 +429,9 @@ def _build():
         PH[:] = ["P", t, 0]
         proofs(t)
     PH[:] = ["E", 0, 0]
-    ACT(F("yso"), F("sct", 1, 257), AF.Copy, 2047.0)
-    add("y", "sto", [("yd", 0), ("yt", 160), ("yz", 320)], [F("fin")], [], 100, dma="wr0", lat=2500)
-    add("y", "stys", None, [F("yso")], [], 50, dma="wr1", lat=2500)
+    TS(F("yso"), F("sct", 1, 257), 2048.0, OP.add, -1.0, OP.max)
+    for k, (nm, src) in enumerate((("yd", F("fin", 0, NM)), ("yt", F("fin", NM, 2 * NM)), ("yz", F("fin", 2 * NM, 3 * NM)), ("ys", F("yso")))):
+        add("y", "sto", (nm, src), [src], [], 50, dma="wr%d" % k, lat=2500)
     return ops
 
 
@@ -453,10 +476,11 @@ def _deps(ops):
             a |= anc[d] | (1 << d)
         anc.append(a)
         if o["call"] == "mm":
-            key = (o["banks"][0], o["w"][-1][1])
+            key = (o["banks"][0],)
             if o["args"][1]:
                 starts.setdefault(key[0], []).append(o["id"])
-                opener[key] = o
+                if not o["args"][2]:
+                    opener[key] = o
             elif o["args"][2]:
                 f = opener[key]
                 for s in starts[key[0]]:
@@ -464,16 +488,96 @@ def _deps(ops):
                         f["dep"].setdefault(s, False)
 
 
-LAT = {"x": 130.0, "own": 80.0, "arr": 3800.0, "fix": 20.0}
-SCALE = 1.1
+LAT = {"x": 250.0, "own": 200.0, "arr": 2500.0}
+SCALE = 1.05
 
 
-def _schedule(ops, bias):
+def _place(ops, pre, rank, back):
     succ = [[] for _ in ops]
-    for o in ops:
-        for d in o["dep"]:
-            succ[d].append(o["id"])
+    left = [len(p) for p in pre]
+    for i, p in enumerate(pre):
+        for (d, w) in p:
+            succ[d].append((i, w))
+    rt = [0.0] * len(ops)
+    start = [0.0] * len(ops)
+    busy, bank, sums, opened, tend = {}, {}, {}, {}, {}
+    ready = sorted((rank[i], i) for i in range(len(ops)) if not left[i])
+    while ready:
+        for k, (_r, i) in enumerate(ready):
+            o = ops[i]
+            q, c, s = o["q"], o["len"], rt[i]
+            first = whole = False
+            if q == "t":
+                b0 = o["banks"][0]
+                st, sp = (o["args"][2], o["args"][1]) if back else o["args"][1:]
+                first, whole = st and not sp, st and sp
+                if first:
+                    if b0 in opened:
+                        continue
+                    s = max(s, tend.get(b0, 0.0))
+            if q != "n":
+                lists = [(busy.setdefault(q, []), 0.0, None)] + [(bank.setdefault(b, []), LAT["x"], q) for b in o["banks"]]
+                if whole:
+                    lists.append((sums.setdefault(b0, []), 0.0, None))
+                moved = True
+                while moved:
+                    moved = False
+                    for L, m, own in lists:
+                        for j in range(len(L) - 1, -1, -1):
+                            a, e, q2 = L[j]
+                            if e + m <= s:
+                                break
+                            if q2 != own and a - m < s + c:
+                                s = e + m
+                                moved = True
+                if whole and b0 in opened and s + c > opened[b0]:
+                    continue
+                for L, m, own in lists[:1 + len(o["banks"])]:
+                    j = len(L)
+                    while j and L[j - 1][1] > s + c:
+                        j -= 1
+                    L.insert(j, (s, s + c, q if own else 1))
+                if q == "t":
+                    tend[b0] = max(tend.get(b0, 0.0), s + c)
+                    if first:
+                        opened[b0] = s
+                    elif sp and not st:
+                        sums.setdefault(b0, []).append((opened.pop(b0), s + c, 1))
+            break
+        else:
+            return None
+        del ready[k]
+        start[i] = s
+        for (y, w) in succ[i]:
+            rt[y] = max(rt[y], s + c + w)
+            left[y] -= 1
+            if not left[y]:
+                j = 0
+                while j < len(ready) and ready[j][0] <= rank[y]:
+                    j += 1
+                ready.insert(j, (rank[y], y))
+    return start
 
+
+def _justify(ops, pre, rank, rounds):
+    post = [[] for _ in ops]
+    for i, p in enumerate(pre):
+        for (d, w) in p:
+            post[d].append((i, w))
+    best = (1e12, None)
+    for k in range(rounds):
+        start = _place(ops, pre, rank, False)
+        if start is None:
+            break
+        best = min(best, (max(s + o["len"] for s, o in zip(start, ops)), start))
+        back = _place(ops, post, [-(s + o["len"]) for s, o in zip(start, ops)], True)
+        if back is None:
+            break
+        rank = [-(s + o["len"]) for s, o in zip(back, ops)]
+    return best
+
+
+def _graph(ops):
     def dly(a, b):
         if a["call"] == "send":
             return LAT["arr"] if b["call"] == "arrive" else 0.0
@@ -482,60 +586,57 @@ def _schedule(ops, bias):
         if not b["dep"][a["id"]]:
             return 0.0
         return LAT["own"] if a["q"] == b["q"] else LAT["x"]
-    pri = [0.0] * len(ops)
-    for o in list(reversed(ops)) * 2:
-        pri[o["id"]] = o["cost"] + max([pri[s] + dly(o, ops[s]) for s in succ[o["id"]]] + [0.0])
-    pri = [p + bias.get((o["ph"][0], o["ph"][2]), 0.0) + bias.get(o["ph"][1:], 0.0) for p, o in zip(pri, ops)]
-    left = [len(o["dep"]) for o in ops]
-    rt = [0.0] * len(ops)
-    ready, free, order, start, end = {}, {}, {}, [0.0] * len(ops), 0.0
-    users, opened, extra = {}, set(), {}
+    seen = {}
     for o in ops:
-        if not left[o["id"]]:
-            ready.setdefault(o["q"], []).append(o["id"])
-    for _ in range(len(ops)):
-        best = None
-        for q, L in ready.items():
-            f = free.get(q, 0.0)
-            for i in L:
-                s = rt[i] if q == "n" else max(f, rt[i])
-                if best is not None and s > best[0][0]:
-                    continue
-                o = ops[i]
-                if o["banks"]:
-                    if q == "t" and o["args"][1] and o["banks"][0] in opened:
-                        continue
-                    for b in o["banks"]:
-                        for q2, (e2, _j) in users.get(b, {}).items():
-                            if q2 != q:
-                                s = max(s, e2 + LAT["x"])
-                k = (s, -pri[i])
-                if best is None or k < best[0]:
-                    best = (k, q, i)
-        (s, _p), q, i = best
-        ready[q].remove(i)
+        o["len"] = 0.0 if o["q"] == "n" else o["cost"] * SCALE
+        k = o["ph"] + (o["q"],)
+        seen[k] = seen.get(k, 0) + 1
+        o["tag"] = (o["ph"][0], o["q"], seen[k])
+    return [[(d, dly(ops[d], o)) for d in o["dep"]] for o in ops]
+
+
+def _alone(ops, pre):
+    ids = [o["id"] for o in ops if o["ph"][1:] == (1, 0) and o["ph"][0] not in "SPAE"]
+    loc = {i: k for k, i in enumerate(ids)}
+    sub = [ops[i] for i in ids]
+    p = [[(loc[d], w) for (d, w) in pre[i] if d in loc] for i in ids]
+    way = [0.0] * len(ids)
+    for k in list(reversed(range(len(ids)))) * 2:
+        for (d, w) in p[k]:
+            way[d] = max(way[d], way[k] + sub[k]["len"] + w)
+    start = _justify(sub, p, [-x - o["len"] for x, o in zip(way, sub)], 3)[1]
+    return {o["tag"]: s for o, s in zip(sub, start)}
+
+
+def _ranks(ops, pre, tau, period, lag, lean):
+    rank = [1e9] * len(ops)
+    for o in ops:
+        ph = o["ph"]
+        if ph[0] in "PAE":
+            rank[o["id"]] = max(rank[d] + ops[d]["len"] + w for (d, w) in pre[o["id"]] if ops[d]["ph"][0] != "S") + lean.get(ph[0], 0.0)
+        elif ph[0] != "S":
+            rank[o["id"]] = tau.get(o["tag"], max(tau.values())) + ph[1] * period + ph[2] * lag + lean.get(ph[0], 0.0)
+    for o in reversed(ops):
+        for (d, w) in pre[o["id"]]:
+            if ops[d]["ph"][0] == "S":
+                rank[d] = min(rank[d], rank[o["id"]] - w - ops[d]["len"] + (lean.get("S", 0.0) if o["ph"][0] != "S" else 0.0))
+    return rank
+
+
+def _orders(ops, start):
+    order, users = {}, {}
+    for i in sorted(range(len(ops)), key=lambda i: (start[i], i)):
         o = ops[i]
-        e = s + o["cost"] + (0.0 if q == "n" else LAT["fix"])
-        extra[i] = [j for b in o["banks"] for q2, (e2, j) in users.get(b, {}).items() if q2 != q]
+        order.setdefault(o["q"], []).append(i)
         for b in o["banks"]:
-            users.setdefault(b, {})[q] = (e, i)
-        if q == "t":
-            if o["args"][2]:
-                opened.discard(o["banks"][0])
-            else:
-                opened.add(o["banks"][0])
-        start[i] = s
-        free[q] = e
-        end = max(end, e)
-        order.setdefault(q, []).append(i)
-        for x in succ[i]:
-            rt[x] = max(rt[x], e + dly(o, ops[x]))
-            left[x] -= 1
-            if not left[x]:
-                ready.setdefault(ops[x]["q"], []).append(x)
-    return end, order, start, extra
+            for q, j in users.setdefault(b, {}).items():
+                if q != o["q"]:
+                    o["dep"][j] = True
+            users[b][o["q"]] = i
+    return order
 
 
+PERIOD, LAG, LEAN = 15400.0, 7500.0, {'r': -7500, 'E': 4800, 'g': -2900, 'k': -400, 'z': 2200, 'y': -100, 'l': 2500, 'f': -100, 'P': -200, 'A': 2000, 'q': -2100, 'd': 900, 'x': 500, 'm': 200, 'e': -100}
 _CACHE = {}
 SEMQ = {"v": "sv", "s": "ss", "t": "st_", "g": "sg"}
 
@@ -545,18 +646,16 @@ def _plan():
         return _CACHE["p"]
     ops = _build()
     _deps(ops)
-    for o in ops:
-        o["cost"] *= SCALE
-    end, order, start, extra = _schedule(ops, BIAS)
+    pre = _graph(ops)
+    end, start = _justify(ops, pre, _ranks(ops, pre, _alone(ops, pre), PERIOD, LAG, LEAN), 6)
+    order = _orders(ops, start)
     cnt = {}
     for q, L in order.items():
         for i in L:
             o = ops[i]
             o["start"] = start[i]
-            for j in extra[i]:
-                o["dep"][j] = True
             if "dma" in o:
-                o["tok"] = (o["dma"], 48 if o["call"] == "sto" else 16)
+                o["tok"] = (o["dma"], 16)
             elif o["call"] == "arrive":
                 o["tok"] = ("arr%d%d%d" % (o["args"][0] + 1, o["args"][1], o["args"][2]), None)
             elif o["call"] != "send":
@@ -617,20 +716,14 @@ def rank_program(g, core, T, topo):
                 t, h, k = a
                 dst = T.cores[(rank + hops[t]) % N]
                 rid, pid = topo.addr(dst, core)
-                c0, c1 = o["r"][0][1:3]
-                g.remote_dma(T.msg[:, c0 + 240 * NH:c1 + 240 * NH], T.out[:, c0:c1], T.sem["arr%d%d%d" % (t + 1, h, k)], T.sem.snd, pid, rid,
-                             topo.mask(core, dst))
+                g.remote_dma(ap(o["to"]), ap(o["r"][0]), T.sem["arr%d%d%d" % (t + 1, h, k)], T.sem.snd, pid, rid, topo.mask(core, dst))
                 nsend += len(topo.engines(core, dst))
                 continue
             if call == "ld":
                 e.dma_start(ap(a[0]), T[a[1]][:, :]).then_inc(T.sem[o["dma"]], 16)
                 continue
             if call == "sto":
-                for nm, c in a:
-                    e.dma_start(T[nm][:, :], T.fin[:, c:c + NM]).then_inc(T.sem[o["dma"]], 16)
-                continue
-            if call == "stys":
-                e.dma_start(T.ys[:, :], T.yso[:, :]).then_inc(T.sem[o["dma"]], 16)
+                e.dma_start(T[a[0]][:, :], ap(a[1])).then_inc(T.sem[o["dma"]], 16)
                 continue
             if call == "mm":
                 lst, st, sp = a
@@ -656,9 +749,11 @@ def rank_program(g, core, T, topo):
                 ins = e.activation(ap(a[0]), ap(a[1]), a[2], ap(a[3]), ap(a[4]), **kw)
             elif call == "iota":
                 ins = e.iota(ap(a[0]), a[1], a[2], a[3], allow_small_or_imprecise_dtypes=True)
+            elif call == "asel":
+                ins = e.affine_select(ap(a[0]), ap(a[1]), a[2], a[3], a[4], a[5], 1)
             ins.then_inc(T.sem[o["tok"][0]], 1)
     g.wait_ge(T.sem.snd, nsend)
     for s, v in sorted(cnt.items()):
         g.wait_ge(T.sem[s], v)
-    g.wait_ge(T.sem.wr0, 48)
-    g.wait_ge(T.sem.wr1, 16)
+    for k in range(4):
+        g.wait_ge(T.sem["wr%d" % k], 16)

@@ -1,3 +1,4 @@
+import numpy as np
 from concourse.mybir import AluOpType, ActivationFunctionType
 
 OP = AluOpType
@@ -8,9 +9,12 @@ NM = 160
 G16 = 16 * n
 VIS = 4
 CW = 4112
-SENDS = [("T", 0, 80), ("D", 0, 160)]
-KY, KX = [(0, 80, "s")], [(0, 40, "s"), (40, 80, "s")]
-ONV = ["TL", "hi"]
+SENDS = [(0, 80), (80, 240)]
+KY, KX = [(0, 40, "s"), (40, 80, "s")], [(0, 26, "s"), (26, 54, "s"), (54, 80, "s")]
+ONV = ["TL", "D", "Z"]
+SG = 0
+EK = False
+VP = False
 PH = ["S", 0, 0]
 
 SCRATCH = {}
@@ -28,16 +32,16 @@ _buf("clkw", CW, "bfloat16")
 for _nm, _c in (("dli", NM), ("tli", NM), ("sci", 256), ("sti", 256), ("thi", 1)):
     _buf(_nm, _c, "int32")
 _buf("zin", NM, "bfloat16")
-for _nm in ("tf", "tf2", "tf3", "tf4"):
-    _buf(_nm, 256, "float32")
+_buf("tf", NM, "float32"); _buf("tf2", NM, "float32")
 _buf("sct", 257 + NM, "float32")
 _buf("stt", 257, "float32")
 _buf("ic", 128, "int32"); _buf("ik", 1, "int32"); _buf("i1", 128, "int32"); _buf("i2", 128, "int32"); _buf("i3", 128, "int32")
 _buf("ki", 3, "int32"); _buf("kf", 8, "float32"); _buf("JF", 128, "bfloat16")
-for _nm in ("J1", "J2", "ZE", "BD", "ID", "NI", "Ik", "Nh", "Ic", "N8", "P8", "N256", "NU", "P512", "N1024", "PBD8", "NBD8"):
+for _nm in ("J1", "J2", "ZE", "BD", "ID", "NI", "Ik", "Nh", "Ic", "N8", "P8", "N256", "NU", "P512", "N1024", "HI", "PBD8", "NBD8"):
     _buf(_nm, 128, "bfloat16")
 _buf("BDf", 128, "float32")
 _buf("ROT", 2048, "float16"); _buf("AS", 2048, "bfloat16"); _buf("SS", 2048, "bfloat16"); _buf("TRI", 2048, "bfloat16")
+_buf("RR", 2048, "bfloat16")
 _buf("seg0", G16, "bfloat16"); _buf("EQ", G16, "bfloat16"); _buf("seg32", NM, "float32"); _buf("seg16", NM, "float32")
 _buf("pen", NM, "float16"); _buf("NE", NM, "bfloat16"); _buf("CN", 5 * n, "float16"); _buf("IT", 272, "bfloat16")
 _buf("DUM", 10, "float32"); _buf("CK", 5, "float32"); _buf("dmi", 10, "int32"); _buf("cki", 5, "int32")
@@ -45,13 +49,12 @@ _buf("thc", 1, "float32"); _buf("lim", 1, "float32"); _buf("As", 1, "int32"); _b
 _buf("t1s", NM, "float32"); _buf("pv", 10, "bfloat16"); _buf("VB", NM, "bfloat16"); _buf("el", 1600, "bfloat16")
 _buf("ls", NM, "float32"); _buf("xa", 10, "float32"); _buf("sou", 10, "uint16")
 _buf("yso", 256, "float32"); _buf("fin", 480, "float32")
-_buf("inT", n * NH * VIS, "uint16"); _buf("outT", n * NH * (VIS - 1), "uint16")
-_buf("inD", NM * NH * VIS, "float16"); _buf("outD", NM * NH * (VIS - 1), "float16")
+_buf("inn", 3 * n * NH * VIS, "uint16"); _buf("out", 3 * n * NH * VIS, "uint16")
 for _h in range(NH):
     for _nm, _c, _d in (("off1", n, "uint16"), ("Y", G16, "bfloat16"), ("X", G16, "bfloat16"), ("mn", G16, "bfloat16"),
                         ("eq", G16, "bfloat16"), ("eg", G16, "bfloat16"), ("tp", G16, "bfloat16"), ("bf", 13 * n, "bfloat16"), ("hf", 7 * n, "float16"),
                         ("f3", 10 * n, "float32"), ("nk", [5, 32], "float32"), ("vs", NM, "int32"), ("ri", n, "int32"),
-                        ("li", 16, "int32"), ("lu", 24, "uint16"), ("lf", 8, "float32")):
+                        ("li", 16, "int32"), ("lu", 32, "uint16"), ("lf", 8, "float32")):
         _buf(_nm + str(_h), _c, _d)
 
 SEMAPHORES = (["sv", "ss", "st_", "sg", "snd"] + ["ld%d" % i for i in range(7)]
@@ -163,8 +166,8 @@ def _build():
     def IO(x, pat, base, mul):
         add("g", "iota", (x, pat, base, mul), [], [x], 130 + 1.7 * wid(x))
 
-    def SEL(out, a, pat, op, fill, base):
-        add("g", "asel", (out, a, pat, op, fill, base), [a], [out], 170 + 1.7 * wid(out))
+    def SEL(out, a, pat, op, fill, base, mul=1):
+        add("g", "asel", (out, a, pat, op, fill, base, mul), [a], [out], 170 + 1.7 * wid(out))
 
     def blk(name, q):
         return F(name, 128 * q, 128 * q + 128)
@@ -203,32 +206,37 @@ def _build():
     for q in range(16):
         TS(blk("ROT", q), F("J1"), float(q), OP.is_equal)
     for q in range(16):
-        TS(blk("SS", q), F("J2"), float(q), OP.is_equal)
+        if q < SG:
+            SEL(blk("SS", q), BD, [[0, 8], [1, 16]], OP.is_equal, 0.0, -q, 0)
+        else:
+            TS(blk("SS", q), F("J2"), float(q), OP.is_equal)
     for nm, c in (("ID", 1.0), ("Ic", 1.0 / 64), ("N8", -8192.0), ("Ik", 1.0 / 4096), ("Nh", -1.0 / 16), ("P8", 8192.0), ("N256", -256.0),
-                  ("NU", -16640.0), ("P512", 512.0), ("N1024", -1024.0), ("NI", -1.0)):
+                  ("NU", -33024.0), ("P512", 512.0), ("N1024", -1024.0), ("NI", -1.0), ("HI", 0.5)):
         SEL(F(nm), F("ZE"), [[-1, 128]], OP.not_equal, c, 0)
     for nm, c in (("PBD8", 8192.0), ("NBD8", -8192.0), ("BDf", 0.5)):
         ACT(F(nm), BD, AF.Copy, 0.0, c)
     for q in range(15):
         SEL(blk("TRI", q), F("PBD8"), [[-16, 8], [0, 16]], OP.is_gt, 0.0, -q)
+    for q in range(16 if VP else 0):
+        SEL(blk("RR", q), BD, [[-16, 8], [0, 16]], OP.is_equal, 0.0, -q)
     for j in range(4):
         for i in range(4):
             o = F("p%d" % (4 + j), 128 * i, 128 * i + 128)
             MM([(o, F("Ic"), blk("ROT", (16 - 4 * j - i) % 16)), (o, N8, ID)])
         ACT(F("AS", 512 * j, 512 * j + 512), F("p%d" % (4 + j)), AF.Copy)
     TS(F("EQ", 0, 128), F("i3"), kp, OP.is_equal)
-    for a, b in ((128, 256), (256, 512), (512, 1024), (1024, 1280)):
+    for a, b in ((128, 160),) if EK else ((128, 256), (256, 512), (512, 1024), (1024, 1280)):
         ACT(F("EQ", a, b), F("EQ", 0, b - a), AF.Copy)
     TS(F("pen", 0, n), F("EQ", 0, n), 60000.0, OP.mult, 1.0 - 60000.0, OP.add)
     TS(F("pen", n, NM), F("EQ", 0, n), 60000.0, OP.mult, -1535.0 - 60000.0, OP.add)
     TS(F("NE"), F("EQ", 0, NM), -256.0, OP.mult, 256.0, OP.add)
-    MS(F("seg0"), 1.0)
+    IO(F("seg0"), [[0, G16]], 1, 0)
     MS(F("seg0", 0, G16, 16), 0.0)
     for nm, k in (("seg32", 32), ("seg16", 16)):
         MS(F(nm), 1e9)
         MS(F(nm, 0, NM, k), -1e9)
-    for i, c in enumerate((-16384.0, 2064.0 - 16384.0, 2064.0 - 8192.0, -1024.0, 1024.0)):
-        MS(CN(i), c)
+    for i, k, c in ((0, 2, 2064.0 - 16384.0), (2, 1, 2064.0 - 8192.0), (3, 1, 1024.0)):
+        MS(CN(i, k), c)
     TS(F("DUM"), F("dmi"), kp, OP.add)
     TS(F("kf", 3, 4), kp, 16.0, OP.mult)
     TS(F("CK"), F("cki"), F("kf", 3, 4), OP.add)
@@ -236,17 +244,15 @@ def _build():
     TS(F("kf", 5, 6), ko, -33554432.0, OP.mult, F("kf", 4, 5), OP.add)
     TS(F("kf", 7, 8), ko, 33554432.0, OP.mult, -33554432.0, OP.add)
     TS(F("kf", 6, 7), F("kf", 7, 8), F("kf", 4, 5), OP.add)
-    for src, tmp, k, c, out in (("tli", "tf", NM, 4.0, None), ("dli", "tf2", NM, 2.0, None), ("sti", "tf3", 256, 4.0, "stt"), ("sci", "tf4", 256, 2.0, "sct")):
-        ACT(F(tmp, 0, k), F(src), AF.Copy, 0.0, c)
-        TT(F(tmp, 0, k), F(tmp, 0, k), F(src), OP.min)
-        if out:
-            MS(F(out), -2048.0 - c)
-            ACT(F(out, 1, 257), F(tmp), AF.Copy, -2048.0)
-    TS(F("inT", 0, NM), F("tf", 0, NM), 16.0, OP.add)
+    for src, tmp, c, out in (("tli", F("p0", 0, NM), 4.0, F("tf", 0, NM)), ("dli", F("p1", 0, NM), 2.0, F("tf2", 0, NM)),
+                             ("sti", F("p2", 0, 256), 4.0, F("stt", 1, 257)), ("sci", F("p3", 0, 256), 2.0, F("sct", 1, 257))):
+        ACT(tmp, F(src), AF.Copy, 0.0, c)
+        TT(out, F(src), tmp, OP.min)
+    MS(F("stt", 0, 1), -4.0)
+    MS(F("sct", 0, 1), -2.0)
     for h in range(NH):
-        ACT(F("inD", NM * h, NM * h + n), F("tf2", h * n, h * n + n), AF.Copy, -2048.0)
-        ACT(F("inD", NM * h + n, NM * h + NM), F("zin", h * n, h * n + n), AF.Copy, 1024.0)
-    TS(F("thc"), F("thi"), 16401.525, OP.add)
+        ACT(F("inn", 3 * h * n, (3 * h + 1) * n), F("tf", h * n, h * n + n), AF.Copy, 16.0)
+    TS(F("thc"), F("thi"), 17.525, OP.add)
     CP(F("lim"), F("thc"))
     MS(F("As"), 0)
 
@@ -258,7 +264,8 @@ def _build():
         last = t == VIS - 1
         H = str(h)
         k0 = NH * t + h
-        offT, D, Z = F("inT", n * k0, n * k0 + n), F("inD", NM * k0, NM * k0 + n), F("inD", NM * k0 + n, NM * k0 + NM)
+        m = 3 * n * k0
+        offT = F("inn", m, m + n)
 
         def P(b, i, k=1):
             return F("p%d" % (4 + 2 * h + b), i * n, (i + k) * n)
@@ -291,17 +298,23 @@ def _build():
         off1, Y = F("off1" + H), F("Y" + H)
         hi, E, hiU, fl, nct, fc, NG, oh, kmT, ykm, A2 = bf(0), bf(1), bf(2), bf(3), bf(4), bf(5), bf(6, 2), bf(8), bf(9), bf(10), bf(11)
         N, G = bf(6), bf(7)
-        TL, cv, sv, wD, yk, r1, tD = [F("hf" + H, i * n, i * n + n) for i in range(7)]
+        TL, D, Z, cv, sv, yk = [F("hf" + H, i * n, i * n + n) for i in range(6)]
         luv, luk, luw = [F("lu" + H, 8 * i, 8 * i + 5) for i in range(3)]
         PH[0] = "y"
         gather("Y" + H, offT, KY)
         PH[0] = "e"
         ACT(TL, offT, AF.Identity, -2064.0, nm="TL")
+        if t:
+            ACT(D, F("inn", m + n, m + NM), AF.Identity, -2064.0, nm="D")
+            ACT(Z, F("inn", m + NM, m + 3 * n), AF.Copy, nm="Z")
+        else:
+            ACT(D, F("tf2", h * n, h * n + n), AF.Identity, -2048.0)
+            Z = F("zin", h * n, h * n + n)
         ACT(hi, offT, AF.Identity, 129 - 143.5 / 256, 1.0 / 256, nm="hi")
         MM([(P(0, 3), BD, hi)])
         ACT(E, P(0, 3), AF.Relu, 2049.0, -1.0, nm="E")
         MM([(P(0, 4), BD, Z)])
-        ACT(hiU, P(0, 4), AF.Identity, 64.501953125, 1.0 / 256, nm="hiU")
+        ACT(hiU, P(0, 4), AF.Identity, 129 - 127.5 / 256, 1.0 / 256, nm="hiU")
         PH[0] = "q"
         acc = R(0, 4)
         compare(TL, D, "eq" + H, lambda q: blk("AS", q), [], [[(acc, ID, D), (acc, F("Ic"), F("eq" + H, 0, n)), (acc, N8, E)], []])
@@ -313,15 +326,17 @@ def _build():
         gather("X" + H, off1, KX)
         SC(F("tp" + H), F("seg0"), F("X" + H), 0.0, OP.mult, OP.max)
         PH[0] = "m"
-        zps, Gp, key = P(1, 0), R(0, 5), P(0, 0)
-        MM([(zps, ID, CN(3)), (zps, ID, Z)])
+        zps, Gp, key = P(1, 0), P(0, 5), P(0, 0)
+        MM([(zps, ID, Z)])
         for q in range(16):
             TT(F("mn" + H, q * n, q * n + n), F("Y" + H, q, G16, 16), zps, OP.min)
-        MM([(Gp, blk("SS", q), F("Y" + H, q, G16, 16)) for q in range(16)] + [(Gp, BD, Z)], True)
-        MM([(Gp, N8, nct)], False, True)
-        MM([(key, F("Ik"), TL), (key, F("Nh"), hi)], True)
+        MM([(key, F("Ik"), TL), (key, F("Nh"), hi), (Gp, BD, Z)], True)
+        for qs in (range(0, 8), range(8, 16)):
+            MM([(Gp, blk("SS", q), F("Y" + H, q, G16, 16)) for q in qs], True, True)
+        MM([(Gp, N8, nct)], True, True)
         for j, qs in enumerate(CH):
             MM([(key, blk("SS", q), F("mn" + H, q * n, q * n + n)) for q in qs], j < 2, True)
+        ops[-1]["after"] = ops[-4]["id"]
         PH[0] = "k"
         ACT(BLK("nk" + H, 0), key, AF.Identity, F("kf", 5, 6), 4096.0, nm="nk0")
         ACT(BLK("nk" + H, 1), key, AF.Identity, F("kf", 6, 7), 4096.0, nm="nk1")
@@ -330,12 +345,17 @@ def _build():
         SC(vs, F("seg32"), vt, -1e9, OP.min, OP.max)
         kb, va, kk = F("vs" + H, 31, NM, 32), F("li" + H, 0, 5), F("li" + H, 8, 13)
         TS(va, kb, 255, OP.bitwise_and)
-        TS(luv, va, 1.0, OP.add)
-        ACT(sv, IND(F("stt"), luv), AF.Copy, nm="sv")
+        ACT(luv, va, AF.Copy, 1.0, nm="luv")
+        ACT(sv, IND(F("stt"), luv), AF.Copy, -2048.0, nm="sv")
         TS(kk, kb, 8, OP.arith_shift_right, 15, OP.bitwise_and)
         TT(luk, F("CK"), kk, OP.subtract)
-        ACT(oh, IND(F("EQ"), luk), AF.Copy, nm="oh")
-        ACT(yk, IND(Y, luk), AF.Copy, nm="yk")
+        if EK:
+            lue = F("lu" + H, 24, 29)
+            TS(lue, kk, -1.0, OP.mult, 15.0, OP.add)
+            ACT(oh, IND(F("EQ", 0, 16), lue), AF.Copy, nm="oh")
+        else:
+            ACT(oh, IND(F("EQ"), luk), AF.Copy, nm="oh")
+        ACT(yk, IND(Y, luk), AF.Copy, -0.5, nm="yk")
         PH[0] = "c"
         K2 = f3(2)
         ACT(K2, key, AF.Identity, F("lim"), 2.0, nm="K2")
@@ -353,8 +373,8 @@ def _build():
         a1 = F("lf" + H, 0, 5)
         TT(a1, va, F("f3" + H, 4 * n + 15, 5 * n, 16), OP.add)
         TT(luw, a1, F("f3" + H, 3 * n + 15, 4 * n, 16), OP.max)
-        wT, tT = f3(8), f3(9)
-        ACT(wT, IND(F("stt"), luw), AF.Identity, 2064.0, nm="wT")
+        wT, tT, wD, tD = f3(5), f3(6), f3(7), f3(8)
+        ACT(wT, IND(F("stt"), luw), AF.Copy, 16.0, nm="wT")
         ACT(F("pv", 5 * h, 5 * h + 5), a1, AF.Abs, 1024.0)
         PH[0] = "d"
         t1p, dg, tg = P(1, 0), P(1, 3), P(1, 4)
@@ -362,44 +382,46 @@ def _build():
         ACT(kmT, t1p, AF.Relu, -6142.0, nm="kmT")
         MM([(P(1, 3, 2), ID, CN(0, 2)), (dg, ID, D), (dg, P8, fl), (tg, ID, TL), (tg, P8, nct), (tg, N8, oh), (dg, P8, G), (tg, P8, G)])
         TT(tT, wT, tg, OP.max)
-        oT, oD, oZ = (f3(5), f3(6), f3(7)) if last else (F("outT", n * k0, n * k0 + n), F("outD", NM * k0, NM * k0 + n), F("outD", NM * k0 + n, NM * k0 + NM))
-        PH[0] = "g"
+        oT, oD, oZ = [F("out", m + i * n, m + i * n + n) for i in range(3)]
+        yield
+        PH[:] = ["g", t, h]
         rT = R(0, 4)
         compare(TL, sv, "eg" + H, lambda q: N8, [(rT, ID, CN(2))], [[(rT, ID, sv), (rT, P8, G)], [(rT, N8, kmT)]])
         TT(oT, tT, rT, OP.max)
         PH[0] = "f"
         ACT(F("t1s", h * n, h * n + n), t1p, AF.Relu, -6142.0, nm="t1s")
-        ACT(F("VB", h * n, h * n + n), IND(F("IT"), luv), AF.Copy, nm="VB")
-        ACT(cv, IND(F("sct", 0, 257), luv), AF.Copy, nm="cv")
-        ACT(wD, IND(F("sct", 0, 257), luw), AF.Copy, nm="wD")
+        if last or not VP:
+            ACT(F("VB", h * n, h * n + n), IND(F("IT"), luv), AF.Copy, nm="VB")
+        ACT(cv, IND(F("sct", 0, 257), luv), AF.Copy, -2048.0, nm="cv")
+        ACT(wD, IND(F("sct", 0, 257), luw), AF.Copy, 16.0, nm="wD")
         TT(tD, wD, dg, OP.max)
         rD = R(0, 4)
         compare(D, cv, "eq" + H, lambda q: N8, [(rD, ID, CN(0)), (rD, N8, fl)], [[(rD, ID, cv), (rD, P8, G)], []])
         TT(oD, tD, rD, OP.max)
         PH[0] = "z"
-        yp, zd, z1, zp = P(0, 3), P(0, 4), P(0, 1), P(0, 2)
+        yp, zd, z1 = P(0, 3), P(0, 4), P(0, 1)
         MM([(yp, ID, yk), (yp, F("P512"), N)])
-        ACT(ykm, yp, AF.Relu, -512.0, nm="ykm")
+        ACT(ykm, yp, AF.Relu, -511.5, nm="ykm")
         MM([(zd, ID, Z), (zd, F("P512"), G), (zd, F("NI"), ykm)])
-        ACT(A2, zd, AF.Abs, -512.0)
-        MM([(z1, F("N1024"), G), (z1, ID, yk), (z1, ID, F("tp" + H, 15, G16, 16))])
-        ACT(r1, z1, AF.Identity, 1535.8, 0.5, nm="r1")
-        MM([(zp, ID, CN(4)), (zp, ID, A2)])
-        TT(oZ, r1, zp, OP.min)
+        ACT(A2, zd, AF.Abs, 512.0)
+        MM([(z1, ID, CN(3)), (z1, F("N1024"), G), (z1, F("HI"), yk), (z1, F("HI"), F("tp" + H, 15, G16, 16))])
+        TT(oZ, A2, z1, OP.min)
         PH[0] = "r"
         if last:
-            TS(F("fin", h * n, h * n + n), oD, 2048.0, OP.add, -1.0, OP.max)
+            TS(F("fin", h * n, h * n + n), oD, -16.0, OP.add, -1.0, OP.max)
             TS(F("fin", 160 + h * n, 160 + h * n + n), oT, -16.0, OP.add, -1.0, OP.max)
-            ACT(F("fin", 320 + h * n, 320 + h * n + n), oZ, AF.Copy, -1024.0)
+            ACT(F("fin", 320 + h * n, 320 + h * n + n), oZ, AF.Copy)
         else:
-            for k, (x, a, b) in enumerate(SENDS):
-                w = n if x == "T" else NM
-                add("g", "send", (t, h, k), [F("out" + x, w * k0 + a, w * k0 + b)], [], 200, to=F("in" + x, w * (k0 + NH) + a, w * (k0 + NH) + b))
+            for k, (a, b) in enumerate(SENDS):
+                add("g", "send", (t, h, k), [F("out", m + a, m + b)], [], 200, to=F("inn", m + 3 * n * NH + a, m + 3 * n * NH + b))
                 add("n", "arrive", (t, h, k), [], [ops[-1]["to"]], 0)
 
     def proofs(t):
         a = 3 * n
         lp = F("p6", a, a + NM)
+        if VP and t < VIS - 1:
+            MM([(F("p6", a + r, a + NM, 16), blk("RR", r), F("pv")) for r in range(16)])
+            ACT(F("VB"), lp, AF.Copy)
         lst = [(lp, N8, F("NE"))]
         for c in range(10):
             TS(F("el", 160 * c, 176 * c + 16), F("VB", 0, 16 * c + 16), F("pv", c, c + 1), OP.is_equal)
@@ -410,7 +432,7 @@ def _build():
         SC(F("ls"), F("seg16"), lp, -1e9, OP.min, OP.max)
         TT(F("xa"), F("ls", 15, NM, 16), F("pv"), OP.max)
         TT(F("sou"), F("xa"), F("DUM"), OP.min)
-        TS(IND(F("sct"), F("sou")), F("t1s"), 1.0, OP.mult, -2050.0, OP.add)
+        TS(IND(F("sct"), F("sou")), F("t1s"), 1.0, OP.mult, -2.0, OP.add)
 
     def count():
         pa = F("p7", 504, 505)
@@ -420,16 +442,17 @@ def _build():
         TS(F("lim"), F("Am"), 8.0, OP.mult, F("thc"), OP.add)
 
     for t in range(VIS):
-        for h in range(NH):
+        halves = [visit(t, h) for h in range(NH)]
+        for h in (0, 1, 0, 1):
             PH[1:] = [t, h]
-            visit(t, h)
+            next(halves[h], None)
         PH[:] = ["A", t, 0]
         if t < VIS - 1:
             count()
         PH[:] = ["P", t, 0]
         proofs(t)
     PH[:] = ["E", 0, 0]
-    TS(F("yso"), F("sct", 1, 257), 2048.0, OP.add, -1.0, OP.max)
+    TS(F("yso"), F("sct", 1, 257), -1.0, OP.max)
     for k, (nm, src) in enumerate((("yd", F("fin", 0, NM)), ("yt", F("fin", NM, 2 * NM)), ("yz", F("fin", 2 * NM, 3 * NM)), ("ys", F("yso")))):
         add("y", "sto", (nm, src), [src], [], 50, dma="wr%d" % k, lat=2500)
     return ops
@@ -467,6 +490,8 @@ def _deps(ops):
             sends[o["args"]] = o["id"]
         if o["call"] == "arrive":
             dep[sends[o["args"]]] = False
+        if "after" in o:
+            dep[o["after"]] = False
         o["dep"] = dep
         o["banks"] = sorted(set(x[0] for (x, wr) in acc if _W[x[0]] == "psum"))
     anc, starts, opener = [], {}, {}
@@ -490,6 +515,7 @@ def _deps(ops):
 
 LAT = {"x": 250.0, "own": 200.0, "arr": 2500.0}
 SCALE = 1.05
+SLOW = {"call": 1.4, "gather": 1.8, "wait": 1.3, "arr": 3500.0}
 
 
 def _place(ops, pre, rank, back):
@@ -623,6 +649,61 @@ def _ranks(ops, pre, tau, period, lag, lean):
     return rank
 
 
+def _refine(ops, pre, end, start, steps, seed=1):
+    post = [[] for _ in ops]
+    for i, p in enumerate(pre):
+        for (d, w) in p:
+            post[d].append((i, w))
+    kinds = {}
+    for o in ops:
+        for k in ((o["ph"][0], o["q"], o["ph"][2]), o["tag"] + (o["ph"][2],), o["ph"] + (o["q"],)):
+            kinds.setdefault(k, []).append(o["id"])
+    kinds = list(kinds.values())
+    rnd = np.random.RandomState(seed)
+    val = end + _slow(ops, pre, start)
+    best = (val, end, start)
+    for _ in range(steps):
+        r = list(start)
+        for _k in range((1, 2, 4)[rnd.randint(3)]):
+            d = float(rnd.randn()) * (150.0, 400.0, 1200.0)[rnd.randint(3)]
+            for i in kinds[rnd.randint(len(kinds))]:
+                r[i] += d
+        if rnd.randint(2):
+            b = _place(ops, post, [-(x + o["len"]) for x, o in zip(r, ops)], True)
+            if b is None:
+                continue
+            r = [-(x + o["len"]) for x, o in zip(b, ops)]
+        s = _place(ops, pre, r, False)
+        if s is None:
+            continue
+        e = max(x + o["len"] for x, o in zip(s, ops))
+        if e > end + 1000.0:
+            continue
+        v = e + _slow(ops, pre, s)
+        if v <= val + 100.0:
+            end, start, val = e, s, v
+            best = min(best, (v, e, s))
+    return best[1:]
+
+
+def _slow(ops, pre, start):
+    end, free, users = [0.0] * len(ops), {}, {}
+    for i in sorted(range(len(ops)), key=lambda i: start[i]):
+        o = ops[i]
+        q = o["q"]
+        s = 0.0 if q == "n" else free.get(q, 0.0)
+        for (d, w) in pre[i]:
+            s = max(s, end[d] + (SLOW["arr"] if q == "n" else w * SLOW["wait"]))
+        for b in o["banks"]:
+            for q2, e2 in users.setdefault(b, {}).items():
+                if q2 != q:
+                    s = max(s, e2 + LAT["x"] * SLOW["wait"])
+        end[i] = free[q] = s + o["len"] * (SLOW["gather"] if o["call"] in ("act", "cp", "ts") and "IND" in (o["args"][0][0], o["args"][1][0]) else SLOW["call"])
+        for b in o["banks"]:
+            users[b][q] = end[i]
+    return max(end) / SLOW["call"]
+
+
 def _orders(ops, start):
     order, users = {}, {}
     for i in sorted(range(len(ops)), key=lambda i: (start[i], i)):
@@ -636,7 +717,7 @@ def _orders(ops, start):
     return order
 
 
-PERIOD, LAG, LEAN = 15400.0, 7500.0, {'r': -7500, 'E': 4800, 'g': -2900, 'k': -400, 'z': 2200, 'y': -100, 'l': 2500, 'f': -100, 'P': -200, 'A': 2000, 'q': -2100, 'd': 900, 'x': 500, 'm': 200, 'e': -100}
+PERIOD, LAG, LEAN, STEPS = (14000.0, 15000.0, 16000.0), (1500.0, 2000.0, 2500.0, 3000.0, 3500.0), {}, 700
 _CACHE = {}
 SEMQ = {"v": "sv", "s": "ss", "t": "st_", "g": "sg"}
 
@@ -647,7 +728,10 @@ def _plan():
     ops = _build()
     _deps(ops)
     pre = _graph(ops)
-    end, start = _justify(ops, pre, _ranks(ops, pre, _alone(ops, pre), PERIOD, LAG, LEAN), 6)
+    tau = _alone(ops, pre)
+    tries = [_justify(ops, pre, _ranks(ops, pre, tau, p, lag, LEAN), 3) for p in PERIOD for lag in LAG]
+    end, start = min(tries, key=lambda x: x[0] + _slow(ops, pre, x[1]))
+    end, start = _refine(ops, pre, end, start, STEPS)
     order = _orders(ops, start)
     cnt = {}
     for q, L in order.items():
@@ -750,7 +834,7 @@ def rank_program(g, core, T, topo):
             elif call == "iota":
                 ins = e.iota(ap(a[0]), a[1], a[2], a[3], allow_small_or_imprecise_dtypes=True)
             elif call == "asel":
-                ins = e.affine_select(ap(a[0]), ap(a[1]), a[2], a[3], a[4], a[5], 1)
+                ins = e.affine_select(ap(a[0]), ap(a[1]), a[2], a[3], a[4], a[5], a[6])
             ins.then_inc(T.sem[o["tok"][0]], 1)
     g.wait_ge(T.sem.snd, nsend)
     for s, v in sorted(cnt.items()):

import numpy as np
from concourse.mybir import AluOpType, ActivationFunctionType

OP = AluOpType
AF = ActivationFunctionType
NH = 2
n = 80
NM = 160
G16 = 16 * n
VIS = 4
CW = 4112
SENDS = [(0, 80), (80, 240)]
KY, KX = [(0, 40, "s"), (40, 80, "s")], [(0, 26, "s"), (26, 54, "s"), (54, 80, "s")]
ONV = ["TL", "D", "Z"]
SG = 0
EK = False
VP = False
PH = ["S", 0, 0]

SCRATCH = {}
_W = {}


def _buf(name, cols, dtype, where="sbuf"):
    SCRATCH[name] = (where, [128] + (cols if isinstance(cols, list) else [cols]), dtype)
    _W[name] = where


for _i in range(8):
    _buf("p%d" % _i, 512, "float32", "psum")
_buf("clkw", CW, "bfloat16")
for _nm, _c in (("dli", NM), ("tli", NM), ("sci", 256), ("sti", 256), ("thi", 1)):
    _buf(_nm, _c, "int32")
_buf("zin", NM, "bfloat16")
_buf("tf", NM, "float32"); _buf("tf2", NM, "float32")
_buf("sct", 257 + NM, "float32")
_buf("stt", 257, "float32")
_buf("ic", 128, "int32"); _buf("ik", 1, "int32"); _buf("i1", 128, "int32"); _buf("i2", 128, "int32"); _buf("i3", 128, "int32")
_buf("ki", 3, "int32"); _buf("kf", 8, "float32"); _buf("JF", 128, "bfloat16")
for _nm in ("J1", "J2", "ZE", "BD", "ID", "NI", "Ik", "Nh", "Ic", "N8", "P8", "N256", "NU", "P512", "N1024", "HI", "PBD8", "NBD8"):
    _buf(_nm, 128, "bfloat16")
_buf("BDf", 128, "float32")
_buf("ROT", 2048, "float16"); _buf("AS", 2048, "bfloat16"); _buf("SS", 2048, "bfloat16"); _buf("TRI", 2048, "bfloat16")
_buf("RR", 2048, "bfloat16")
_buf("seg0", G16, "bfloat16"); _buf("EQ", G16, "bfloat16"); _buf("seg32", NM, "float32"); _buf("seg16", NM, "float32")
_buf("pen", NM, "float16"); _buf("NE", NM, "bfloat16"); _buf("CN", 5 * n, "float16"); _buf("IT", 272, "bfloat16")
_buf("DUM", 10, "float32"); _buf("CK", 5, "float32"); _buf("dmi", 10, "int32"); _buf("cki", 5, "int32")
_buf("thc", 1, "float32"); _buf("lim", 1, "float32"); _buf("As", 1, "int32"); _buf("Am", 1, "int32"); _buf("ac", 2, "float32")
_buf("t1s", NM, "float32"); _buf("pv", 10, "bfloat16"); _buf("VB", NM, "bfloat16"); _buf("el", 1600, "bfloat16")
_buf("ls", NM, "float32"); _buf("xa", 10, "float32"); _buf("sou", 10, "uint16")
_buf("yso", 256, "float32"); _buf("fin", 480, "float32")
_buf("inn", 3 * n * NH * VIS, "uint16"); _buf("out", 3 * n * NH * VIS, "uint16")
for _h in range(NH):
    for _nm, _c, _d in (("off1", n, "uint16"), ("Y", G16, "bfloat16"), ("X", G16, "bfloat16"), ("mn", G16, "bfloat16"),
                        ("eq", G16, "bfloat16"), ("eg", G16, "bfloat16"), ("tp", G16, "bfloat16"), ("bf", 13 * n, "bfloat16"), ("hf", 7 * n, "float16"),
                        ("f3", 10 * n, "float32"), ("nk", [5, 32], "float32"), ("vs", NM, "int32"), ("ri", n, "int32"),
                        ("li", 16, "int32"), ("lu", 32, "uint16"), ("lf", 8, "float32")):
        _buf(_nm + str(_h), _c, _d)

SEMAPHORES = (["sv", "ss", "st_", "sg", "snd"] + ["ld%d" % i for i in range(7)]
              + ["arr%d%d%d" % (t, h, k) for t in range(1, VIS) for h in range(NH) for k in range(len(SENDS))] + ["wr0", "wr1", "wr2", "wr3"])


def _cols(name):
    c = 1
    for x in SCRATCH[name][1][1:]:
        c *= x
    return c


def F(name, a=0, b=None, s=1):
    return (name, a, _cols(name) if b is None else b, s)


def BLK(name, j):
    return (name, 0, _cols(name), 1, j)


def IND(win, off):
    return ("IND", win, off)


def wid(x):
    if x[0] == "IND":
        return 16 * (x[2][2] - x[2][1])
    return x[2] // 2 if len(x) == 5 else -(-(x[2] - x[1]) // x[3])


def _build():
    ops = []
    PH[:] = ["S", 0, 0]
    ring = [0]

    def add(q, call, args, reads, writes, cost, **kw):
        d = {"ph": tuple(PH), "q": q, "call": call, "args": args, "r": reads, "w": writes, "cost": cost, "id": len(ops)}
        d.update(kw)
        ops.append(d)

    def rd(*refs):
        res = []
        for x in refs:
            res += [x[1], x[2]] if x[0] == "IND" else [x]
        return res

    def two(x):
        return SCRATCH[x[0]][2] in ("bfloat16", "float16", "uint16")

    def ps(x):
        return _W[x[0]] == "psum"

    CY = 0.83

    def vcost(out, ins, tt):
        k = wid(out)
        if any(x[0] == "IND" for x in ins):
            return 50 + 1.56 * CY * k
        if out[0] == "IND":
            return 50 + 3.8 * CY * k
        if tt:
            k = k if any(ps(x) for x in ins) else 2 * k
        elif all(two(x) for x in ins + [out]):
            k = k / 2
        return max(64, k) * CY

    def TT(out, a, b, op):
        add("v", "tt", (out, a, b, op), rd(a, b), [out], vcost(out, [a, b], True))

    def TS(out, a, s1, op0, s2=None, op1=None):
        sr = [x for x in (s1, s2) if isinstance(x, tuple)]
        ind = out[0] == "IND"
        add("v", "ts", (out, a, s1, s2, op0, op1), rd(a) + sr + ([out[2]] if ind else []), [out[1] if ind else out], vcost(out, [a], False))

    def CP(out, a):
        add("v", "cp", (out, a), rd(a), [out], vcost(out, [a], False))

    def MS(out, c):
        add("v", "ms", (out, c), [], [out], max(64, wid(out) * (0.5 if two(out) else 1)) * CY)

    def SC(out, d0, d1, init, op0, op1):
        add("v", "sc", (out, d0, d1, init, op0, op1), [d0, d1], [out], vcost(out, [d0, d1], False))

    def VT(out, a):
        add("v", "vt", (out, a), [a], [out], vcost(out, [a], False))

    def ACT(out, a, f, bias=0.0, scale=1.0, acc=None, nm=None):
        k = wid(out)
        if nm == "v" or nm in ONV:
            if f == AF.Relu:
                return TS(out, a, bias, OP.add, 0.0, OP.max) if scale == 1.0 else TS(out, a, bias - 0.5, OP.is_lt)
            if scale == 1.0:
                return CP(out, a) if bias == 0.0 else TS(out, a, bias, OP.add)
            return TS(out, a, scale, OP.mult, bias, OP.add)
        c = 65 + 1.56 * CY * k if a[0] == "IND" else 10 + max(64, k) * CY + (20 if acc else 0)
        add("s", "act", (out, a, f, bias, scale, acc), rd(a) + [x for x in (bias, scale) if isinstance(x, tuple)], [out] + ([acc] if acc else []), c)

    def MM(lst, more=False, cont=False):
        c = 0
        for (o, l, r) in lst:
            c += max(64, wid(r)) * 0.42 * (4 if SCRATCH[r[0]][2] == "float32" else 1)
        reads = [x[1] for x in lst] + [x[2] for x in lst]
        add("t", "mm", (lst, not cont, not more), reads, [x[0] for x in lst], c)

    def LD(q, out, name, sem):
        add(q, "ld", (out, name), [], [out], 50, dma=sem, lat=6000 if name == "clk" else 2500)

    def IO(x, pat, base, mul):
        add("g", "iota", (x, pat, base, mul), [], [x], 130 + 1.7 * wid(x))

    def SEL(out, a, pat, op, fill, base, mul=1):
        add("g", "asel", (out, a, pat, op, fill, base, mul), [a], [out], 170 + 1.7 * wid(out))

    def blk(name, q):
        return F(name, 128 * q, 128 * q + 128)

    def CN(i, k=1):
        return F("CN", i * n, (i + k) * n)

    ID, BD, N8, P8 = F("ID"), F("BD"), F("N8"), F("P8")
    LD("s", F("clkw", 16, CW), "clk", "ld6")
    LD("y", F("tli"), "tl", "ld0")
    LD("y", F("dli"), "dl", "ld1")
    LD("y", F("zin"), "z0", "ld2")
    LD("y", F("thi"), "th", "ld3")
    LD("y", F("sti"), "st", "ld5")
    LD("y", F("sci"), "sc", "ld4")
    IO(F("ik"), [[0, 1]], 0, 1)
    IO(F("ic"), [[1, 128]], 0, 0)
    IO(F("i1"), [[-1, 128]], 128, 1)
    IO(F("dmi"), [[16, 10]], 257, 0)
    IO(F("cki"), [[256, 5]], 15, 0)
    IO(F("IT"), [[1, 272]], 0, 0)
    MS(F("clkw", 0, 16), -1.0)
    MS(F("ZE"), 0.0)
    TS(F("ki", 0, 1), F("ik"), 4, OP.arith_shift_right)
    TS(F("ki", 1, 2), F("ik"), 15, OP.bitwise_and)
    TS(F("ki", 2, 3), F("ik"), 4, OP.arith_shift_right, 1, OP.bitwise_and)
    CP(F("kf", 0, 3), F("ki"))
    kg, kp, ko = F("kf", 0, 1), F("kf", 1, 2), F("kf", 2, 3)
    TS(F("i2"), F("ic"), 4, OP.arith_shift_right)
    TS(BD, F("i2"), kg, OP.is_equal)
    TS(F("JF"), F("i2"), kg, OP.not_equal, 99.0, OP.mult)
    TS(F("i1"), F("i1"), 15, OP.bitwise_and)
    TS(F("i3"), F("ic"), 15, OP.bitwise_and)
    TT(F("J1"), F("i1"), F("JF"), OP.max)
    TT(F("J2"), F("i3"), F("JF"), OP.max)
    for q in range(16):
        TS(blk("ROT", q), F("J1"), float(q), OP.is_equal)
    for q in range(16):
        if q < SG:
            SEL(blk("SS", q), BD, [[0, 8], [1, 16]], OP.is_equal, 0.0, -q, 0)
        else:
            TS(blk("SS", q), F("J2"), float(q), OP.is_equal)
    for nm, c in (("ID", 1.0), ("Ic", 1.0 / 64), ("N8", -8192.0), ("Ik", 1.0 / 4096), ("Nh", -1.0 / 16), ("P8", 8192.0), ("N256", -256.0),
                  ("NU", -33024.0), ("P512", 512.0), ("N1024", -1024.0), ("NI", -1.0), ("HI", 0.5)):
        SEL(F(nm), F("ZE"), [[-1, 128]], OP.not_equal, c, 0)
    for nm, c in (("PBD8", 8192.0), ("NBD8", -8192.0), ("BDf", 0.5)):
        ACT(F(nm), BD, AF.Copy, 0.0, c)
    for q in range(15):
        SEL(blk("TRI", q), F("PBD8"), [[-16, 8], [0, 16]], OP.is_gt, 0.0, -q)
    for q in range(16 if VP else 0):
        SEL(blk("RR", q), BD, [[-16, 8], [0, 16]], OP.is_equal, 0.0, -q)
    for j in range(4):
        for i in range(4):
            o = F("p%d" % (4 + j), 128 * i, 128 * i + 128)
            MM([(o, F("Ic"), blk("ROT", (16 - 4 * j - i) % 16)), (o, N8, ID)])
        ACT(F("AS", 512 * j, 512 * j + 512), F("p%d" % (4 + j)), AF.Copy)
    TS(F("EQ", 0, 128), F("i3"), kp, OP.is_equal)
    for a, b in ((128, 160),) if EK else ((128, 256), (256, 512), (512, 1024), (1024, 1280)):
        ACT(F("EQ", a, b), F("EQ", 0, b - a), AF.Copy)
    TS(F("pen", 0, n), F("EQ", 0, n), 60000.0, OP.mult, 1.0 - 60000.0, OP.add)
    TS(F("pen", n, NM), F("EQ", 0, n), 60000.0, OP.mult, -1535.0 - 60000.0, OP.add)
    TS(F("NE"), F("EQ", 0, NM), -256.0, OP.mult, 256.0, OP.add)
    IO(F("seg0"), [[0, G16]], 1, 0)
    MS(F("seg0", 0, G16, 16), 0.0)
    for nm, k in (("seg32", 32), ("seg16", 16)):
        MS(F(nm), 1e9)
        MS(F(nm, 0, NM, k), -1e9)
    for i, k, c in ((0, 2, 2064.0 - 16384.0), (2, 1, 2064.0 - 8192.0), (3, 1, 1024.0)):
        MS(CN(i, k), c)
    TS(F("DUM"), F("dmi"), kp, OP.add)
    TS(F("kf", 3, 4), kp, 16.0, OP.mult)
    TS(F("CK"), F("cki"), F("kf", 3, 4), OP.add)
    TS(F("kf", 4, 5), kp, -256.0, OP.mult, 35072.0 + 3840.0, OP.add)
    TS(F("kf", 5, 6), ko, -33554432.0, OP.mult, F("kf", 4, 5), OP.add)
    TS(F("kf", 7, 8), ko, 33554432.0, OP.mult, -33554432.0, OP.add)
    TS(F("kf", 6, 7), F("kf", 7, 8), F("kf", 4, 5), OP.add)
    for src, tmp, c, out in (("tli", F("p0", 0, NM), 4.0, F("tf", 0, NM)), ("dli", F("p1", 0, NM), 2.0, F("tf2", 0, NM)),
                             ("sti", F("p2", 0, 256), 4.0, F("stt", 1, 257)), ("sci", F("p3", 0, 256), 2.0, F("sct", 1, 257))):
        ACT(tmp, F(src), AF.Copy, 0.0, c)
        TT(out, F(src), tmp, OP.min)
    MS(F("stt", 0, 1), -4.0)
    MS(F("sct", 0, 1), -2.0)
    for h in range(NH):
        ACT(F("inn", 3 * h * n, (3 * h + 1) * n), F("tf", h * n, h * n + n), AF.Copy, 16.0)
    TS(F("thc"), F("thi"), 17.525, OP.add)
    CP(F("lim"), F("thc"))
    MS(F("As"), 0)

    CH = [range(0, 7), range(7, 14), range(14, 16)]
    CQ = [range(0, 4), range(4, 10), range(10, 16)]
    CS = [range(0, 7), range(7, 14)]

    def visit(t, h):
        last = t == VIS - 1
        H = str(h)
        k0 = NH * t + h
        m = 3 * n * k0
        offT = F("inn", m, m + n)

        def P(b, i, k=1):
            return F("p%d" % (4 + 2 * h + b), i * n, (i + k) * n)

        def R(j, i):
            return F("p%d" % (j + 1 if j else ring[0] % 2), i * n, i * n + n)

        def bf(i, k=1):
            return F("bf" + H, i * n, (i + k) * n)

        def f3(i, k=1):
            return F("f3" + H, i * n, (i + k) * n)

        def compare(src, own, e, w, first, rest):
            for j, qs in enumerate(CQ):
                MM([(R(j, i), blk("ROT", q), src) for i, q in enumerate(qs)])
            for j, qs in enumerate(CQ):
                for i, q in enumerate(qs):
                    TT(F(e, q * n, q * n + n), own, R(j, i), OP.is_equal)
            for j, qs in enumerate(CS):
                MM((first if j == 0 else []) + [(R(0, 4), w(q), F(e, q * n, q * n + n)) for q in qs], True, j > 0)
            MM(rest[0], True, True)
            MM([(R(0, 4), w(q), F(e, q * n, q * n + n)) for q in (14, 15)] + rest[1], False, True)
            ring[0] += 1

        def gather(out, off, parts):
            for a, b, q in parts:
                ACT(F(out, 16 * a, 16 * b), IND(F("clkw"), F(off[0], off[1] + a, off[1] + b)), AF.Copy, nm=q)

        off1, Y = F("off1" + H), F("Y" + H)
        hi, E, hiU, fl, nct, fc, NG, oh, kmT, ykm, A2 = bf(0), bf(1), bf(2), bf(3), bf(4), bf(5), bf(6, 2), bf(8), bf(9), bf(10), bf(11)
        N, G = bf(6), bf(7)
        TL, D, Z, cv, sv, yk = [F("hf" + H, i * n, i * n + n) for i in range(6)]
        luv, luk, luw = [F("lu" + H, 8 * i, 8 * i + 5) for i in range(3)]
        PH[0] = "y"
        gather("Y" + H, offT, KY)
        PH[0] = "e"
        ACT(TL, offT, AF.Identity, -2064.0, nm="TL")
        if t:
            ACT(D, F("inn", m + n, m + NM), AF.Identity, -2064.0, nm="D")
            ACT(Z, F("inn", m + NM, m + 3 * n), AF.Copy, nm="Z")
        else:
            ACT(D, F("tf2", h * n, h * n + n), AF.Identity, -2048.0)
            Z = F("zin", h * n, h * n + n)
        ACT(hi, offT, AF.Identity, 129 - 143.5 / 256, 1.0 / 256, nm="hi")
        MM([(P(0, 3), BD, hi)])
        ACT(E, P(0, 3), AF.Relu, 2049.0, -1.0, nm="E")
        MM([(P(0, 4), BD, Z)])
        ACT(hiU, P(0, 4), AF.Identity, 129 - 127.5 / 256, 1.0 / 256, nm="hiU")
        PH[0] = "q"
        acc = R(0, 4)
        compare(TL, D, "eq" + H, lambda q: blk("AS", q), [], [[(acc, ID, D), (acc, F("Ic"), F("eq" + H, 0, n)), (acc, N8, E)], []])
        PH[0] = "x"
        ACT(F("ri" + H), acc, AF.Identity, nm="ri")
        TT(nct, F("ri" + H), acc, OP.is_equal)
        ACT(off1, acc, AF.Relu, 2064.0, nm="off1")
        ACT(fl, acc, AF.Sign, 2049.0)
        gather("X" + H, off1, KX)
        SC(F("tp" + H), F("seg0"), F("X" + H), 0.0, OP.mult, OP.max)
        PH[0] = "m"
        zps, Gp, key = P(1, 0), P(0, 5), P(0, 0)
        MM([(zps, ID, Z)])
        for q in range(16):
            TT(F("mn" + H, q * n, q * n + n), F("Y" + H, q, G16, 16), zps, OP.min)
        MM([(key, F("Ik"), TL), (key, F("Nh"), hi), (Gp, BD, Z)], True)
        for qs in (range(0, 8), range(8, 16)):
            MM([(Gp, blk("SS", q), F("Y" + H, q, G16, 16)) for q in qs], True, True)
        MM([(Gp, N8, nct)], True, True)
        for j, qs in enumerate(CH):
            MM([(key, blk("SS", q), F("mn" + H, q * n, q * n + n)) for q in qs], j < 2, True)
        ops[-1]["after"] = ops[-4]["id"]
        PH[0] = "k"
        ACT(BLK("nk" + H, 0), key, AF.Identity, F("kf", 5, 6), 4096.0, nm="nk0")
        ACT(BLK("nk" + H, 1), key, AF.Identity, F("kf", 6, 7), 4096.0, nm="nk1")
        vt, vs = f3(0, 2), F("vs" + H)
        VT(vt, F("nk" + H))
        SC(vs, F("seg32"), vt, -1e9, OP.min, OP.max)
        kb, va, kk = F("vs" + H, 31, NM, 32), F("li" + H, 0, 5), F("li" + H, 8, 13)
        TS(va, kb, 255, OP.bitwise_and)
        ACT(luv, va, AF.Copy, 1.0, nm="luv")
        ACT(sv, IND(F("stt"), luv), AF.Copy, -2048.0, nm="sv")
        TS(kk, kb, 8, OP.arith_shift_right, 15, OP.bitwise_and)
        TT(luk, F("CK"), kk, OP.subtract)
        if EK:
            lue = F("lu" + H, 24, 29)
            TS(lue, kk, -1.0, OP.mult, 15.0, OP.add)
            ACT(oh, IND(F("EQ", 0, 16), lue), AF.Copy, nm="oh")
        else:
            ACT(oh, IND(F("EQ"), luk), AF.Copy, nm="oh")
        ACT(yk, IND(Y, luk), AF.Copy, -0.5, nm="yk")
        PH[0] = "c"
        K2 = f3(2)
        ACT(K2, key, AF.Identity, F("lim"), 2.0, nm="K2")
        TT(fc, K2, Gp, OP.is_lt)
        MM([(P(0, 1), BD, fl), (P(0, 2), BD, fl), (P(0, 1), F("PBD8"), fc), (P(0, 2), F("NBD8"), fc)])
        ACT(NG, P(0, 1, 2), AF.Sign, 15.0)
        if not last:
            cx = P(1, 5)
            MM([(cx, ID, D), (cx, N8, fl), (cx, N8, E), (cx, F("NBD8"), fc)])
            ACT(bf(12), cx, AF.Sign, -6143.0, 1.0, F("ac", h, h + 1))
        PH[0] = "l"
        X1, X2 = P(1, 1), P(1, 2)
        MM([(P(1, 1, 2), ID, F("pen")), (X1, BD, Z), (X1, F("N256"), hiU), (X2, F("N1024"), E), (X1, F("NU"), N), (X2, F("P512"), N), (X2, F("N1024"), G)])
        SC(f3(3, 2), F("seg16"), P(1, 1, 2), -1e9, OP.min, OP.max)
        a1 = F("lf" + H, 0, 5)
        TT(a1, va, F("f3" + H, 4 * n + 15, 5 * n, 16), OP.add)
        TT(luw, a1, F("f3" + H, 3 * n + 15, 4 * n, 16), OP.max)
        wT, tT, wD, tD = f3(5), f3(6), f3(7), f3(8)
        ACT(wT, IND(F("stt"), luw), AF.Copy, 16.0, nm="wT")
        ACT(F("pv", 5 * h, 5 * h + 5), a1, AF.Abs, 1024.0)
        PH[0] = "d"
        t1p, dg, tg = P(1, 0), P(1, 3), P(1, 4)
        MM([(t1p, ID, TL), (t1p, P8, nct), (t1p, N8, oh)])
        ACT(kmT, t1p, AF.Relu, -6142.0, nm="kmT")
        MM([(P(1, 3, 2), ID, CN(0, 2)), (dg, ID, D), (dg, P8, fl), (tg, ID, TL), (tg, P8, nct), (tg, N8, oh), (dg, P8, G), (tg, P8, G)])
        TT(tT, wT, tg, OP.max)
        oT, oD, oZ = [F("out", m + i * n, m + i * n + n) for i in range(3)]
        yield
        PH[:] = ["g", t, h]
        rT = R(0, 4)
        compare(TL, sv, "eg" + H, lambda q: N8, [(rT, ID, CN(2))], [[(rT, ID, sv), (rT, P8, G)], [(rT, N8, kmT)]])
        TT(oT, tT, rT, OP.max)
        PH[0] = "f"
        ACT(F("t1s", h * n, h * n + n), t1p, AF.Relu, -6142.0, nm="t1s")
        if last or not VP:
            ACT(F("VB", h * n, h * n + n), IND(F("IT"), luv), AF.Copy, nm="VB")
        ACT(cv, IND(F("sct", 0, 257), luv), AF.Copy, -2048.0, nm="cv")
        ACT(wD, IND(F("sct", 0, 257), luw), AF.Copy, 16.0, nm="wD")
        TT(tD, wD, dg, OP.max)
        rD = R(0, 4)
        compare(D, cv, "eq" + H, lambda q: N8, [(rD, ID, CN(0)), (rD, N8, fl)], [[(rD, ID, cv), (rD, P8, G)], []])
        TT(oD, tD, rD, OP.max)
        PH[0] = "z"
        yp, zd, z1 = P(0, 3), P(0, 4), P(0, 1)
        MM([(yp, ID, yk), (yp, F("P512"), N)])
        ACT(ykm, yp, AF.Relu, -511.5, nm="ykm")
        MM([(zd, ID, Z), (zd, F("P512"), G), (zd, F("NI"), ykm)])
        ACT(A2, zd, AF.Abs, 512.0)
        MM([(z1, ID, CN(3)), (z1, F("N1024"), G), (z1, F("HI"), yk), (z1, F("HI"), F("tp" + H, 15, G16, 16))])
        TT(oZ, A2, z1, OP.min)
        PH[0] = "r"
        if last:
            TS(F("fin", h * n, h * n + n), oD, -16.0, OP.add, -1.0, OP.max)
            TS(F("fin", 160 + h * n, 160 + h * n + n), oT, -16.0, OP.add, -1.0, OP.max)
            ACT(F("fin", 320 + h * n, 320 + h * n + n), oZ, AF.Copy)
        else:
            for k, (a, b) in enumerate(SENDS):
                add("g", "send", (t, h, k), [F("out", m + a, m + b)], [], 200, to=F("inn", m + 3 * n * NH + a, m + 3 * n * NH + b))
                add("n", "arrive", (t, h, k), [], [ops[-1]["to"]], 0)

    def proofs(t):
        a = 3 * n
        lp = F("p6", a, a + NM)
        if VP and t < VIS - 1:
            MM([(F("p6", a + r, a + NM, 16), blk("RR", r), F("pv")) for r in range(16)])
            ACT(F("VB"), lp, AF.Copy)
        lst = [(lp, N8, F("NE"))]
        for c in range(10):
            TS(F("el", 160 * c, 176 * c + 16), F("VB", 0, 16 * c + 16), F("pv", c, c + 1), OP.is_equal)
            if c:
                lst.append((F("p6", a, a + 16 * c), F("PBD8"), F("el", 160 * c, 176 * c)))
        lst += [(F("p6", a + r, a + NM, 16), blk("TRI", r), F("el", r, 1600, 176)) for r in range(15)]
        MM(lst)
        SC(F("ls"), F("seg16"), lp, -1e9, OP.min, OP.max)
        TT(F("xa"), F("ls", 15, NM, 16), F("pv"), OP.max)
        TT(F("sou"), F("xa"), F("DUM"), OP.min)
        TS(IND(F("sct"), F("sou")), F("t1s"), 1.0, OP.mult, -2.0, OP.add)

    def count():
        pa = F("p7", 504, 505)
        MM([(pa, F("BDf"), F("ac", 0, 1)), (pa, F("BDf"), F("ac", 1, 2))])
        TT(F("As"), F("As"), pa, OP.add)
        TS(F("Am"), F("As"), 31, OP.bitwise_and)
        TS(F("lim"), F("Am"), 8.0, OP.mult, F("thc"), OP.add)

    for t in range(VIS):
        halves = [visit(t, h) for h in range(NH)]
        for h in (0, 1, 0, 1):
            PH[1:] = [t, h]
            next(halves[h], None)
        PH[:] = ["A", t, 0]
        if t < VIS - 1:
            count()
        PH[:] = ["P", t, 0]
        proofs(t)
    PH[:] = ["E", 0, 0]
    TS(F("yso"), F("sct", 1, 257), -1.0, OP.max)
    for k, (nm, src) in enumerate((("yd", F("fin", 0, NM)), ("yt", F("fin", NM, 2 * NM)), ("yz", F("fin", 2 * NM, 3 * NM)), ("ys", F("yso")))):
        add("y", "sto", (nm, src), [src], [], 50, dma="wr%d" % k, lat=2500)
    return ops


def _overlap(a, b):
    if a[0] != b[0] or a[1] >= b[2] or b[1] >= a[2]:
        return False
    if len(a) == 5 and len(b) == 5:
        return a[4] == b[4]
    return not (a[3] == b[3] and a[3] > 1 and (a[1] - b[1]) % a[3])


def _covers(a, b):
    return len(a) == 4 and a[3] == 1 and a[1] <= b[1] and a[2] >= b[2] or a == b


def _deps(ops):
    hist = {}
    sends = {}
    for o in ops:
        dep = {}
        acc = [(x, False) for x in o["r"]] + [(x, True) for x in o["w"]]
        for (x, wr) in acc:
            for (y, ywr, yo) in hist.get(x[0], []):
                if yo is not o and (wr or ywr) and _overlap(x, y):
                    need = yo["q"] != o["q"] or (ywr and o["q"] != "t")
                    dep[yo["id"]] = dep.get(yo["id"], False) or need
        for (x, wr) in acc:
            L = hist.setdefault(x[0], [])
            if wr:
                L[:] = [e for e in L if e[2] is o or not _covers(x, e[0])]
            L.append((x, wr, o))
        if o["call"] == "send":
            sends[o["args"]] = o["id"]
        if o["call"] == "arrive":
            dep[sends[o["args"]]] = False
        if "after" in o:
            dep[o["after"]] = False
        o["dep"] = dep
        o["banks"] = sorted(set(x[0] for (x, wr) in acc if _W[x[0]] == "psum"))
    anc, starts, opener = [], {}, {}
    for o in ops:
        a = 0
        for d in o["dep"]:
            a |= anc[d] | (1 << d)
        anc.append(a)
        if o["call"] == "mm":
            key = (o["banks"][0],)
            if o["args"][1]:
                starts.setdefault(key[0], []).append(o["id"])
                if not o["args"][2]:
                    opener[key] = o
            elif o["args"][2]:
                f = opener[key]
                for s in starts[key[0]]:
                    if s != f["id"] and a >> s & 1 and not anc[s] >> f["id"] & 1:
                        f["dep"].setdefault(s, False)


LAT = {"x": 250.0, "own": 200.0, "arr": 2500.0}
SCALE = 1.05
SLOW = {"call": 1.4, "gather": 1.8, "wait": 1.3, "arr": 3500.0}


def _place(ops, pre, rank, back):
    succ = [[] for _ in ops]
    left = [len(p) for p in pre]
    for i, p in enumerate(pre):
        for (d, w) in p:
            succ[d].append((i, w))
    rt = [0.0] * len(ops)
    start = [0.0] * len(ops)
    busy, bank, sums, opened, tend = {}, {}, {}, {}, {}
    ready = sorted((rank[i], i) for i in range(len(ops)) if not left[i])
    while ready:
        for k, (_r, i) in enumerate(ready):
            o = ops[i]
            q, c, s = o["q"], o["len"], rt[i]
            first = whole = False
            if q == "t":
                b0 = o["banks"][0]
                st, sp = (o["args"][2], o["args"][1]) if back else o["args"][1:]
                first, whole = st and not sp, st and sp
                if first:
                    if b0 in opened:
                        continue
                    s = max(s, tend.get(b0, 0.0))
            if q != "n":
                lists = [(busy.setdefault(q, []), 0.0, None)] + [(bank.setdefault(b, []), LAT["x"], q) for b in o["banks"]]
                if whole:
                    lists.append((sums.setdefault(b0, []), 0.0, None))
                moved = True
                while moved:
                    moved = False
                    for L, m, own in lists:
                        for j in range(len(L) - 1, -1, -1):
                            a, e, q2 = L[j]
                            if e + m <= s:
                                break
                            if q2 != own and a - m < s + c:
                                s = e + m
                                moved = True
                if whole and b0 in opened and s + c > opened[b0]:
                    continue
                for L, m, own in lists[:1 + len(o["banks"])]:
                    j = len(L)
                    while j and L[j - 1][1] > s + c:
                        j -= 1
                    L.insert(j, (s, s + c, q if own else 1))
                if q == "t":
                    tend[b0] = max(tend.get(b0, 0.0), s + c)
                    if first:
                        opened[b0] = s
                    elif sp and not st:
                        sums.setdefault(b0, []).append((opened.pop(b0), s + c, 1))
            break
        else:
            return None
        del ready[k]
        start[i] = s
        for (y, w) in succ[i]:
            rt[y] = max(rt[y], s + c + w)
            left[y] -= 1
            if not left[y]:
                j = 0
                while j < len(ready) and ready[j][0] <= rank[y]:
                    j += 1
                ready.insert(j, (rank[y], y))
    return start


def _justify(ops, pre, rank, rounds):
    post = [[] for _ in ops]
    for i, p in enumerate(pre):
        for (d, w) in p:
            post[d].append((i, w))
    best = (1e12, None)
    for k in range(rounds):
        start = _place(ops, pre, rank, False)
        if start is None:
            break
        best = min(best, (max(s + o["len"] for s, o in zip(start, ops)), start))
        back = _place(ops, post, [-(s + o["len"]) for s, o in zip(start, ops)], True)
        if back is None:
            break
        rank = [-(s + o["len"]) for s, o in zip(back, ops)]
    return best


def _graph(ops):
    def dly(a, b):
        if a["call"] == "send":
            return LAT["arr"] if b["call"] == "arrive" else 0.0
        if "dma" in a:
            return a["lat"]
        if not b["dep"][a["id"]]:
            return 0.0
        return LAT["own"] if a["q"] == b["q"] else LAT["x"]
    seen = {}
    for o in ops:
        o["len"] = 0.0 if o["q"] == "n" else o["cost"] * SCALE
        k = o["ph"] + (o["q"],)
        seen[k] = seen.get(k, 0) + 1
        o["tag"] = (o["ph"][0], o["q"], seen[k])
    return [[(d, dly(ops[d], o)) for d in o["dep"]] for o in ops]


def _alone(ops, pre):
    ids = [o["id"] for o in ops if o["ph"][1:] == (1, 0) and o["ph"][0] not in "SPAE"]
    loc = {i: k for k, i in enumerate(ids)}
    sub = [ops[i] for i in ids]
    p = [[(loc[d], w) for (d, w) in pre[i] if d in loc] for i in ids]
    way = [0.0] * len(ids)
    for k in list(reversed(range(len(ids)))) * 2:
        for (d, w) in p[k]:
            way[d] = max(way[d], way[k] + sub[k]["len"] + w)
    start = _justify(sub, p, [-x - o["len"] for x, o in zip(way, sub)], 3)[1]
    return {o["tag"]: s for o, s in zip(sub, start)}


def _ranks(ops, pre, tau, period, lag, lean):
    rank = [1e9] * len(ops)
    for o in ops:
        ph = o["ph"]
        if ph[0] in "PAE":
            rank[o["id"]] = max(rank[d] + ops[d]["len"] + w for (d, w) in pre[o["id"]] if ops[d]["ph"][0] != "S") + lean.get(ph[0], 0.0)
        elif ph[0] != "S":
            rank[o["id"]] = tau.get(o["tag"], max(tau.values())) + ph[1] * period + ph[2] * lag + lean.get(ph[0], 0.0)
    for o in reversed(ops):
        for (d, w) in pre[o["id"]]:
            if ops[d]["ph"][0] == "S":
                rank[d] = min(rank[d], rank[o["id"]] - w - ops[d]["len"] + (lean.get("S", 0.0) if o["ph"][0] != "S" else 0.0))
    return rank


def _refine(ops, pre, end, start, steps, seed=1):
    post = [[] for _ in ops]
    for i, p in enumerate(pre):
        for (d, w) in p:
            post[d].append((i, w))
    kinds = {}
    for o in ops:
        for k in ((o["ph"][0], o["q"], o["ph"][2]), o["tag"] + (o["ph"][2],), o["ph"] + (o["q"],)):
            kinds.setdefault(k, []).append(o["id"])
    kinds = list(kinds.values())
    rnd = np.random.RandomState(seed)
    val = end + _slow(ops, pre, start)
    best = (val, end, start)
    for _ in range(steps):
        r = list(start)
        for _k in range((1, 2, 4)[rnd.randint(3)]):
            d = float(rnd.randn()) * (150.0, 400.0, 1200.0)[rnd.randint(3)]
            for i in kinds[rnd.randint(len(kinds))]:
                r[i] += d
        if rnd.randint(2):
            b = _place(ops, post, [-(x + o["len"]) for x, o in zip(r, ops)], True)
            if b is None:
                continue
            r = [-(x + o["len"]) for x, o in zip(b, ops)]
        s = _place(ops, pre, r, False)
        if s is None:
            continue
        e = max(x + o["len"] for x, o in zip(s, ops))
        if e > end + 1000.0:
            continue
        v = e + _slow(ops, pre, s)
        if v <= val + 100.0:
            end, start, val = e, s, v
            best = min(best, (v, e, s))
    return best[1:]


def _slow(ops, pre, start):
    end, free, users = [0.0] * len(ops), {}, {}
    for i in sorted(range(len(ops)), key=lambda i: start[i]):
        o = ops[i]
        q = o["q"]
        s = 0.0 if q == "n" else free.get(q, 0.0)
        for (d, w) in pre[i]:
            s = max(s, end[d] + (SLOW["arr"] if q == "n" else w * SLOW["wait"]))
        for b in o["banks"]:
            for q2, e2 in users.setdefault(b, {}).items():
                if q2 != q:
                    s = max(s, e2 + LAT["x"] * SLOW["wait"])
        end[i] = free[q] = s + o["len"] * (SLOW["gather"] if o["call"] in ("act", "cp", "ts") and "IND" in (o["args"][0][0], o["args"][1][0]) else SLOW["call"])
        for b in o["banks"]:
            users[b][q] = end[i]
    return max(end) / SLOW["call"]


def _orders(ops, start):
    order, users = {}, {}
    for i in sorted(range(len(ops)), key=lambda i: (start[i], i)):
        o = ops[i]
        order.setdefault(o["q"], []).append(i)
        for b in o["banks"]:
            for q, j in users.setdefault(b, {}).items():
                if q != o["q"]:
                    o["dep"][j] = True
            users[b][o["q"]] = i
    return order


PERIOD, LAG, LEAN, STEPS = (14000.0, 15000.0, 16000.0), (1500.0, 2000.0, 2500.0, 3000.0, 3500.0), {}, 700
_CACHE = {}
SEMQ = {"v": "sv", "s": "ss", "t": "st_", "g": "sg"}


def _plan():
    if "p" in _CACHE:
        return _CACHE["p"]
    ops = _build()
    _deps(ops)
    pre = _graph(ops)
    tau = _alone(ops, pre)
    tries = [_justify(ops, pre, _ranks(ops, pre, tau, p, lag, LEAN), 3) for p in PERIOD for lag in LAG]
    end, start = min(tries, key=lambda x: x[0] + _slow(ops, pre, x[1]))
    end, start = _refine(ops, pre, end, start, STEPS)
    order = _orders(ops, start)
    cnt = {}
    for q, L in order.items():
        for i in L:
            o = ops[i]
            o["start"] = start[i]
            if "dma" in o:
                o["tok"] = (o["dma"], 16)
            elif o["call"] == "arrive":
                o["tok"] = ("arr%d%d%d" % (o["args"][0] + 1, o["args"][1], o["args"][2]), None)
            elif o["call"] != "send":
                cnt[SEMQ[q]] = cnt.get(SEMQ[q], 0) + 1
                o["tok"] = (SEMQ[q], cnt[SEMQ[q]])
    known = {}
    for i in sorted((i for L in order.values() for i in L), key=lambda i: (ops[i]["start"], i)):
        o = ops[i]
        kn = known.setdefault(o["q"], {})
        w = {}
        for d in sorted((d for d, nd in o["dep"].items() if nd), key=lambda d: -ops[d]["start"]):
            s, v = ops[d]["tok"]
            if v is None:
                v = 1
            if kn.get(s, 0) >= v:
                continue
            w[s] = max(w.get(s, 0), v)
            for s2, v2 in list(ops[d]["kn"].items()) + [(s, v)]:
                kn[s2] = max(kn.get(s2, 0), v2)
        o["wait"] = sorted(w.items())
        o["kn"] = {} if o["call"] == "arrive" else dict(kn)
    _CACHE["p"] = (ops, order, cnt, end)
    return _CACHE["p"]


def rank_program(g, core, T, topo):
    rank = T.rank_of(core)
    if rank is None:
        return
    ops, order, cnt, _end = _plan()
    hops = [1, 4, 2]
    eng = {"v": g.vector, "s": g.scalar, "t": g.tensor, "g": g, "y": g.sync}
    N = len(T.cores)
    arrn = [0] + [len(topo.engines(T.cores[(rank - hops[t]) % N], core)) for t in range(VIS - 1)]

    def ap(x):
        if not isinstance(x, tuple):
            return x
        if x[0] == "IND":
            return ap(x[1]).indirect(ap(x[2]))
        if len(x) == 5:
            return T[x[0]][:, :, 16 * x[4]:16 * x[4] + 16]
        if len(SCRATCH[x[0]][1]) == 3:
            return T[x[0]][:]
        if x[3] == 1:
            return T[x[0]][:, x[1]:x[2]]
        return T[x[0]][:, x[1]:x[2]:x[3]]

    nsend = 0
    for q in ("y", "s", "v", "t", "g"):
        e = eng[q]
        for i in order[q]:
            o = ops[i]
            for s, v in o["wait"]:
                e.wait_ge(T.sem[s], arrn[int(s[3])] if s[:3] == "arr" else v)
            a, call = o["args"], o["call"]
            if call == "send":
                t, h, k = a
                dst = T.cores[(rank + hops[t]) % N]
                rid, pid = topo.addr(dst, core)
                g.remote_dma(ap(o["to"]), ap(o["r"][0]), T.sem["arr%d%d%d" % (t + 1, h, k)], T.sem.snd, pid, rid, topo.mask(core, dst))
                nsend += len(topo.engines(core, dst))
                continue
            if call == "ld":
                e.dma_start(ap(a[0]), T[a[1]][:, :]).then_inc(T.sem[o["dma"]], 16)
                continue
            if call == "sto":
                e.dma_start(T[a[0]][:, :], ap(a[1])).then_inc(T.sem[o["dma"]], 16)
                continue
            if call == "mm":
                lst, st, sp = a
                for k, (oo, l, r) in enumerate(lst):
                    ins = e.matmul(ap(oo), ap(l), ap(r), st and k == 0, sp and k == len(lst) - 1)
            elif call == "tt":
                ins = e.tensor_tensor(ap(a[0]), ap(a[1]), ap(a[2]), a[3])
            elif call == "ts":
                if a[5] is None:
                    ins = e.tensor_scalar(ap(a[0]), ap(a[1]), ap(a[2]), None, a[4])
                else:
                    ins = e.tensor_scalar(ap(a[0]), ap(a[1]), ap(a[2]), ap(a[3]), a[4], a[5])
            elif call == "cp":
                ins = e.tensor_copy(ap(a[0]), ap(a[1]))
            elif call == "ms":
                ins = e.memset(ap(a[0]), a[1])
            elif call == "sc":
                ins = e.tensor_tensor_scan(ap(a[0]), ap(a[1]), ap(a[2]), a[3], a[4], a[5])
            elif call == "vt":
                ins = e.transpose(ap(a[0]), ap(a[1]))
            elif call == "act":
                kw = {} if a[5] is None else {"accum_out": ap(a[5])}
                ins = e.activation(ap(a[0]), ap(a[1]), a[2], ap(a[3]), ap(a[4]), **kw)
            elif call == "iota":
                ins = e.iota(ap(a[0]), a[1], a[2], a[3], allow_small_or_imprecise_dtypes=True)
            elif call == "asel":
                ins = e.affine_select(ap(a[0]), ap(a[1]), a[2], a[3], a[4], a[5], a[6])
            ins.then_inc(T.sem[o["tok"][0]], 1)
    g.wait_ge(T.sem.snd, nsend)
    for s, v in sorted(cnt.items()):
        g.wait_ge(T.sem[s], v)
    for k in range(4):
        g.wait_ge(T.sem["wr%d" % k], 16)
